import numpy as np
import ml_dtypes


def mxq(x, axis, fmt="e4m3"):
    dtype, down = {"e4m3": (ml_dtypes.float8_e4m3fn, 7), "e5m2": (ml_dtypes.float8_e5m2, 14)}[fmt]
    v = np.moveaxis(np.asarray(x, np.float32).astype(ml_dtypes.bfloat16).astype(np.float64), axis, -1)
    blocks = v.reshape(v.shape[:-1] + (-1, 32))
    amax = np.abs(blocks).max(-1, keepdims=True)
    byte = np.maximum(np.where(amax > 0, np.frexp(amax)[1] - 1 + 127, 0) - down, 1)
    scale = np.exp2(byte - 127.0)
    codes = (blocks / scale).astype(np.float32).astype(dtype).astype(np.float64)
    return np.moveaxis((codes * scale).reshape(v.shape), -1, axis)


WIDE = False


def mx_kscale(k):
    if not WIDE:
        return np.ones(k)
    levels = np.array([10, -10, 5, -5, 0])
    if k % 512:
        return np.exp2(np.random.permutation(np.resize(levels, k // 32))).repeat(32)
    a = np.empty((k // 512, 16))
    for p in range(k // 512):
        a[p, :8] = np.random.permutation(np.resize(levels, 8))
        for g in range(8):
            far = levels[np.abs(levels - a[p, g]) >= 10]
            a[p, g + 8] = far[np.random.randint(len(far))]
    return np.exp2(a.ravel()).repeat(32)


BF16 = ml_dtypes.bfloat16


def bf(x):
    return np.asarray(x, np.float32).astype(BF16)


def f64(x):
    return np.asarray(x).astype(np.float64)

def planes(Y):
    n, m = Y.shape
    b = f64(bf(Y)).reshape(n // 32, 32, m)
    amax = np.abs(b).max(1)
    byte = np.clip(np.where(amax > 0, np.frexp(amax)[1] - 1 + 127 - 7, 1), 1, 254)
    codes = (b * np.exp2(127.0 - byte)[:, None, :]).reshape(n, m).astype(np.float32).astype(ml_dtypes.float8_e4m3fn).view(np.uint8)
    words = codes.reshape(n // 512, 128, 4, m).transpose(0, 1, 3, 2)
    return np.ascontiguousarray(words), np.ascontiguousarray(byte.astype(np.uint8).reshape(n // 512, 16, m))


T, D, E, R, F = 1024, 512, 4, 512, 512


def expert_scores(a):
    return np.sqrt(np.sum(a * a, axis=-1))


def silu(v):
    return v / (1.0 + np.exp(-v))


def softmax_experts(score):
    e = np.exp(score - score.max(axis=0, keepdims=True))
    return e / e.sum(axis=0, keepdims=True)


def setup_inputs():
    s, t = mx_kscale(D), mx_kscale(R)
    return {"x": bf(np.random.standard_normal((T, D)) * s),
            "wdown": bf(np.random.standard_normal((E, D, R)) / np.sqrt(D) / s[None, :, None]),
            "rgain": bf((1.0 + 0.1 * np.random.standard_normal((E, R))) * t),
            "wup": bf(np.random.standard_normal((E, R, F)) * 1.5 / np.sqrt(R) / t[None, :, None]),
            "wp": bf(np.random.standard_normal((E, D, F)) / np.sqrt(D) / s[None, :, None])}


def core(x, wdown, rgain, wup, wp):
    xq = mxq(f64(x), 1, "e4m3")
    a = xq @ mxq(f64(wdown), 1, "e4m3")
    score = expert_scores(a)
    g = softmax_experts(score)
    b = a * f64(rgain)[:, None, :]
    u = mxq(b, 2, "e4m3") @ mxq(f64(wup), 1, "e4m3")
    p = xq @ mxq(f64(wp), 1, "e4m3")
    return np.sum(g[:, :, None] * silu(u) * p, axis=0)


def reference(x, wdown, rgain, wup, wp):
    R_out = core(x, wdown, rgain, wup, wp)
    words, scales = planes(R_out)
    return R_out, words, scales

@@ -1,0 +1,387 @@
+import math
+from contextlib import ExitStack
+
+import concourse.mybir as mybir
+from concourse.masks import make_identity
+
+T, D, E, R, F = 1024, 512, 4, 512, 512
+FLOPS = 2 * T * E * (D * R + R * F + D * F)
+
+F32 = mybir.dt.float32
+BF16 = mybir.dt.bfloat16
+U32 = mybir.dt.uint32
+I32 = mybir.dt.int32
+U8 = mybir.dt.uint8
+FP8X4 = mybir.dt.float8_e4m3fn_x4
+ALU = mybir.AluOpType
+ACT = mybir.ActivationFunctionType
+AX = mybir.AxisListType
+
+P = 128
+PACK = 4
+GROUP = 512
+LOG2E = math.log2(math.e)
+
+
+def tile_autonomyofexpertsnormgate_x1_kernel(tc, x, wdown, rgain, wup, wp, out_0, out_1, out_2):
+    nc = tc.nc
+    G = T // GROUP
+    PAIRS = G * E * 2
+    LEAD = 18
+    VADDS = (2, 5, 10, 12, 14, 15, )
+    SB = ()
+    CLUSTERS = (5, 7, 9, 11, 13, 99, )
+
+    with ExitStack() as ctx:
+        keep = ctx.enter_context(tc.tile_pool(name="keep", bufs=1))
+        work = ctx.enter_context(tc.tile_pool(name="work", bufs=3))
+        psum = ctx.enter_context(tc.psum_pool(name="psum", bufs=4))
+        ctx.enter_context(tc.manual_schedule())
+        gain = keep.tile([P, E, 16], BF16, name="gain")
+        ident = keep.tile([P, P], F32, name="ident")
+        ident_b = keep.tile([P, P], BF16, name="ident_b")
+        gain32 = keep.tile([P, E, PACK], F32, name="gain32")
+        half = keep.tile([P, 16], F32, name="half")
+        two = keep.tile([P, 16], F32, name="two")
+        minus = keep.tile([P, 4], F32, name="minus")
+        warm = keep.tile([P, 1], F32, name="warm")
+        x_raw = [keep.tile([P, PACK, D], BF16, name="x_raw%d" % g, align_bytes=64) for g in range(G)]
+        names = ["wd%d" % e for e in range(E)] + ["wp%d" % e for e in range(E)] + ["wu%d" % e for e in range(E)]
+        raw = {n: keep.tile([P, PACK, 512], BF16, name="raw_" + n, align_bytes=64) for n in names}
+        xc = [keep.tile([P, GROUP], U32, name="xc%d" % g, align_bytes=64) for g in range(G)]
+        xs = [keep.tile([P, GROUP], U8, name="xs%d" % g, align_bytes=64) for g in range(G)]
+        dcodes = [keep.tile([P, 512], U32, name="dcodes%d" % e, align_bytes=64) for e in range(E)]
+        dscales = [keep.tile([P, 512], U8, name="dscales%d" % e, align_bytes=64) for e in range(E)]
+        dgrp = [keep.tile([P, 512, PACK], BF16, name="dgrp%d" % e, align_bytes=64) for e in range(E)]
+        pcodes = [keep.tile([P, 2, 512], U32, name="pcodes%d" % e, align_bytes=64) for e in range(E)]
+        pscales = [keep.tile([P, 2, 512], U8, name="pscales%d" % e, align_bytes=64) for e in range(E)]
+        pgrp = [keep.tile([P, 2, 512, PACK], BF16, name="pgrp%d" % e, align_bytes=64) for e in range(E)]
+        sumsq = [keep.tile([P, PACK, E], F32, name="sumsq%d" % g) for g in range(G)]
+        gate = [keep.tile([P, PACK, E], F32, name="gate%d" % g) for g in range(G)]
+        acc = [keep.tile([P, PACK, F], F32, name="acc%d" % g) for g in range(G)]
+
+        src = {}
+        for e in range(E):
+            src["wd%d" % e] = wdown[e]
+            src["wp%d" % e] = wp[e]
+            src["wu%d" % e] = wup[e]
+
+        nc.scalar.dma_start(out=gain[:, :, 0:PACK], in_=rgain.rearrange("e (p t) -> p e t", t=PACK))
+
+        def load_x(g):
+            nc.sync.dma_start(out=x_raw[g][:], in_=x[g * GROUP:(g + 1) * GROUP, :].rearrange("(p t) d -> p t d", t=PACK))
+
+        def load_w(n):
+            nc.sync.dma_start(out=raw[n][:], in_=src[n].rearrange("(p j) c -> p j c", j=PACK))
+
+        load_w("wd0")
+        load_x(0)
+        for n in ("wd1", "wd2", "wd3", "wp0", "wu0"):
+            load_w(n)
+        load_x(1)
+        for n in ("wp1", "wu1", "wp2", "wu2", "wp3", "wu3"):
+            load_w(n)
+
+        nc.vector.memset(warm[:], 0.0)
+        nc.scalar.activation(out=warm[:], in_=warm[:], func=ACT.Silu)
+        nc.vector.tensor_copy(out=gain32[:], in_=gain[:, :, 0:PACK])
+        make_identity(nc, ident[:])
+        nc.gpsimd.tensor_copy(out=ident_b[:], in_=ident[:])
+        nc.gpsimd.memset(half[:], 0.5)
+        nc.gpsimd.memset(two[:], 2.0)
+        nc.gpsimd.memset(minus[:], -1.0)
+
+        def copy_on(eng, out, in_):
+            if eng == "V":
+                nc.vector.tensor_copy(out=out, in_=in_)
+            elif eng == "S":
+                nc.scalar.copy(out=out, in_=in_)
+            else:
+                nc.gpsimd.tensor_scalar(out=out, in0=in_, scalar1=1.0, scalar2=0.0, op0=ALU.mult, op1=ALU.add)
+
+        def ilv(n, eng, lo=0, hi=4):
+            e = int(n[2:])
+            if n.startswith("wd"):
+                copy_on(eng, dgrp[e][:].rearrange("p (t m) j -> p t m j", t=4)[:, lo:hi],
+                        raw[n][:].rearrange("p j (m t) -> p t m j", t=4)[:, lo:hi])
+            else:
+                w = 0 if n.startswith("wp") else 1
+                copy_on(eng, pgrp[e][:, w, 128 * lo:128 * hi, :], raw[n][:, :, 128 * lo:128 * hi].rearrange("p j c -> p c j"))
+
+        banks = {}
+
+        def pe_turn(n, h):
+            bank = psum.tile([P, 1024], BF16, name="pw", tag="ps", bufs=4)
+            banks[n, h] = bank
+            for q in range(2):
+                c0 = 256 * h + 128 * q
+                nc.tensor.matmul(out=bank[:, 512 * q:512 * (q + 1)].rearrange("p (m j) -> p m j", j=PACK), lhsT=ident_b[:],
+                                 rhs=raw[n][:, :, c0:c0 + 128].rearrange("p j m -> p m j"), start=True, stop=True)
+
+        def pe_out(n, h):
+            w = 0 if n.startswith("wp") else 1
+            nc.scalar.copy(out=pgrp[int(n[2:])][:, w, 256 * h:256 * (h + 1), :].rearrange("p m j -> p (m j)"), in_=banks[n, h][:])
+
+        def quant_d(e):
+            nc.vector.quantize_mx(out=dcodes[e][:].bitcast(FP8X4), scales=dscales[e][:],
+                                  in_=dgrp[e][:].rearrange("p c j -> p (c j)"))
+
+        def quant_p(e):
+            nc.vector.quantize_mx(out=pcodes[e][:].rearrange("p w c -> p (w c)").bitcast(FP8X4),
+                                  scales=pscales[e][:].rearrange("p w c -> p (w c)"),
+                                  in_=pgrp[e][:].rearrange("p w c j -> p (w c j)"))
+
+        xg = {}
+
+        def x_turn(g, engs):
+            xg[g] = work.tile([P, GROUP, PACK], BF16, name="xgrp", align_bytes=64, bufs=1)
+            words = x_raw[g][:].rearrange("p t d -> p (t d)").bitcast(F32)
+            dstw = xg[g][:].rearrange("p c j -> p (c j)").bitcast(F32).rearrange("p (s r u) -> p s r u", r=P, u=2)
+            for h in range(2):
+                bank = psum.tile([P, 512], F32, name="pt", tag="ps", bufs=4)
+                view = bank[:].rearrange("p (s u r) -> p s u r", s=2, u=2)
+                for s in range(2):
+                    t = 2 * h + s
+                    for u in range(2):
+                        nc.tensor.transpose(view[:, s, u, :], words[:, 256 * t + u:256 * (t + 1):2], ident[:])
+                copy_on(engs[h], dstw[:, 2 * h:2 * h + 2], view.rearrange("p s u r -> p s r u"))
+
+        def x_quant(g):
+            nc.vector.quantize_mx(out=xc[g][:].bitcast(FP8X4), scales=xs[g][:],
+                                  in_=xg[g][:].rearrange("p c j -> p (c j)"))
+
+        bgrp = {}
+        bcodes = {}
+        bscales = {}
+
+        def cols(t):
+            return slice(P * t, P * (t + 1))
+
+        def a_pair(i):
+            g, e, h = i // 8, (i // 2) % 4, i % 2
+            ts = (2 * h, 2 * h + 1)
+            wc, ws = dcodes[e], dscales[e]
+            ar = {}
+            at = {}
+            for t in ts:
+                arb = psum.tile([P, 512], F32, name="pa", tag="pv", bufs=4)
+                ar[t] = arb[:].rearrange("p (k n) -> p k n", k=4)
+                for k in range(4):
+                    nc.tensor.matmul_mx(out=ar[t][:, k, :], lhsT=wc[:, cols(k)].bitcast(FP8X4), lhsT_scale=ws[:, cols(k)],
+                                        rhs=xc[g][:, cols(t)].bitcast(FP8X4), rhs_scale=xs[g][:, cols(t)],
+                                        start=True, stop=True)
+            for t in ts:
+                atb = psum.tile([P, 512], F32, name="pb", tag="ps", bufs=4)
+                at[t] = atb
+                nc.tensor.matmul_mx(out=atb[:], lhsT=xc[g][:, cols(t)].bitcast(FP8X4), lhsT_scale=xs[g][:, cols(t)],
+                                    rhs=wc[:].bitcast(FP8X4), rhs_scale=ws[:], start=True, stop=True)
+            if h == 0:
+                bgrp[g, e] = work.tile([P, GROUP, PACK], BF16, name="bgrp", align_bytes=64, bufs=3)
+            for t in reversed(ts):
+                sq = work.tile([P, 512], F32, name="sq", bufs=2)
+                nc.scalar.activation(out=sq[:], in_=at[t][:], func=ACT.Square, accum_out=sumsq[g][:, t, e:e + 1])
+            for t in reversed(ts):
+                if 2 * i + t % 2 in SB:
+                    for k in range(4):
+                        nc.scalar.activation(out=bgrp[g, e][:, cols(t), k], in_=ar[t][:, k, :], func=ACT.Copy,
+                                             scale=gain32[:, e, k:k + 1])
+                    continue
+                nc.vector.tensor_tensor(out=bgrp[g, e][:, cols(t), :], in0=ar[t].rearrange("p k n -> p n k"),
+                                        in1=gain[:, e, 0:PACK].unsqueeze(1).to_broadcast([P, P, PACK]), op=ALU.mult)
+
+        def b_quant(g, e):
+            bcodes[g, e] = keep.tile([P, GROUP], U32, name="bc%d%d" % (g, e), align_bytes=64)
+            bscales[g, e] = keep.tile([P, GROUP], U8, name="bs%d%d" % (g, e), align_bytes=64)
+            nc.vector.quantize_mx(out=bcodes[g, e][:].bitcast(FP8X4), scales=bscales[g, e][:],
+                                  in_=bgrp[g, e][:].rearrange("p c j -> p (c j)"))
+
+        soft = {}
+
+        def soft_step(g, k):
+            if k == 0:
+                soft["sc", g] = keep.tile([P, PACK, E], F32, name="sc%d" % g)
+                soft["mx", g] = keep.tile([P, PACK], F32, name="mx%d" % g)
+                soft["ex", g] = keep.tile([P, PACK, E], F32, name="ex%d" % g)
+                soft["s2", g] = keep.tile([P, PACK, 2], F32, name="s2%d" % g)
+                soft["sm", g] = keep.tile([P, PACK], F32, name="sm%d" % g)
+                nc.gpsimd.tensor_tensor(out=soft["sc", g][:].rearrange("p t e -> p (t e)"),
+                                        in0=sumsq[g][:].rearrange("p t e -> p (t e)"), in1=half[:], op=ALU.pow)
+                nc.gpsimd.tensor_scalar(out=soft["sc", g][:], in0=soft["sc", g][:], scalar1=LOG2E, scalar2=0.0,
+                                        op0=ALU.mult, op1=ALU.add)
+            elif k == 1:
+                nc.vector.tensor_reduce(out=soft["mx", g][:], in_=soft["sc", g][:], axis=AX.X, op=ALU.max)
+            else:
+                ex = soft["ex", g]
+                nc.gpsimd.tensor_tensor(out=soft["sc", g][:], in0=soft["sc", g][:],
+                                        in1=soft["mx", g][:].unsqueeze(2).to_broadcast([P, PACK, E]), op=ALU.subtract)
+                nc.gpsimd.tensor_tensor(out=ex[:].rearrange("p t e -> p (t e)"), in0=two[:],
+                                        in1=soft["sc", g][:].rearrange("p t e -> p (t e)"), op=ALU.pow)
+                nc.gpsimd.tensor_tensor(out=soft["s2", g][:], in0=ex[:, :, 0:2], in1=ex[:, :, 2:4], op=ALU.add)
+                nc.gpsimd.tensor_tensor(out=soft["sm", g][:], in0=soft["s2", g][:, :, 0], in1=soft["s2", g][:, :, 1], op=ALU.add)
+                nc.gpsimd.tensor_tensor(out=soft["mx", g][:], in0=soft["sm", g][:], in1=minus[:], op=ALU.pow)
+                nc.gpsimd.tensor_tensor(out=gate[g][:], in0=ex[:], in1=soft["mx", g][:].unsqueeze(2).to_broadcast([P, PACK, E]),
+                                        op=ALU.mult)
+
+        ypair = {}
+
+        def b_pair(i):
+            g, e, h = i // 8, (i // 2) % 4, i % 2
+            ts = (2 * h, 2 * h + 1)
+            pps = {}
+            ups = {}
+            for t in ts:
+                pb_ = psum.tile([P, 512], F32, name="pp", tag="pv", bufs=4)
+                pps[t] = pb_
+                nc.tensor.matmul_mx(out=pb_[:], lhsT=xc[g][:, cols(t)].bitcast(FP8X4), lhsT_scale=xs[g][:, cols(t)],
+                                    rhs=pcodes[e][:, 0, :].bitcast(FP8X4), rhs_scale=pscales[e][:, 0, :], start=True, stop=True)
+            for t in ts:
+                ub_ = psum.tile([P, 512], F32, name="pu", tag="ps", bufs=4)
+                ups[t] = ub_
+                nc.tensor.matmul_mx(out=ub_[:], lhsT=bcodes[g, e][:, cols(t)].bitcast(FP8X4), lhsT_scale=bscales[g, e][:, cols(t)],
+                                    rhs=pcodes[e][:, 1, :].bitcast(FP8X4), rhs_scale=pscales[e][:, 1, :], start=True, stop=True)
+            sl = work.tile([P, 2, F], F32, name="sl", bufs=3)
+            if e > 0:
+                ypair[i] = work.tile([P, 2, F], F32, name="y", bufs=4)
+            for t in reversed(ts):
+                nc.scalar.activation(out=sl[:, t - 2 * h, :], in_=ups[t][:], func=ACT.Silu)
+            for t in ts:
+                dst = acc[g][:, t, :] if e == 0 else ypair[i][:, t - 2 * h, :]
+                nc.vector.scalar_tensor_tensor(out=dst, in0=pps[t][:], scalar=gate[g][:, t, e:e + 1], in1=sl[:, t - 2 * h, :],
+                                               op0=ALU.mult, op1=ALU.mult)
+
+        summed = {}
+
+        def b_add(i):
+            g, e, h = i // 8, (i // 2) % 4, i % 2
+            if e == 0:
+                return
+            half_ = acc[g][:, 2 * h:2 * h + 2, :]
+            eng = nc.vector if i in VADDS else nc.gpsimd
+            eng.tensor_tensor(out=half_, in0=half_, in1=ypair[i][:], op=ALU.add)
+            summed[g, h] = summed.get((g, h), 0) + 1
+            if summed[g, h] == E - 1:
+                nc.sync.dma_start(out=out_0[g * GROUP:(g + 1) * GROUP, :].rearrange("(p t) f -> p t f", t=PACK)[:, 2 * h:2 * h + 2, :],
+                                  in_=half_)
+
+        og = {}
+        oc = {}
+        osc = {}
+
+        def o_ilv(g, eng, lo, hi):
+            assert all(summed[g, h] == E - 1 for h in range(2))
+            if g not in og:
+                og[g] = work.tile([P, F, PACK], BF16, name="og", align_bytes=64, bufs=1)
+            copy_on(eng, og[g][:, lo:hi, :], acc[g][:].rearrange("p t f -> p f t")[:, lo:hi, :])
+
+        def o_quant(g):
+            oc[g] = keep.tile([P, F], U32, name="oc%d" % g, align_bytes=64)
+            osc[g] = keep.tile([P, F], U8, name="osc%d" % g, align_bytes=64)
+            nc.vector.quantize_mx(out=oc[g][:].bitcast(FP8X4), scales=osc[g][:],
+                                  in_=og[g][:].rearrange("p c j -> p (c j)"))
+            nc.sync.dma_start(out=out_1[g].rearrange("p m b -> p (m b)").bitcast(I32), in_=oc[g][:].bitcast(I32))
+            for q in range(4):
+                nc.sync.dma_start(out=out_2[g, 4 * q:4 * q + 4, :].bitcast(I32),
+                                  in_=osc[g][32 * q:32 * q + 4, :].bitcast(I32))
+
+        ilv("wd0", "S", 3, 4)
+        ilv("wd0", "V", 0, 3)
+        x_turn(0, ("S", "S"))
+        quant_d(0)
+        ilv("wd1", "V", 0, 2)
+        x_quant(0)
+        ilv("wd1", "V", 2, 4)
+
+        jobs = {}
+        for s, kind, n, h in (
+            (-1, 'G', 'wd3', 1),
+            (-1, 'G', 'wd3', 0),
+            (-1, 'S', 'wd2', 0),
+            (-1, 'G', 'wp1', 1),
+            (-1, 'S', 'wd2', 1),
+            (0, 'G', 'wp1', 0),
+            (0, 'S', 'wp0', 0),
+            (1, 'QD', 1, 0),
+            (1, 'QD', 3, 0),
+            (1, 'XT', 1, 0),
+            (1, 'QD', 2, 0),
+            (2, 'G', 'wp2', 0),
+            (3, 'G', 'wu2', 1),
+            (3, 'G', 'wp2', 1),
+            (4, 'XQ', 1, 0),
+            (4, 'G', 'wu0', 1),
+            (5, 'G', 'wu2', 0),
+            (6, 'S', 'wu1', 1),
+            (6, 'S', 'wp0', 1),
+            (7, 'S', 'wu1', 0),
+            (9, 'SM', 0, 0),
+            (9, 'S', 'wu0', 0),
+            (10, 'SM', 0, 1),
+            (10, 'G', 'wu3', 1),
+            (14, 'QP', 0, 0),
+            (15, 'SM', 0, 2),
+            (15, 'SM', 1, 0),
+            (15, 'QP', 1, 0),
+            (16, 'S', 'wp3', 0),
+            (17, 'SM', 1, 1),
+            (19, 'SM', 1, 2),
+            (19, 'S', 'wp3', 1),
+            (19, 'QP', 2, 0),
+            (21, 'G', 'wu3', 0),
+            (21, 'QP', 3, 0),
+            (27, 'OI', 'G', 2),
+            (29, 'OI', 'S', 0),
+            (31, 'OI', 'S', 3),
+            (31, 'OI', 'S', 1),
+            (31, 'OQ', 0, 0),
+        ):
+            jobs.setdefault(s, []).append((kind, n, h))
+
+        def do_job(kind, n, h):
+            if kind == "QD":
+                quant_d(n)
+            elif kind == "QP":
+                quant_p(n)
+            elif kind == "XT":
+                x_turn(1, ("S", "S"))
+            elif kind == "XQ":
+                x_quant(1)
+            elif kind == "SM":
+                soft_step(n, h)
+            elif kind == "OI":
+                o_ilv(0, n, 128 * h, 128 * (h + 1))
+            elif kind == "OQ":
+                o_quant(0)
+            elif kind == "PE":
+                pe_turn(n, h)
+            elif kind == "ES":
+                pe_out(n, h)
+            else:
+                ilv(n, kind, 2 * h, 2 * h + 2)
+
+        added = set()
+
+        def flush(k):
+            for i in range(PAIRS):
+                if i not in added and (i <= k - 1 and k in CLUSTERS if i in VADDS else i <= k - 1):
+                    added.add(i)
+                    b_add(i)
+
+        for s in range(-1, PAIRS + LEAD):
+            if 0 <= s < PAIRS:
+                a_pair(s)
+            if s > 0 and s % 2 == 0 and s <= PAIRS:
+                b_quant((s // 2 - 1) // E, (s // 2 - 1) % E)
+            k = s - LEAD
+            for job in jobs.get(s, []):
+                if job[0] == "SM":
+                    do_job(*job)
+            if k >= 0:
+                b_pair(k)
+                flush(k)
+            for job in jobs.get(s, []):
+                if job[0] != "SM":
+                    do_job(*job)
+        flush(99)
+        o_ilv(1, "S", 352, 512)
+        o_ilv(1, "V", 0, 352)
+        o_quant(1)

@@ -1,4 +1,3 @@
-import math
 from contextlib import ExitStack
 
 import concourse.mybir as mybir
@@ -20,17 +19,14 @@ AX = mybir.AxisListType
 P = 128
 PACK = 4
 GROUP = 512
-LOG2E = math.log2(math.e)
+G = T // GROUP
+S_SHARE_A = 80
+S_SHARE_HEAD = 40
+V_SHARE_TAIL = 352
 
 
 def tile_autonomyofexpertsnormgate_x1_kernel(tc, x, wdown, rgain, wup, wp, out_0, out_1, out_2):
     nc = tc.nc
-    G = T // GROUP
-    PAIRS = G * E * 2
-    LEAD = 18
-    VADDS = (2, 5, 10, 12, 14, 15, )
-    SB = ()
-    CLUSTERS = (5, 7, 9, 11, 13, 99, )
 
     with ExitStack() as ctx:
         keep = ctx.enter_context(tc.tile_pool(name="keep", bufs=1))
@@ -39,349 +35,222 @@ def tile_autonomyofexpertsnormgate_x1_kernel(tc, x, wdown, rgain, wup, wp, out_0
         ctx.enter_context(tc.manual_schedule())
         gain = keep.tile([P, E, 16], BF16, name="gain")
         ident = keep.tile([P, P], F32, name="ident")
-        ident_b = keep.tile([P, P], BF16, name="ident_b")
-        gain32 = keep.tile([P, E, PACK], F32, name="gain32")
-        half = keep.tile([P, 16], F32, name="half")
-        two = keep.tile([P, 16], F32, name="two")
-        minus = keep.tile([P, 4], F32, name="minus")
+        half = keep.tile([P, PACK], F32, name="half")
         warm = keep.tile([P, 1], F32, name="warm")
-        x_raw = [keep.tile([P, PACK, D], BF16, name="x_raw%d" % g, align_bytes=64) for g in range(G)]
-        names = ["wd%d" % e for e in range(E)] + ["wp%d" % e for e in range(E)] + ["wu%d" % e for e in range(E)]
-        raw = {n: keep.tile([P, PACK, 512], BF16, name="raw_" + n, align_bytes=64) for n in names}
-        xc = [keep.tile([P, GROUP], U32, name="xc%d" % g, align_bytes=64) for g in range(G)]
-        xs = [keep.tile([P, GROUP], U8, name="xs%d" % g, align_bytes=64) for g in range(G)]
-        dcodes = [keep.tile([P, 512], U32, name="dcodes%d" % e, align_bytes=64) for e in range(E)]
-        dscales = [keep.tile([P, 512], U8, name="dscales%d" % e, align_bytes=64) for e in range(E)]
-        dgrp = [keep.tile([P, 512, PACK], BF16, name="dgrp%d" % e, align_bytes=64) for e in range(E)]
-        pcodes = [keep.tile([P, 2, 512], U32, name="pcodes%d" % e, align_bytes=64) for e in range(E)]
-        pscales = [keep.tile([P, 2, 512], U8, name="pscales%d" % e, align_bytes=64) for e in range(E)]
-        pgrp = [keep.tile([P, 2, 512, PACK], BF16, name="pgrp%d" % e, align_bytes=64) for e in range(E)]
-        sumsq = [keep.tile([P, PACK, E], F32, name="sumsq%d" % g) for g in range(G)]
-        gate = [keep.tile([P, PACK, E], F32, name="gate%d" % g) for g in range(G)]
-        acc = [keep.tile([P, PACK, F], F32, name="acc%d" % g) for g in range(G)]
-
+        x_raw = {(g, h): keep.tile([P, 2 * D], BF16, name="x_raw%d%d" % (g, h), align_bytes=64)
+                 for g in range(G) for h in range(2)}
         src = {}
         for e in range(E):
-            src["wd%d" % e] = wdown[e]
-            src["wp%d" % e] = wp[e]
-            src["wu%d" % e] = wup[e]
+            src["wd", e], src["wp", e], src["wu", e] = wdown[e], wp[e], wup[e]
+        raw = {n: keep.tile([P, PACK, 512], BF16, name="raw_%s%d" % n, align_bytes=64) for n in src}
+        grp = {n: keep.tile([P, 512, PACK], BF16, name="grp_%s%d" % n, align_bytes=64) for n in src}
+        wc = {n: keep.tile([P, 512], U32, name="wc_%s%d" % n, align_bytes=64) for n in src}
+        ws = {n: keep.tile([P, 512], U8, name="ws_%s%d" % n, align_bytes=64) for n in src}
+        xg = [keep.tile([P, GROUP, PACK], BF16, name="xg%d" % g, align_bytes=64) for g in range(G)]
+        xc = [keep.tile([P, GROUP], U32, name="xc%d" % g, align_bytes=64) for g in range(G)]
+        xs = [keep.tile([P, GROUP], U8, name="xs%d" % g, align_bytes=64) for g in range(G)]
+        sumsq = {(e, g): keep.tile([P, PACK], F32, name="sumsq%d%d" % (e, g)) for e in range(E) for g in range(G)}
+        gate = [keep.tile([P, PACK, E], F32, name="gate%d" % g) for g in range(G)]
+        res = [keep.tile([P, PACK, F], F32, name="res%d" % g) for g in range(G)]
 
-        nc.scalar.dma_start(out=gain[:, :, 0:PACK], in_=rgain.rearrange("e (p t) -> p e t", t=PACK))
+        def tokens(ap, g):
+            return ap[g * GROUP:(g + 1) * GROUP, :].rearrange("(p t) d -> p t d", t=PACK)
 
-        def load_x(g):
-            nc.sync.dma_start(out=x_raw[g][:], in_=x[g * GROUP:(g + 1) * GROUP, :].rearrange("(p t) d -> p t d", t=PACK))
+        def load_x(g, h):
+            nc.sync.dma_start(out=x_raw[g, h][:].rearrange("p (s d) -> p s d", s=2), in_=tokens(x, g)[:, 2 * h:2 * h + 2, :])
 
         def load_w(n):
             nc.sync.dma_start(out=raw[n][:], in_=src[n].rearrange("(p j) c -> p j c", j=PACK))
 
-        load_w("wd0")
-        load_x(0)
-        for n in ("wd1", "wd2", "wd3", "wp0", "wu0"):
-            load_w(n)
-        load_x(1)
-        for n in ("wp1", "wu1", "wp2", "wu2", "wp3", "wu3"):
-            load_w(n)
+        nc.scalar.dma_start(out=gain[:, :, 0:PACK], in_=rgain.rearrange("e (p t) -> p e t", t=PACK))
+        load_x(0, 0)
+        load_w(("wd", 0))
+        load_x(0, 1)
+        load_x(1, 0)
+        load_x(1, 1)
+        for e in range(1, E):
+            load_w(("wd", e))
+        for e in range(E):
+            load_w(("wp", e))
+            load_w(("wu", e))
 
         nc.vector.memset(warm[:], 0.0)
         nc.scalar.activation(out=warm[:], in_=warm[:], func=ACT.Silu)
-        nc.vector.tensor_copy(out=gain32[:], in_=gain[:, :, 0:PACK])
         make_identity(nc, ident[:])
-        nc.gpsimd.tensor_copy(out=ident_b[:], in_=ident[:])
         nc.gpsimd.memset(half[:], 0.5)
-        nc.gpsimd.memset(two[:], 2.0)
-        nc.gpsimd.memset(minus[:], -1.0)
-
-        def copy_on(eng, out, in_):
-            if eng == "V":
-                nc.vector.tensor_copy(out=out, in_=in_)
-            elif eng == "S":
-                nc.scalar.copy(out=out, in_=in_)
-            else:
-                nc.gpsimd.tensor_scalar(out=out, in0=in_, scalar1=1.0, scalar2=0.0, op0=ALU.mult, op1=ALU.add)
-
-        def ilv(n, eng, lo=0, hi=4):
-            e = int(n[2:])
-            if n.startswith("wd"):
-                copy_on(eng, dgrp[e][:].rearrange("p (t m) j -> p t m j", t=4)[:, lo:hi],
-                        raw[n][:].rearrange("p j (m t) -> p t m j", t=4)[:, lo:hi])
-            else:
-                w = 0 if n.startswith("wp") else 1
-                copy_on(eng, pgrp[e][:, w, 128 * lo:128 * hi, :], raw[n][:, :, 128 * lo:128 * hi].rearrange("p j c -> p c j"))
-
-        banks = {}
-
-        def pe_turn(n, h):
-            bank = psum.tile([P, 1024], BF16, name="pw", tag="ps", bufs=4)
-            banks[n, h] = bank
-            for q in range(2):
-                c0 = 256 * h + 128 * q
-                nc.tensor.matmul(out=bank[:, 512 * q:512 * (q + 1)].rearrange("p (m j) -> p m j", j=PACK), lhsT=ident_b[:],
-                                 rhs=raw[n][:, :, c0:c0 + 128].rearrange("p j m -> p m j"), start=True, stop=True)
-
-        def pe_out(n, h):
-            w = 0 if n.startswith("wp") else 1
-            nc.scalar.copy(out=pgrp[int(n[2:])][:, w, 256 * h:256 * (h + 1), :].rearrange("p m j -> p (m j)"), in_=banks[n, h][:])
-
-        def quant_d(e):
-            nc.vector.quantize_mx(out=dcodes[e][:].bitcast(FP8X4), scales=dscales[e][:],
-                                  in_=dgrp[e][:].rearrange("p c j -> p (c j)"))
-
-        def quant_p(e):
-            nc.vector.quantize_mx(out=pcodes[e][:].rearrange("p w c -> p (w c)").bitcast(FP8X4),
-                                  scales=pscales[e][:].rearrange("p w c -> p (w c)"),
-                                  in_=pgrp[e][:].rearrange("p w c j -> p (w c j)"))
-
-        xg = {}
-
-        def x_turn(g, engs):
-            xg[g] = work.tile([P, GROUP, PACK], BF16, name="xgrp", align_bytes=64, bufs=1)
-            words = x_raw[g][:].rearrange("p t d -> p (t d)").bitcast(F32)
-            dstw = xg[g][:].rearrange("p c j -> p (c j)").bitcast(F32).rearrange("p (s r u) -> p s r u", r=P, u=2)
-            for h in range(2):
-                bank = psum.tile([P, 512], F32, name="pt", tag="ps", bufs=4)
-                view = bank[:].rearrange("p (s u r) -> p s u r", s=2, u=2)
-                for s in range(2):
-                    t = 2 * h + s
-                    for u in range(2):
-                        nc.tensor.transpose(view[:, s, u, :], words[:, 256 * t + u:256 * (t + 1):2], ident[:])
-                copy_on(engs[h], dstw[:, 2 * h:2 * h + 2], view.rearrange("p s u r -> p s r u"))
-
-        def x_quant(g):
-            nc.vector.quantize_mx(out=xc[g][:].bitcast(FP8X4), scales=xs[g][:],
-                                  in_=xg[g][:].rearrange("p c j -> p (c j)"))
-
-        bgrp = {}
-        bcodes = {}
-        bscales = {}
 
         def cols(t):
             return slice(P * t, P * (t + 1))
 
-        def a_pair(i):
-            g, e, h = i // 8, (i // 2) % 4, i % 2
-            ts = (2 * h, 2 * h + 1)
-            wc, ws = dcodes[e], dscales[e]
-            ar = {}
-            at = {}
-            for t in ts:
-                arb = psum.tile([P, 512], F32, name="pa", tag="pv", bufs=4)
-                ar[t] = arb[:].rearrange("p (k n) -> p k n", k=4)
-                for k in range(4):
-                    nc.tensor.matmul_mx(out=ar[t][:, k, :], lhsT=wc[:, cols(k)].bitcast(FP8X4), lhsT_scale=ws[:, cols(k)],
-                                        rhs=xc[g][:, cols(t)].bitcast(FP8X4), rhs_scale=xs[g][:, cols(t)],
-                                        start=True, stop=True)
-            for t in ts:
-                atb = psum.tile([P, 512], F32, name="pb", tag="ps", bufs=4)
-                at[t] = atb
-                nc.tensor.matmul_mx(out=atb[:], lhsT=xc[g][:, cols(t)].bitcast(FP8X4), lhsT_scale=xs[g][:, cols(t)],
-                                    rhs=wc[:].bitcast(FP8X4), rhs_scale=ws[:], start=True, stop=True)
-            if h == 0:
-                bgrp[g, e] = work.tile([P, GROUP, PACK], BF16, name="bgrp", align_bytes=64, bufs=3)
-            for t in reversed(ts):
-                sq = work.tile([P, 512], F32, name="sq", bufs=2)
-                nc.scalar.activation(out=sq[:], in_=at[t][:], func=ACT.Square, accum_out=sumsq[g][:, t, e:e + 1])
-            for t in reversed(ts):
-                if 2 * i + t % 2 in SB:
-                    for k in range(4):
-                        nc.scalar.activation(out=bgrp[g, e][:, cols(t), k], in_=ar[t][:, k, :], func=ACT.Copy,
-                                             scale=gain32[:, e, k:k + 1])
-                    continue
-                nc.vector.tensor_tensor(out=bgrp[g, e][:, cols(t), :], in0=ar[t].rearrange("p k n -> p n k"),
-                                        in1=gain[:, e, 0:PACK].unsqueeze(1).to_broadcast([P, P, PACK]), op=ALU.mult)
+        def ilv_views(n):
+            dst = grp[n][:].rearrange("p (q m) j -> p q m j", q=4)
+            if n[0] == "wd":
+                return dst, raw[n][:].rearrange("p j (m q) -> p q m j", q=4)
+            return dst, raw[n][:].rearrange("p j (q m) -> p q m j", q=4)
 
-        def b_quant(g, e):
-            bcodes[g, e] = keep.tile([P, GROUP], U32, name="bc%d%d" % (g, e), align_bytes=64)
-            bscales[g, e] = keep.tile([P, GROUP], U8, name="bs%d%d" % (g, e), align_bytes=64)
-            nc.vector.quantize_mx(out=bcodes[g, e][:].bitcast(FP8X4), scales=bscales[g, e][:],
-                                  in_=bgrp[g, e][:].rearrange("p c j -> p (c j)"))
+        def ilv_scalar(n, q, share):
+            dst, rows = ilv_views(n)
+            nc.scalar.copy(out=dst[:, q, 0:share, :], in_=rows[:, q, 0:share, :])
 
-        soft = {}
+        def ilv_vector(n, share):
+            dst, rows = ilv_views(n)
+            nc.vector.tensor_copy(out=dst[:, :, share:P, :], in_=rows[:, :, share:P, :])
 
-        def soft_step(g, k):
+        def quant(codes, scales, grouped):
+            nc.vector.quantize_mx(out=codes[:].bitcast(FP8X4), scales=scales[:], in_=grouped[:].rearrange("p c j -> p (c j)"))
+
+        def quant_w(n):
+            quant(wc[n], ws[n], grp[n])
+
+        def x_turn(g, h):
+            words = x_raw[g, h][:].bitcast(F32)
+            dstw = xg[g][:].rearrange("p c j -> p (c j)").bitcast(F32).rearrange("p (s r u) -> p s r u", r=P, u=2)
+            bank = psum.tile([P, 512], F32, name="pt", tag="ps")
+            view = bank[:].rearrange("p (s u r) -> p s u r", s=2, u=2)
+            for s in range(2):
+                for u in range(2):
+                    nc.tensor.transpose(view[:, s, u, :], words[:, 256 * s + u:256 * (s + 1):2], ident[:])
+            nc.scalar.copy(out=dstw[:, 2 * h:2 * h + 2], in_=view.rearrange("p s u r -> p s r u"))
+
+        bgrp, bc, bs = {}, {}, {}
+
+        def a_unit(e, g, t):
+            n = ("wd", e)
+            ranks = psum.tile([P, 512], F32, name="pa", tag="pv")
+            for k in range(PACK):
+                nc.tensor.matmul_mx(out=ranks[:, cols(k)], lhsT=wc[n][:, cols(k)].bitcast(FP8X4), lhsT_scale=ws[n][:, cols(k)],
+                                    rhs=xc[g][:, cols(t)].bitcast(FP8X4), rhs_scale=xs[g][:, cols(t)], start=True, stop=True)
+            toks = psum.tile([P, 512], F32, name="pb", tag="ps")
+            nc.tensor.matmul_mx(out=toks[:], lhsT=xc[g][:, cols(t)].bitcast(FP8X4), lhsT_scale=xs[g][:, cols(t)],
+                                rhs=wc[n][:].bitcast(FP8X4), rhs_scale=ws[n][:], start=True, stop=True)
+            if t == 0:
+                bgrp[e, g] = work.tile([P, GROUP, PACK], BF16, name="bgrp", align_bytes=64, bufs=2)
+            nc.vector.tensor_tensor(out=bgrp[e, g][:, cols(t), :], in0=ranks[:].rearrange("p (k n) -> p n k", k=PACK),
+                                    in1=gain[:, e, 0:PACK].unsqueeze(1).to_broadcast([P, P, PACK]), op=ALU.mult)
+            sq = work.tile([P, 512], BF16, name="sq", bufs=2)
+            nc.scalar.activation(out=sq[:], in_=toks[:], func=ACT.Square, scale=0.5, accum_out=sumsq[e, g][:, t:t + 1])
+
+        def b_quant(e, g):
+            bc[e, g] = keep.tile([P, GROUP], U32, name="bc%d%d" % (e, g), align_bytes=64)
+            bs[e, g] = keep.tile([P, GROUP], U8, name="bs%d%d" % (e, g), align_bytes=64)
+            quant(bc[e, g], bs[e, g], bgrp[e, g])
+
+        def small(name, width):
+            return [keep.tile([P, PACK, width], F32, name="%s%d" % (name, g)) for g in range(G)]
+
+        score, diff, th, rest, quot, ex = (small(name, E) for name in ("score", "diff", "th", "rest", "quot", "ex"))
+        s2, top, den, inv = small("s2", 2), small("top", 1), small("den", 1), small("inv", 1)
+
+        def over_experts(tile):
+            return tile[:].to_broadcast([P, PACK, E])
+
+        def half_score(e, g):
+            nc.gpsimd.tensor_tensor(out=score[g][:, :, e], in0=sumsq[e, g][:], in1=half[:], op=ALU.pow)
+
+        def gate_part(g, k):
             if k == 0:
-                soft["sc", g] = keep.tile([P, PACK, E], F32, name="sc%d" % g)
-                soft["mx", g] = keep.tile([P, PACK], F32, name="mx%d" % g)
-                soft["ex", g] = keep.tile([P, PACK, E], F32, name="ex%d" % g)
-                soft["s2", g] = keep.tile([P, PACK, 2], F32, name="s2%d" % g)
-                soft["sm", g] = keep.tile([P, PACK], F32, name="sm%d" % g)
-                nc.gpsimd.tensor_tensor(out=soft["sc", g][:].rearrange("p t e -> p (t e)"),
-                                        in0=sumsq[g][:].rearrange("p t e -> p (t e)"), in1=half[:], op=ALU.pow)
-                nc.gpsimd.tensor_scalar(out=soft["sc", g][:], in0=soft["sc", g][:], scalar1=LOG2E, scalar2=0.0,
-                                        op0=ALU.mult, op1=ALU.add)
+                nc.vector.tensor_reduce(out=top[g][:, :, 0], in_=score[g][:], axis=AX.X, op=ALU.max)
+                nc.gpsimd.tensor_tensor(out=diff[g][:], in0=score[g][:], in1=over_experts(top[g]), op=ALU.subtract)
             elif k == 1:
-                nc.vector.tensor_reduce(out=soft["mx", g][:], in_=soft["sc", g][:], axis=AX.X, op=ALU.max)
+                nc.scalar.activation(out=th[g][:], in_=diff[g][:], func=ACT.Tanh)
+                nc.gpsimd.tensor_scalar(out=rest[g][:], in0=th[g][:], scalar1=-1.0, scalar2=1.0, op0=ALU.mult, op1=ALU.add)
+            elif k == 2:
+                nc.vector.reciprocal(out=quot[g][:], in_=rest[g][:])
+                nc.gpsimd.tensor_scalar(out=ex[g][:], in0=quot[g][:], scalar1=2.0, scalar2=-1.0, op0=ALU.mult, op1=ALU.add)
+                nc.gpsimd.tensor_tensor(out=s2[g][:], in0=ex[g][:, :, 0:2], in1=ex[g][:, :, 2:4], op=ALU.add)
+                nc.gpsimd.tensor_tensor(out=den[g][:], in0=s2[g][:, :, 0:1], in1=s2[g][:, :, 1:2], op=ALU.add)
             else:
-                ex = soft["ex", g]
-                nc.gpsimd.tensor_tensor(out=soft["sc", g][:], in0=soft["sc", g][:],
-                                        in1=soft["mx", g][:].unsqueeze(2).to_broadcast([P, PACK, E]), op=ALU.subtract)
-                nc.gpsimd.tensor_tensor(out=ex[:].rearrange("p t e -> p (t e)"), in0=two[:],
-                                        in1=soft["sc", g][:].rearrange("p t e -> p (t e)"), op=ALU.pow)
-                nc.gpsimd.tensor_tensor(out=soft["s2", g][:], in0=ex[:, :, 0:2], in1=ex[:, :, 2:4], op=ALU.add)
-                nc.gpsimd.tensor_tensor(out=soft["sm", g][:], in0=soft["s2", g][:, :, 0], in1=soft["s2", g][:, :, 1], op=ALU.add)
-                nc.gpsimd.tensor_tensor(out=soft["mx", g][:], in0=soft["sm", g][:], in1=minus[:], op=ALU.pow)
-                nc.gpsimd.tensor_tensor(out=gate[g][:], in0=ex[:], in1=soft["mx", g][:].unsqueeze(2).to_broadcast([P, PACK, E]),
-                                        op=ALU.mult)
+                nc.vector.reciprocal(out=inv[g][:], in_=den[g][:])
+                nc.gpsimd.tensor_tensor(out=gate[g][:], in0=ex[g][:], in1=over_experts(inv[g]), op=ALU.mult)
 
-        ypair = {}
+        term = {}
 
-        def b_pair(i):
-            g, e, h = i // 8, (i // 2) % 4, i % 2
-            ts = (2 * h, 2 * h + 1)
-            pps = {}
-            ups = {}
-            for t in ts:
-                pb_ = psum.tile([P, 512], F32, name="pp", tag="pv", bufs=4)
-                pps[t] = pb_
-                nc.tensor.matmul_mx(out=pb_[:], lhsT=xc[g][:, cols(t)].bitcast(FP8X4), lhsT_scale=xs[g][:, cols(t)],
-                                    rhs=pcodes[e][:, 0, :].bitcast(FP8X4), rhs_scale=pscales[e][:, 0, :], start=True, stop=True)
-            for t in ts:
-                ub_ = psum.tile([P, 512], F32, name="pu", tag="ps", bufs=4)
-                ups[t] = ub_
-                nc.tensor.matmul_mx(out=ub_[:], lhsT=bcodes[g, e][:, cols(t)].bitcast(FP8X4), lhsT_scale=bscales[g, e][:, cols(t)],
-                                    rhs=pcodes[e][:, 1, :].bitcast(FP8X4), rhs_scale=pscales[e][:, 1, :], start=True, stop=True)
-            sl = work.tile([P, 2, F], F32, name="sl", bufs=3)
-            if e > 0:
-                ypair[i] = work.tile([P, 2, F], F32, name="y", bufs=4)
-            for t in reversed(ts):
-                nc.scalar.activation(out=sl[:, t - 2 * h, :], in_=ups[t][:], func=ACT.Silu)
-            for t in ts:
-                dst = acc[g][:, t, :] if e == 0 else ypair[i][:, t - 2 * h, :]
-                nc.vector.scalar_tensor_tensor(out=dst, in0=pps[t][:], scalar=gate[g][:, t, e:e + 1], in1=sl[:, t - 2 * h, :],
-                                               op0=ALU.mult, op1=ALU.mult)
+        def b_unit(e, g, t):
+            lin = psum.tile([P, 512], F32, name="pp", tag="pv")
+            up = psum.tile([P, 512], F32, name="pu", tag="ps")
+            nc.tensor.matmul_mx(out=up[:], lhsT=bc[e, g][:, cols(t)].bitcast(FP8X4), lhsT_scale=bs[e, g][:, cols(t)],
+                                rhs=wc["wu", e][:].bitcast(FP8X4), rhs_scale=ws["wu", e][:], start=True, stop=True)
+            nc.tensor.matmul_mx(out=lin[:], lhsT=xc[g][:, cols(t)].bitcast(FP8X4), lhsT_scale=xs[g][:, cols(t)],
+                                rhs=wc["wp", e][:].bitcast(FP8X4), rhs_scale=ws["wp", e][:], start=True, stop=True)
+            act = work.tile([P, F], F32, name="act", bufs=4)
+            nc.scalar.activation(out=act[:], in_=up[:], func=ACT.Silu)
+            term[e, g, t] = res[g][:, t, :] if e == 0 else work.tile([P, F], F32, name="term", bufs=3)[:]
+            nc.vector.scalar_tensor_tensor(out=term[e, g, t], in0=lin[:], scalar=gate[g][:, t, e:e + 1], in1=act[:],
+                                           op0=ALU.mult, op1=ALU.mult)
 
-        summed = {}
-
-        def b_add(i):
-            g, e, h = i // 8, (i // 2) % 4, i % 2
+        def b_add(e, g, t):
             if e == 0:
                 return
-            half_ = acc[g][:, 2 * h:2 * h + 2, :]
-            eng = nc.vector if i in VADDS else nc.gpsimd
-            eng.tensor_tensor(out=half_, in0=half_, in1=ypair[i][:], op=ALU.add)
-            summed[g, h] = summed.get((g, h), 0) + 1
-            if summed[g, h] == E - 1:
-                nc.sync.dma_start(out=out_0[g * GROUP:(g + 1) * GROUP, :].rearrange("(p t) f -> p t f", t=PACK)[:, 2 * h:2 * h + 2, :],
-                                  in_=half_)
+            dst = res[g][:, t, :]
+            nc.vector.tensor_tensor(out=dst, in0=dst, in1=term[e, g, t], op=ALU.add)
+            if e == E - 1:
+                nc.sync.dma_start(out=tokens(out_0, g)[:, t, :], in_=dst)
 
-        og = {}
-        oc = {}
-        osc = {}
+        og = [keep.tile([P, F, PACK], BF16, name="og%d" % g, align_bytes=64) for g in range(G)]
+        oc = [keep.tile([P, F], U32, name="oc%d" % g, align_bytes=64) for g in range(G)]
+        osc = [keep.tile([P, F], U8, name="osc%d" % g, align_bytes=64) for g in range(G)]
 
-        def o_ilv(g, eng, lo, hi):
-            assert all(summed[g, h] == E - 1 for h in range(2))
-            if g not in og:
-                og[g] = work.tile([P, F, PACK], BF16, name="og", align_bytes=64, bufs=1)
-            copy_on(eng, og[g][:, lo:hi, :], acc[g][:].rearrange("p t f -> p f t")[:, lo:hi, :])
+        def o_views(g, lo, hi):
+            return og[g][:, lo:hi, :], res[g][:].rearrange("p t f -> p f t")[:, lo:hi, :]
 
         def o_quant(g):
-            oc[g] = keep.tile([P, F], U32, name="oc%d" % g, align_bytes=64)
-            osc[g] = keep.tile([P, F], U8, name="osc%d" % g, align_bytes=64)
-            nc.vector.quantize_mx(out=oc[g][:].bitcast(FP8X4), scales=osc[g][:],
-                                  in_=og[g][:].rearrange("p c j -> p (c j)"))
+            quant(oc[g], osc[g], og[g])
             nc.sync.dma_start(out=out_1[g].rearrange("p m b -> p (m b)").bitcast(I32), in_=oc[g][:].bitcast(I32))
             for q in range(4):
-                nc.sync.dma_start(out=out_2[g, 4 * q:4 * q + 4, :].bitcast(I32),
-                                  in_=osc[g][32 * q:32 * q + 4, :].bitcast(I32))
+                nc.sync.dma_start(out=out_2[g, 4 * q:4 * q + 4, :].bitcast(I32), in_=osc[g][32 * q:32 * q + 4, :].bitcast(I32))
 
-        ilv("wd0", "S", 3, 4)
-        ilv("wd0", "V", 0, 3)
-        x_turn(0, ("S", "S"))
-        quant_d(0)
-        ilv("wd1", "V", 0, 2)
-        x_quant(0)
-        ilv("wd1", "V", 2, 4)
+        x_turn(0, 0)
+        for q in range(4):
+            ilv_scalar(("wd", 0), q, S_SHARE_HEAD)
+        ilv_vector(("wd", 0), S_SHARE_HEAD)
+        x_turn(0, 1)
+        quant_w(("wd", 0))
+        quant(xc[0], xs[0], xg[0])
+        x_turn(1, 0)
+        x_turn(1, 1)
 
-        jobs = {}
-        for s, kind, n, h in (
-            (-1, 'G', 'wd3', 1),
-            (-1, 'G', 'wd3', 0),
-            (-1, 'S', 'wd2', 0),
-            (-1, 'G', 'wp1', 1),
-            (-1, 'S', 'wd2', 1),
-            (0, 'G', 'wp1', 0),
-            (0, 'S', 'wp0', 0),
-            (1, 'QD', 1, 0),
-            (1, 'QD', 3, 0),
-            (1, 'XT', 1, 0),
-            (1, 'QD', 2, 0),
-            (2, 'G', 'wp2', 0),
-            (3, 'G', 'wu2', 1),
-            (3, 'G', 'wp2', 1),
-            (4, 'XQ', 1, 0),
-            (4, 'G', 'wu0', 1),
-            (5, 'G', 'wu2', 0),
-            (6, 'S', 'wu1', 1),
-            (6, 'S', 'wp0', 1),
-            (7, 'S', 'wu1', 0),
-            (9, 'SM', 0, 0),
-            (9, 'S', 'wu0', 0),
-            (10, 'SM', 0, 1),
-            (10, 'G', 'wu3', 1),
-            (14, 'QP', 0, 0),
-            (15, 'SM', 0, 2),
-            (15, 'SM', 1, 0),
-            (15, 'QP', 1, 0),
-            (16, 'S', 'wp3', 0),
-            (17, 'SM', 1, 1),
-            (19, 'SM', 1, 2),
-            (19, 'S', 'wp3', 1),
-            (19, 'QP', 2, 0),
-            (21, 'G', 'wu3', 0),
-            (21, 'QP', 3, 0),
-            (27, 'OI', 'G', 2),
-            (29, 'OI', 'S', 0),
-            (31, 'OI', 'S', 3),
-            (31, 'OI', 'S', 1),
-            (31, 'OQ', 0, 0),
-        ):
-            jobs.setdefault(s, []).append((kind, n, h))
+        steps = [(0, 0), (0, 1), (1, 0), (1, 1), (2, 0), (3, 0), (2, 1), (3, 1)]
+        later = [("wd", 1), ("wd", 2), ("wd", 3), ("wp", 0), ("wu", 0), ("wp", 1), ("wu", 1)]
+        for s, (e, g) in enumerate(steps):
+            for t in range(PACK):
+                a_unit(e, g, t)
+                if s < len(later):
+                    ilv_scalar(later[s], t, S_SHARE_A)
+                if t == 1:
+                    if s == 0:
+                        quant(xc[1], xs[1], xg[1])
+                    else:
+                        quant_w(later[s - 1])
+                        b_quant(*steps[s - 1])
+                    if s < len(later):
+                        ilv_vector(later[s], S_SHARE_A)
+                if s >= len(steps) - 2 and t % 2 == 1:
+                    gate_part(0, 2 * (s - len(steps) + 2) + t // 2)
+            half_score(e, g)
 
-        def do_job(kind, n, h):
-            if kind == "QD":
-                quant_d(n)
-            elif kind == "QP":
-                quant_p(n)
-            elif kind == "XT":
-                x_turn(1, ("S", "S"))
-            elif kind == "XQ":
-                x_quant(1)
-            elif kind == "SM":
-                soft_step(n, h)
-            elif kind == "OI":
-                o_ilv(0, n, 128 * h, 128 * (h + 1))
-            elif kind == "OQ":
-                o_quant(0)
-            elif kind == "PE":
-                pe_turn(n, h)
-            elif kind == "ES":
-                pe_out(n, h)
-            else:
-                ilv(n, kind, 2 * h, 2 * h + 2)
-
-        added = set()
-
-        def flush(k):
-            for i in range(PAIRS):
-                if i not in added and (i <= k - 1 and k in CLUSTERS if i in VADDS else i <= k - 1):
-                    added.add(i)
-                    b_add(i)
-
-        for s in range(-1, PAIRS + LEAD):
-            if 0 <= s < PAIRS:
-                a_pair(s)
-            if s > 0 and s % 2 == 0 and s <= PAIRS:
-                b_quant((s // 2 - 1) // E, (s // 2 - 1) % E)
-            k = s - LEAD
-            for job in jobs.get(s, []):
-                if job[0] == "SM":
-                    do_job(*job)
-            if k >= 0:
-                b_pair(k)
-                flush(k)
-            for job in jobs.get(s, []):
-                if job[0] != "SM":
-                    do_job(*job)
-        flush(99)
-        o_ilv(1, "S", 352, 512)
-        o_ilv(1, "V", 0, 352)
+        pairs = [(0, 0), (1, 0), (0, 1), (1, 1), (2, 0), (2, 1), (3, 0), (3, 1)]
+        last = [("wp", 2), ("wu", 2), ("wp", 3), ("wu", 3)]
+        units = [(e, g, t) for e, g in pairs for t in range(PACK)]
+        for i, (e, g, t) in enumerate(units):
+            s = i // PACK
+            b_unit(e, g, t)
+            if i > 0:
+                b_add(*units[i - 1])
+            if i == 0:
+                b_quant(*steps[-1])
+            if s < 2 and t % 2 == 1:
+                gate_part(1, 2 * s + t // 2)
+            if 1 <= s <= len(last):
+                ilv_scalar(last[s - 1], t, P)
+            if 2 <= s <= len(last) + 1 and t == 1:
+                quant_w(last[s - 2])
+            if s == len(pairs) - 1:
+                dst, rows = o_views(0, P * t, P * (t + 1))
+                nc.scalar.copy(out=dst, in_=rows)
+        b_add(*units[-1])
+        o_quant(0)
+        dst, rows = o_views(1, V_SHARE_TAIL, F)
+        nc.scalar.copy(out=dst, in_=rows)
+        dst, rows = o_views(1, 0, V_SHARE_TAIL)
+        nc.vector.tensor_copy(out=dst, in_=rows)
         o_quant(1)

@@ -23,6 +23,7 @@ G = T // GROUP
 S_SHARE_A = 80
 S_SHARE_HEAD = 40
 V_SHARE_TAIL = 352
+LEAD = 2
 
 
 def tile_autonomyofexpertsnormgate_x1_kernel(tc, x, wdown, rgain, wup, wp, out_0, out_1, out_2):
@@ -35,7 +36,6 @@ def tile_autonomyofexpertsnormgate_x1_kernel(tc, x, wdown, rgain, wup, wp, out_0
         ctx.enter_context(tc.manual_schedule())
         gain = keep.tile([P, E, 16], BF16, name="gain")
         ident = keep.tile([P, P], F32, name="ident")
-        half = keep.tile([P, PACK], F32, name="half")
         warm = keep.tile([P, 1], F32, name="warm")
         x_raw = {(g, h): keep.tile([P, 2 * D], BF16, name="x_raw%d%d" % (g, h), align_bytes=64)
                  for g in range(G) for h in range(2)}
@@ -49,7 +49,7 @@ def tile_autonomyofexpertsnormgate_x1_kernel(tc, x, wdown, rgain, wup, wp, out_0
         xg = [keep.tile([P, GROUP, PACK], BF16, name="xg%d" % g, align_bytes=64) for g in range(G)]
         xc = [keep.tile([P, GROUP], U32, name="xc%d" % g, align_bytes=64) for g in range(G)]
         xs = [keep.tile([P, GROUP], U8, name="xs%d" % g, align_bytes=64) for g in range(G)]
-        sumsq = {(e, g): keep.tile([P, PACK], F32, name="sumsq%d%d" % (e, g)) for e in range(E) for g in range(G)}
+        sumsq = [keep.tile([P, PACK, E], F32, name="sumsq%d" % g) for g in range(G)]
         gate = [keep.tile([P, PACK, E], F32, name="gate%d" % g) for g in range(G)]
         res = [keep.tile([P, PACK, F], F32, name="res%d" % g) for g in range(G)]
 
@@ -75,9 +75,8 @@ def tile_autonomyofexpertsnormgate_x1_kernel(tc, x, wdown, rgain, wup, wp, out_0
             load_w(("wu", e))
 
         nc.vector.memset(warm[:], 0.0)
-        nc.scalar.activation(out=warm[:], in_=warm[:], func=ACT.Silu)
+        nc.scalar.activation(out=warm[:], in_=warm[:], func=ACT.Sqrt)
         make_identity(nc, ident[:])
-        nc.gpsimd.memset(half[:], 0.5)
 
         def cols(t):
             return slice(P * t, P * (t + 1))
@@ -120,15 +119,18 @@ def tile_autonomyofexpertsnormgate_x1_kernel(tc, x, wdown, rgain, wup, wp, out_0
             for k in range(PACK):
                 nc.tensor.matmul_mx(out=ranks[:, cols(k)], lhsT=wc[n][:, cols(k)].bitcast(FP8X4), lhsT_scale=ws[n][:, cols(k)],
                                     rhs=xc[g][:, cols(t)].bitcast(FP8X4), rhs_scale=xs[g][:, cols(t)], start=True, stop=True)
-            toks = psum.tile([P, 512], F32, name="pb", tag="ps")
-            nc.tensor.matmul_mx(out=toks[:], lhsT=xc[g][:, cols(t)].bitcast(FP8X4), lhsT_scale=xs[g][:, cols(t)],
-                                rhs=wc[n][:].bitcast(FP8X4), rhs_scale=ws[n][:], start=True, stop=True)
             if t == 0:
                 bgrp[e, g] = work.tile([P, GROUP, PACK], BF16, name="bgrp", align_bytes=64, bufs=2)
             nc.vector.tensor_tensor(out=bgrp[e, g][:, cols(t), :], in0=ranks[:].rearrange("p (k n) -> p n k", k=PACK),
                                     in1=gain[:, e, 0:PACK].unsqueeze(1).to_broadcast([P, P, PACK]), op=ALU.mult)
+
+        def sq_unit(e, g, t):
+            n = ("wd", e)
+            toks = psum.tile([P, 512], F32, name="pb", tag="ps")
+            nc.tensor.matmul_mx(out=toks[:], lhsT=xc[g][:, cols(t)].bitcast(FP8X4), lhsT_scale=xs[g][:, cols(t)],
+                                rhs=wc[n][:].bitcast(FP8X4), rhs_scale=ws[n][:], start=True, stop=True)
             sq = work.tile([P, 512], BF16, name="sq", bufs=2)
-            nc.scalar.activation(out=sq[:], in_=toks[:], func=ACT.Square, scale=0.5, accum_out=sumsq[e, g][:, t:t + 1])
+            nc.scalar.activation(out=sq[:], in_=toks[:], func=ACT.Square, scale=0.5, accum_out=sumsq[g][:, t, e:e + 1])
 
         def b_quant(e, g):
             bc[e, g] = keep.tile([P, GROUP], U32, name="bc%d%d" % (e, g), align_bytes=64)
@@ -144,8 +146,8 @@ def tile_autonomyofexpertsnormgate_x1_kernel(tc, x, wdown, rgain, wup, wp, out_0
         def over_experts(tile):
             return tile[:].to_broadcast([P, PACK, E])
 
-        def half_score(e, g):
-            nc.gpsimd.tensor_tensor(out=score[g][:, :, e], in0=sumsq[e, g][:], in1=half[:], op=ALU.pow)
+        def half_score(g):
+            nc.scalar.activation(out=score[g][:], in_=sumsq[g][:], func=ACT.Sqrt)
 
         def gate_part(g, k):
             if k == 0:
@@ -165,24 +167,36 @@ def tile_autonomyofexpertsnormgate_x1_kernel(tc, x, wdown, rgain, wup, wp, out_0
 
         term = {}
 
-        def b_unit(e, g, t):
-            lin = psum.tile([P, 512], F32, name="pp", tag="pv")
+        acts = {}
+
+        def u_unit(e, g, t):
             up = psum.tile([P, 512], F32, name="pu", tag="ps")
             nc.tensor.matmul_mx(out=up[:], lhsT=bc[e, g][:, cols(t)].bitcast(FP8X4), lhsT_scale=bs[e, g][:, cols(t)],
                                 rhs=wc["wu", e][:].bitcast(FP8X4), rhs_scale=ws["wu", e][:], start=True, stop=True)
+            acts[e, g, t] = work.tile([P, F], F32, name="act", bufs=4)
+            nc.scalar.activation(out=acts[e, g, t][:], in_=up[:], func=ACT.Silu)
+
+        def b_unit(e, g, t):
+            lin = psum.tile([P, 512], F32, name="pp", tag="pv")
             nc.tensor.matmul_mx(out=lin[:], lhsT=xc[g][:, cols(t)].bitcast(FP8X4), lhsT_scale=xs[g][:, cols(t)],
                                 rhs=wc["wp", e][:].bitcast(FP8X4), rhs_scale=ws["wp", e][:], start=True, stop=True)
-            act = work.tile([P, F], F32, name="act", bufs=4)
-            nc.scalar.activation(out=act[:], in_=up[:], func=ACT.Silu)
+            act = acts[e, g, t]
             term[e, g, t] = res[g][:, t, :] if e == 0 else work.tile([P, F], F32, name="term", bufs=3)[:]
-            nc.vector.scalar_tensor_tensor(out=term[e, g, t], in0=lin[:], scalar=gate[g][:, t, e:e + 1], in1=act[:],
-                                           op0=ALU.mult, op1=ALU.mult)
+            if e == 0:
+                nc.vector.tensor_tensor(out=term[e, g, t], in0=lin[:], in1=act[:], op=ALU.mult)
+            else:
+                nc.vector.scalar_tensor_tensor(out=term[e, g, t], in0=lin[:], scalar=gate[g][:, t, e:e + 1], in1=act[:],
+                                               op0=ALU.mult, op1=ALU.mult)
 
         def b_add(e, g, t):
             if e == 0:
                 return
             dst = res[g][:, t, :]
-            nc.vector.tensor_tensor(out=dst, in0=dst, in1=term[e, g, t], op=ALU.add)
+            if e == 1:
+                nc.vector.scalar_tensor_tensor(out=dst, in0=dst, scalar=gate[g][:, t, 0:1], in1=term[e, g, t],
+                                               op0=ALU.mult, op1=ALU.add)
+            else:
+                nc.vector.tensor_tensor(out=dst, in0=dst, in1=term[e, g, t], op=ALU.add)
             if e == E - 1:
                 nc.sync.dma_start(out=tokens(out_0, g)[:, t, :], in_=dst)
 
@@ -211,35 +225,50 @@ def tile_autonomyofexpertsnormgate_x1_kernel(tc, x, wdown, rgain, wup, wp, out_0
 
         steps = [(0, 0), (0, 1), (1, 0), (1, 1), (2, 0), (3, 0), (2, 1), (3, 1)]
         later = [("wd", 1), ("wd", 2), ("wd", 3), ("wp", 0), ("wu", 0), ("wp", 1), ("wu", 1)]
-        for s, (e, g) in enumerate(steps):
-            for t in range(PACK):
-                a_unit(e, g, t)
-                if s < len(later):
-                    ilv_scalar(later[s], t, S_SHARE_A)
-                if t == 1:
-                    if s == 0:
-                        quant(xc[1], xs[1], xg[1])
-                    else:
-                        quant_w(later[s - 1])
-                        b_quant(*steps[s - 1])
-                    if s < len(later):
-                        ilv_vector(later[s], S_SHARE_A)
-                if s >= len(steps) - 2 and t % 2 == 1:
-                    gate_part(0, 2 * (s - len(steps) + 2) + t // 2)
-            half_score(e, g)
-
-        pairs = [(0, 0), (1, 0), (0, 1), (1, 1), (2, 0), (2, 1), (3, 0), (3, 1)]
+        a_units = [(e, g, t) for e, g in steps for t in range(PACK)]
+        pairs = [(e, g) for e in range(E) for g in range(G)]
         last = [("wp", 2), ("wu", 2), ("wp", 3), ("wu", 3)]
         units = [(e, g, t) for e, g in pairs for t in range(PACK)]
+
+        def scalar_side(j):
+            if j < len(a_units):
+                e, g, t = a_units[j]
+                sq_unit(e, g, t)
+                if (e, t) == (E - 1, PACK - 1):
+                    half_score(g)
+            elif j < len(a_units) + len(units):
+                u_unit(*units[j - len(a_units)])
+
+        for j in range(LEAD):
+            scalar_side(j)
+        for i, (e, g, t) in enumerate(a_units):
+            s = i // PACK
+            a_unit(e, g, t)
+            scalar_side(i + LEAD)
+            if s < len(later):
+                ilv_scalar(later[s], t, S_SHARE_A)
+            if t == 1:
+                if s == 0:
+                    quant(xc[1], xs[1], xg[1])
+                else:
+                    quant_w(later[s - 1])
+                    b_quant(*steps[s - 1])
+                if s < len(later):
+                    ilv_vector(later[s], S_SHARE_A)
+            if i == len(a_units) - 2:
+                gate_part(0, 0)
+        gate_part(1, 0)
+
         for i, (e, g, t) in enumerate(units):
             s = i // PACK
             b_unit(e, g, t)
+            scalar_side(len(a_units) + i + LEAD)
             if i > 0:
                 b_add(*units[i - 1])
             if i == 0:
                 b_quant(*steps[-1])
-            if s < 2 and t % 2 == 1:
-                gate_part(1, 2 * s + t // 2)
+            if i < 3 * G:
+                gate_part(i % G, 1 + i // G)
             if 1 <= s <= len(last):
                 ilv_scalar(last[s - 1], t, P)
             if 2 <= s <= len(last) + 1 and t == 1:

@@ -20,7 +20,7 @@ P = 128
 PACK = 4
 GROUP = 512
 G = T // GROUP
-S_SHARE_A = 80
+S_SHARE_A = 48
 S_SHARE_HEAD = 40
 V_SHARE_TAIL = 352
 LEAD = 2
@@ -43,7 +43,7 @@ def tile_autonomyofexpertsnormgate_x1_kernel(tc, x, wdown, rgain, wup, wp, out_0
         for e in range(E):
             src["wd", e], src["wp", e], src["wu", e] = wdown[e], wp[e], wup[e]
         raw = {n: keep.tile([P, PACK, 512], BF16, name="raw_%s%d" % n, align_bytes=64) for n in src}
-        grp = {n: keep.tile([P, 512, PACK], BF16, name="grp_%s%d" % n, align_bytes=64) for n in src}
+        grp = {}
         wc = {n: keep.tile([P, 512], U32, name="wc_%s%d" % n, align_bytes=64) for n in src}
         ws = {n: keep.tile([P, 512], U8, name="ws_%s%d" % n, align_bytes=64) for n in src}
         xg = [keep.tile([P, GROUP, PACK], BF16, name="xg%d" % g, align_bytes=64) for g in range(G)]
@@ -86,6 +86,14 @@ def tile_autonomyofexpertsnormgate_x1_kernel(tc, x, wdown, rgain, wup, wp, out_0
             if n[0] == "wd":
                 return dst, raw[n][:].rearrange("p j (m q) -> p q m j", q=4)
             return dst, raw[n][:].rearrange("p j (q m) -> p q m j", q=4)
+
+        def stage(n, tag):
+            grp[n] = work.tile([P, 512, PACK], BF16, name="grp", tag=tag, align_bytes=64, bufs=1)
+
+        def ilv_gpsimd(n, share):
+            dst, rows = ilv_views(n)
+            nc.gpsimd.tensor_scalar(out=dst[:, :, share:P, :], in0=rows[:, :, share:P, :], scalar1=1.0, scalar2=0.0,
+                                    op0=ALU.mult, op1=ALU.add)
 
         def ilv_scalar(n, q, share):
             dst, rows = ilv_views(n)
@@ -213,6 +221,7 @@ def tile_autonomyofexpertsnormgate_x1_kernel(tc, x, wdown, rgain, wup, wp, out_0
             for q in range(4):
                 nc.sync.dma_start(out=out_2[g, 4 * q:4 * q + 4, :].bitcast(I32), in_=osc[g][32 * q:32 * q + 4, :].bitcast(I32))
 
+        stage(("wd", 0), "head")
         x_turn(0, 0)
         for q in range(4):
             ilv_scalar(("wd", 0), q, S_SHARE_HEAD)
@@ -245,16 +254,18 @@ def tile_autonomyofexpertsnormgate_x1_kernel(tc, x, wdown, rgain, wup, wp, out_0
             s = i // PACK
             a_unit(e, g, t)
             scalar_side(i + LEAD)
-            if s < len(later):
-                ilv_scalar(later[s], t, S_SHARE_A)
             if t == 1:
                 if s == 0:
                     quant(xc[1], xs[1], xg[1])
                 else:
-                    quant_w(later[s - 1])
                     b_quant(*steps[s - 1])
+                    quant_w(later[s - 1])
                 if s < len(later):
-                    ilv_vector(later[s], S_SHARE_A)
+                    stage(later[s], "shared")
+                    ilv_gpsimd(later[s], S_SHARE_A)
+            if t >= 2 and s < len(later):
+                ilv_scalar(later[s], 2 * t - 4, S_SHARE_A)
+                ilv_scalar(later[s], 2 * t - 3, S_SHARE_A)
             if i == len(a_units) - 2:
                 gate_part(0, 0)
         gate_part(1, 0)
@@ -270,6 +281,8 @@ def tile_autonomyofexpertsnormgate_x1_kernel(tc, x, wdown, rgain, wup, wp, out_0
             if i < 3 * G:
                 gate_part(i % G, 1 + i // G)
             if 1 <= s <= len(last):
+                if t == 0:
+                    stage(last[s - 1], "late%d" % (s % 2))
                 ilv_scalar(last[s - 1], t, P)
             if 2 <= s <= len(last) + 1 and t == 1:
                 quant_w(last[s - 2])

@@ -49,8 +49,8 @@ def tile_autonomyofexpertsnormgate_x1_kernel(tc, x, wdown, rgain, wup, wp, out_0
         xg = [keep.tile([P, GROUP, PACK], BF16, name="xg%d" % g, align_bytes=64) for g in range(G)]
         xc = [keep.tile([P, GROUP], U32, name="xc%d" % g, align_bytes=64) for g in range(G)]
         xs = [keep.tile([P, GROUP], U8, name="xs%d" % g, align_bytes=64) for g in range(G)]
-        sumsq = [keep.tile([P, PACK, E], F32, name="sumsq%d" % g) for g in range(G)]
-        gate = [keep.tile([P, PACK, E], F32, name="gate%d" % g) for g in range(G)]
+        sumsq = keep.tile([P, G * PACK, E], F32, name="sumsq")
+        gate = keep.tile([P, G * PACK, E], F32, name="gate")
         res = [keep.tile([P, PACK, F], F32, name="res%d" % g) for g in range(G)]
 
         def tokens(ap, g):
@@ -138,40 +138,19 @@ def tile_autonomyofexpertsnormgate_x1_kernel(tc, x, wdown, rgain, wup, wp, out_0
             nc.tensor.matmul_mx(out=toks[:], lhsT=xc[g][:, cols(t)].bitcast(FP8X4), lhsT_scale=xs[g][:, cols(t)],
                                 rhs=wc[n][:].bitcast(FP8X4), rhs_scale=ws[n][:], start=True, stop=True)
             sq = work.tile([P, 512], BF16, name="sq", bufs=2)
-            nc.scalar.activation(out=sq[:], in_=toks[:], func=ACT.Square, scale=0.5, accum_out=sumsq[g][:, t, e:e + 1])
+            nc.scalar.activation(out=sq[:], in_=toks[:], func=ACT.Square, scale=0.5, accum_out=sumsq[:, PACK * g + t, e:e + 1])
 
         def b_quant(e, g):
             bc[e, g] = keep.tile([P, GROUP], U32, name="bc%d%d" % (e, g), align_bytes=64)
             bs[e, g] = keep.tile([P, GROUP], U8, name="bs%d%d" % (e, g), align_bytes=64)
             quant(bc[e, g], bs[e, g], bgrp[e, g])
 
-        def small(name, width):
-            return [keep.tile([P, PACK, width], F32, name="%s%d" % (name, g)) for g in range(G)]
-
-        score, diff, th, rest, quot, ex = (small(name, E) for name in ("score", "diff", "th", "rest", "quot", "ex"))
-        s2, top, den, inv = small("s2", 2), small("top", 1), small("den", 1), small("inv", 1)
+        score, diff, th, rest, quot = (keep.tile([P, G * PACK, E], F32, name=name)
+                                       for name in ("score", "diff", "th", "rest", "quot"))
+        top, total, den, inv = (keep.tile([P, G * PACK, 1], F32, name=name) for name in ("top", "total", "den", "inv"))
 
         def over_experts(tile):
-            return tile[:].to_broadcast([P, PACK, E])
-
-        def half_score(g):
-            nc.scalar.activation(out=score[g][:], in_=sumsq[g][:], func=ACT.Sqrt)
-
-        def gate_part(g, k):
-            if k == 0:
-                nc.vector.tensor_reduce(out=top[g][:, :, 0], in_=score[g][:], axis=AX.X, op=ALU.max)
-                nc.gpsimd.tensor_tensor(out=diff[g][:], in0=score[g][:], in1=over_experts(top[g]), op=ALU.subtract)
-            elif k == 1:
-                nc.scalar.activation(out=th[g][:], in_=diff[g][:], func=ACT.Tanh)
-                nc.gpsimd.tensor_scalar(out=rest[g][:], in0=th[g][:], scalar1=-1.0, scalar2=1.0, op0=ALU.mult, op1=ALU.add)
-            elif k == 2:
-                nc.vector.reciprocal(out=quot[g][:], in_=rest[g][:])
-                nc.gpsimd.tensor_scalar(out=ex[g][:], in0=quot[g][:], scalar1=2.0, scalar2=-1.0, op0=ALU.mult, op1=ALU.add)
-                nc.gpsimd.tensor_tensor(out=s2[g][:], in0=ex[g][:, :, 0:2], in1=ex[g][:, :, 2:4], op=ALU.add)
-                nc.gpsimd.tensor_tensor(out=den[g][:], in0=s2[g][:, :, 0:1], in1=s2[g][:, :, 1:2], op=ALU.add)
-            else:
-                nc.vector.reciprocal(out=inv[g][:], in_=den[g][:])
-                nc.gpsimd.tensor_tensor(out=gate[g][:], in0=ex[g][:], in1=over_experts(inv[g]), op=ALU.mult)
+            return tile[:].to_broadcast([P, G * PACK, E])
 
         term = {}
 
@@ -188,25 +167,17 @@ def tile_autonomyofexpertsnormgate_x1_kernel(tc, x, wdown, rgain, wup, wp, out_0
             lin = psum.tile([P, 512], F32, name="pp", tag="pv")
             nc.tensor.matmul_mx(out=lin[:], lhsT=xc[g][:, cols(t)].bitcast(FP8X4), lhsT_scale=xs[g][:, cols(t)],
                                 rhs=wc["wp", e][:].bitcast(FP8X4), rhs_scale=ws["wp", e][:], start=True, stop=True)
-            act = acts[e, g, t]
-            term[e, g, t] = res[g][:, t, :] if e == 0 else work.tile([P, F], F32, name="term", bufs=3)[:]
-            if e == 0:
-                nc.vector.tensor_tensor(out=term[e, g, t], in0=lin[:], in1=act[:], op=ALU.mult)
-            else:
-                nc.vector.scalar_tensor_tensor(out=term[e, g, t], in0=lin[:], scalar=gate[g][:, t, e:e + 1], in1=act[:],
-                                               op0=ALU.mult, op1=ALU.mult)
+            if e > 0 and t % 2 == 0:
+                term[e, g, t // 2] = work.tile([P, 2, F], F32, name="term", bufs=4)
+            dst = res[g][:, t, :] if e == 0 else term[e, g, t // 2][:, t % 2, :]
+            nc.vector.scalar_tensor_tensor(out=dst, in0=lin[:], scalar=gate[:, PACK * g + t, e:e + 1], in1=acts[e, g, t][:],
+                                           op0=ALU.mult, op1=ALU.mult)
 
-        def b_add(e, g, t):
-            if e == 0:
-                return
-            dst = res[g][:, t, :]
-            if e == 1:
-                nc.vector.scalar_tensor_tensor(out=dst, in0=dst, scalar=gate[g][:, t, 0:1], in1=term[e, g, t],
-                                               op0=ALU.mult, op1=ALU.add)
-            else:
-                nc.vector.tensor_tensor(out=dst, in0=dst, in1=term[e, g, t], op=ALU.add)
+        def b_add(engine, e, g, h):
+            dst = res[g][:, 2 * h:2 * h + 2, :]
+            engine.tensor_tensor(out=dst, in0=dst, in1=term[e, g, h][:], op=ALU.add)
             if e == E - 1:
-                nc.sync.dma_start(out=tokens(out_0, g)[:, t, :], in_=dst)
+                nc.sync.dma_start(out=tokens(out_0, g)[:, 2 * h:2 * h + 2, :], in_=dst)
 
         og = [keep.tile([P, F, PACK], BF16, name="og%d" % g, align_bytes=64) for g in range(G)]
         oc = [keep.tile([P, F], U32, name="oc%d" % g, align_bytes=64) for g in range(G)]
@@ -235,18 +206,26 @@ def tile_autonomyofexpertsnormgate_x1_kernel(tc, x, wdown, rgain, wup, wp, out_0
         steps = [(0, 0), (0, 1), (1, 0), (1, 1), (2, 0), (3, 0), (2, 1), (3, 1)]
         later = [("wd", 1), ("wd", 2), ("wd", 3), ("wp", 0), ("wu", 0), ("wp", 1), ("wu", 1)]
         a_units = [(e, g, t) for e, g in steps for t in range(PACK)]
-        pairs = [(e, g) for e in range(E) for g in range(G)]
-        last = [("wp", 2), ("wu", 2), ("wp", 3), ("wu", 3)]
-        units = [(e, g, t) for e, g in pairs for t in range(PACK)]
+        cycles = [(0, 0), (0, 1), (1, 0), (1, 1), (2, 0), (3, 0), (2, 1), (3, 1)]
+        last = [("wp", 2), ("wp", 3), ("wu", 3)]
+        units = [(e, g, t) for e, g in cycles for t in range(PACK)]
 
         def scalar_side(j):
             if j < len(a_units):
-                e, g, t = a_units[j]
-                sq_unit(e, g, t)
-                if (e, t) == (E - 1, PACK - 1):
-                    half_score(g)
+                sq_unit(*a_units[j])
+                if j == len(a_units) - 1:
+                    nc.scalar.activation(out=score[:], in_=sumsq[:], func=ACT.Sqrt)
             elif j < len(a_units) + len(units):
                 u_unit(*units[j - len(a_units)])
+
+        def share_out(n):
+            stage(n, "shared")
+            ilv_gpsimd(n, S_SHARE_A)
+
+        def scalar_share(n, t):
+            if t >= 2:
+                ilv_scalar(n, 2 * t - 4, S_SHARE_A)
+                ilv_scalar(n, 2 * t - 3, S_SHARE_A)
 
         for j in range(LEAD):
             scalar_side(j)
@@ -259,37 +238,51 @@ def tile_autonomyofexpertsnormgate_x1_kernel(tc, x, wdown, rgain, wup, wp, out_0
                     quant(xc[1], xs[1], xg[1])
                 else:
                     b_quant(*steps[s - 1])
+                if 0 < s < len(later):
                     quant_w(later[s - 1])
                 if s < len(later):
-                    stage(later[s], "shared")
-                    ilv_gpsimd(later[s], S_SHARE_A)
-            if t >= 2 and s < len(later):
-                ilv_scalar(later[s], 2 * t - 4, S_SHARE_A)
-                ilv_scalar(later[s], 2 * t - 3, S_SHARE_A)
-            if i == len(a_units) - 2:
-                gate_part(0, 0)
-        gate_part(1, 0)
+                    share_out(later[s])
+            if s < len(later):
+                scalar_share(later[s], t)
+
+        alone = ("wu", 2)
+        stage(alone, "head")
+        dst, rows = ilv_views(alone)
+        nc.vector.tensor_reduce(out=top[:, :, 0], in_=score[:], axis=AX.X, op=ALU.max)
+        nc.vector.tensor_copy(out=dst[:, 0:2], in_=rows[:, 0:2])
+        nc.vector.tensor_tensor(out=diff[:], in0=score[:], in1=over_experts(top), op=ALU.subtract)
+        nc.scalar.activation(out=th[:], in_=diff[:], func=ACT.Tanh)
+        nc.scalar.activation(out=rest[:], in_=th[:], func=ACT.Identity, scale=-1.0, bias=1.0)
+        nc.vector.tensor_copy(out=dst[:, 2:4], in_=rows[:, 2:4])
+        nc.vector.reciprocal(out=quot[:], in_=rest[:])
+        b_quant(*steps[-1])
+        nc.vector.tensor_reduce(out=total[:, :, 0], in_=quot[:], axis=AX.X, op=ALU.add)
+        quant_w(alone)
+        nc.vector.tensor_scalar(out=den[:], in0=total[:], scalar1=-0.5 * E, scalar2=None, op0=ALU.add)
+        nc.vector.reciprocal(out=inv[:], in_=den[:])
+        nc.vector.scalar_tensor_tensor(out=gate[:], in0=quot[:], scalar=-0.5, in1=over_experts(inv), op0=ALU.add, op1=ALU.mult)
+        quant_w(later[-1])
 
         for i, (e, g, t) in enumerate(units):
-            s = i // PACK
+            c = i // PACK
+            if t == 0 and c < len(last):
+                if c > 0:
+                    quant_w(last[c - 1])
+                share_out(last[c])
+            if c == len(last) and t == PACK - 1:
+                quant_w(last[-1])
+                b_add(nc.vector, e, g, 0)
             b_unit(e, g, t)
             scalar_side(len(a_units) + i + LEAD)
-            if i > 0:
-                b_add(*units[i - 1])
-            if i == 0:
-                b_quant(*steps[-1])
-            if i < 3 * G:
-                gate_part(i % G, 1 + i // G)
-            if 1 <= s <= len(last):
-                if t == 0:
-                    stage(last[s - 1], "late%d" % (s % 2))
-                ilv_scalar(last[s - 1], t, P)
-            if 2 <= s <= len(last) + 1 and t == 1:
-                quant_w(last[s - 2])
-            if s == len(pairs) - 1:
+            if c < len(last):
+                scalar_share(last[c], t)
+            if e > 0 and t == PACK - 1:
+                if c != len(last):
+                    b_add(nc.vector, e, g, 0)
+                b_add(nc.gpsimd if c < len(cycles) - 1 else nc.vector, e, g, 1)
+            if c == len(cycles) - 1:
                 dst, rows = o_views(0, P * t, P * (t + 1))
                 nc.scalar.copy(out=dst, in_=rows)
-        b_add(*units[-1])
         o_quant(0)
         dst, rows = o_views(1, V_SHARE_TAIL, F)
         nc.scalar.copy(out=dst, in_=rows)

@@ -20,10 +20,11 @@ P = 128
 PACK = 4
 GROUP = 512
 G = T // GROUP
-S_SHARE_A = 48
+S_SHARE_A = 36
+S_SHARE_B = 28
 S_SHARE_HEAD = 40
-V_SHARE_TAIL = 352
-LEAD = 2
+LEAD = 4
+LEAD_B = 2
 
 
 def tile_autonomyofexpertsnormgate_x1_kernel(tc, x, wdown, rgain, wup, wp, out_0, out_1, out_2):
@@ -34,7 +35,8 @@ def tile_autonomyofexpertsnormgate_x1_kernel(tc, x, wdown, rgain, wup, wp, out_0
         work = ctx.enter_context(tc.tile_pool(name="work", bufs=3))
         psum = ctx.enter_context(tc.psum_pool(name="psum", bufs=4))
         ctx.enter_context(tc.manual_schedule())
-        gain = keep.tile([P, E, 16], BF16, name="gain")
+        gain_rows = keep.tile([P, R], BF16, name="gain_rows")
+        gain = keep.tile([P, E, PACK], BF16, name="gain")
         ident = keep.tile([P, P], F32, name="ident")
         warm = keep.tile([P, 1], F32, name="warm")
         x_raw = {(g, h): keep.tile([P, 2 * D], BF16, name="x_raw%d%d" % (g, h), align_bytes=64)
@@ -46,7 +48,7 @@ def tile_autonomyofexpertsnormgate_x1_kernel(tc, x, wdown, rgain, wup, wp, out_0
         grp = {}
         wc = {n: keep.tile([P, 512], U32, name="wc_%s%d" % n, align_bytes=64) for n in src}
         ws = {n: keep.tile([P, 512], U8, name="ws_%s%d" % n, align_bytes=64) for n in src}
-        xg = [keep.tile([P, GROUP, PACK], BF16, name="xg%d" % g, align_bytes=64) for g in range(G)]
+        xg = [work.tile([P, GROUP, PACK], BF16, name="xg", tag=tag, align_bytes=64, bufs=1) for tag in ("x0", "shared")]
         xc = [keep.tile([P, GROUP], U32, name="xc%d" % g, align_bytes=64) for g in range(G)]
         xs = [keep.tile([P, GROUP], U8, name="xs%d" % g, align_bytes=64) for g in range(G)]
         sumsq = keep.tile([P, G * PACK, E], F32, name="sumsq")
@@ -62,8 +64,9 @@ def tile_autonomyofexpertsnormgate_x1_kernel(tc, x, wdown, rgain, wup, wp, out_0
         def load_w(n):
             nc.sync.dma_start(out=raw[n][:], in_=src[n].rearrange("(p j) c -> p j c", j=PACK))
 
-        nc.scalar.dma_start(out=gain[:, :, 0:PACK], in_=rgain.rearrange("e (p t) -> p e t", t=PACK))
+        nc.vector.memset(gain_rows[:].bitcast(I32), 0)
         load_x(0, 0)
+        nc.sync.dma_start(out=gain_rows[0:E, :], in_=rgain)
         load_w(("wd", 0))
         load_x(0, 1)
         load_x(1, 0)
@@ -95,9 +98,9 @@ def tile_autonomyofexpertsnormgate_x1_kernel(tc, x, wdown, rgain, wup, wp, out_0
             nc.gpsimd.tensor_scalar(out=dst[:, :, share:P, :], in0=rows[:, :, share:P, :], scalar1=1.0, scalar2=0.0,
                                     op0=ALU.mult, op1=ALU.add)
 
-        def ilv_scalar(n, q, share):
+        def ilv_scalar(n, h, share):
             dst, rows = ilv_views(n)
-            nc.scalar.copy(out=dst[:, q, 0:share, :], in_=rows[:, q, 0:share, :])
+            nc.scalar.copy(out=dst[:, 2 * h:2 * h + 2, 0:share, :], in_=rows[:, 2 * h:2 * h + 2, 0:share, :])
 
         def ilv_vector(n, share):
             dst, rows = ilv_views(n)
@@ -105,6 +108,10 @@ def tile_autonomyofexpertsnormgate_x1_kernel(tc, x, wdown, rgain, wup, wp, out_0
 
         def quant(codes, scales, grouped):
             nc.vector.quantize_mx(out=codes[:].bitcast(FP8X4), scales=scales[:], in_=grouped[:].rearrange("p c j -> p (c j)"))
+
+        def quant_cols(codes, scales, grouped, lo, hi):
+            nc.vector.quantize_mx(out=codes[:, lo:hi].bitcast(FP8X4), scales=scales[:, lo:hi],
+                                  in_=grouped[:, lo:hi, :].rearrange("p c j -> p (c j)"))
 
         def quant_w(n):
             quant(wc[n], ws[n], grp[n])
@@ -119,6 +126,14 @@ def tile_autonomyofexpertsnormgate_x1_kernel(tc, x, wdown, rgain, wup, wp, out_0
                     nc.tensor.transpose(view[:, s, u, :], words[:, 256 * s + u:256 * (s + 1):2], ident[:])
             nc.scalar.copy(out=dstw[:, 2 * h:2 * h + 2], in_=view.rearrange("p s u r -> p s r u"))
 
+        def gain_turn():
+            words = gain_rows[:].bitcast(F32)
+            bank = psum.tile([P, 2, P], F32, name="pg", tag="ps")
+            for u in range(2):
+                nc.tensor.transpose(bank[:, u, :], words[:, u::2], ident[:])
+            nc.scalar.copy(out=gain[:].rearrange("p e j -> p (e j)").bitcast(F32).rearrange("p (e u) -> p e u", u=2),
+                           in_=bank[:, :, 0:E].rearrange("p u e -> p e u"))
+
         bgrp, bc, bs = {}, {}, {}
 
         def a_unit(e, g, t):
@@ -130,7 +145,7 @@ def tile_autonomyofexpertsnormgate_x1_kernel(tc, x, wdown, rgain, wup, wp, out_0
             if t == 0:
                 bgrp[e, g] = work.tile([P, GROUP, PACK], BF16, name="bgrp", align_bytes=64, bufs=2)
             nc.vector.tensor_tensor(out=bgrp[e, g][:, cols(t), :], in0=ranks[:].rearrange("p (k n) -> p n k", k=PACK),
-                                    in1=gain[:, e, 0:PACK].unsqueeze(1).to_broadcast([P, P, PACK]), op=ALU.mult)
+                                    in1=gain[:, e, :].unsqueeze(1).to_broadcast([P, P, PACK]), op=ALU.mult)
 
         def sq_unit(e, g, t):
             n = ("wd", e)
@@ -140,9 +155,12 @@ def tile_autonomyofexpertsnormgate_x1_kernel(tc, x, wdown, rgain, wup, wp, out_0
             sq = work.tile([P, 512], BF16, name="sq", bufs=2)
             nc.scalar.activation(out=sq[:], in_=toks[:], func=ACT.Square, scale=0.5, accum_out=sumsq[:, PACK * g + t, e:e + 1])
 
-        def b_quant(e, g):
+        def b_codes(e, g):
             bc[e, g] = keep.tile([P, GROUP], U32, name="bc%d%d" % (e, g), align_bytes=64)
             bs[e, g] = keep.tile([P, GROUP], U8, name="bs%d%d" % (e, g), align_bytes=64)
+
+        def b_quant(e, g):
+            b_codes(e, g)
             quant(bc[e, g], bs[e, g], bgrp[e, g])
 
         score, diff, th, rest, quot = (keep.tile([P, G * PACK, E], F32, name=name)
@@ -153,6 +171,7 @@ def tile_autonomyofexpertsnormgate_x1_kernel(tc, x, wdown, rgain, wup, wp, out_0
             return tile[:].to_broadcast([P, G * PACK, E])
 
         term = {}
+        last_term = keep.tile([P, PACK, F], F32, name="last_term")
 
         acts = {}
 
@@ -167,9 +186,14 @@ def tile_autonomyofexpertsnormgate_x1_kernel(tc, x, wdown, rgain, wup, wp, out_0
             lin = psum.tile([P, 512], F32, name="pp", tag="pv")
             nc.tensor.matmul_mx(out=lin[:], lhsT=xc[g][:, cols(t)].bitcast(FP8X4), lhsT_scale=xs[g][:, cols(t)],
                                 rhs=wc["wp", e][:].bitcast(FP8X4), rhs_scale=ws["wp", e][:], start=True, stop=True)
-            if e > 0 and t % 2 == 0:
-                term[e, g, t // 2] = work.tile([P, 2, F], F32, name="term", bufs=4)
-            dst = res[g][:, t, :] if e == 0 else term[e, g, t // 2][:, t % 2, :]
+            if (e, g) == (E - 1, G - 1):
+                dst = last_term[:, t, :]
+            elif e == 0:
+                dst = res[g][:, t, :]
+            else:
+                if t % 2 == 0:
+                    term[e, g, t // 2] = work.tile([P, 2, F], F32, name="term", tag="term%d" % (t // 2), bufs=2)
+                dst = term[e, g, t // 2][:, t % 2, :]
             nc.vector.scalar_tensor_tensor(out=dst, in0=lin[:], scalar=gate[:, PACK * g + t, e:e + 1], in1=acts[e, g, t][:],
                                            op0=ALU.mult, op1=ALU.mult)
 
@@ -181,33 +205,37 @@ def tile_autonomyofexpertsnormgate_x1_kernel(tc, x, wdown, rgain, wup, wp, out_0
 
         og = [keep.tile([P, F, PACK], BF16, name="og%d" % g, align_bytes=64) for g in range(G)]
         oc = [keep.tile([P, F], U32, name="oc%d" % g, align_bytes=64) for g in range(G)]
-        osc = [keep.tile([P, F], U8, name="osc%d" % g, align_bytes=64) for g in range(G)]
+        osc = keep.tile([P, F], U8, name="osc", align_bytes=64)
 
         def o_views(g, lo, hi):
             return og[g][:, lo:hi, :], res[g][:].rearrange("p t f -> p f t")[:, lo:hi, :]
 
-        def o_quant(g):
-            quant(oc[g], osc[g], og[g])
-            nc.sync.dma_start(out=out_1[g].rearrange("p m b -> p (m b)").bitcast(I32), in_=oc[g][:].bitcast(I32))
+        def o_quant(g, lo, hi):
+            nc.vector.quantize_mx(out=oc[g][:, lo:hi].bitcast(FP8X4), scales=osc[4 * g:P, lo:hi],
+                                  in_=og[g][:, lo:hi, :].rearrange("p c j -> p (c j)"))
+            nc.sync.dma_start(out=out_1[g].rearrange("p m b -> p (m b)").bitcast(I32)[:, lo:hi], in_=oc[g][:, lo:hi].bitcast(I32))
+
+        def o_scales():
             for q in range(4):
-                nc.sync.dma_start(out=out_2[g, 4 * q:4 * q + 4, :].bitcast(I32), in_=osc[g][32 * q:32 * q + 4, :].bitcast(I32))
+                nc.sync.dma_start(out=out_2[:, 4 * q:4 * q + 4, :].bitcast(I32), in_=osc[32 * q:32 * q + 4 * G, :].bitcast(I32))
 
         stage(("wd", 0), "head")
         x_turn(0, 0)
-        for q in range(4):
-            ilv_scalar(("wd", 0), q, S_SHARE_HEAD)
+        gain_turn()
+        for h in range(2):
+            ilv_scalar(("wd", 0), h, S_SHARE_HEAD)
         ilv_vector(("wd", 0), S_SHARE_HEAD)
+        quant_cols(xc[0], xs[0], xg[0], 0, 2 * P)
         x_turn(0, 1)
         quant_w(("wd", 0))
-        quant(xc[0], xs[0], xg[0])
+        quant_cols(xc[0], xs[0], xg[0], 2 * P, 4 * P)
         x_turn(1, 0)
-        x_turn(1, 1)
 
         steps = [(0, 0), (0, 1), (1, 0), (1, 1), (2, 0), (3, 0), (2, 1), (3, 1)]
         later = [("wd", 1), ("wd", 2), ("wd", 3), ("wp", 0), ("wu", 0), ("wp", 1), ("wu", 1)]
         a_units = [(e, g, t) for e, g in steps for t in range(PACK)]
         cycles = [(0, 0), (0, 1), (1, 0), (1, 1), (2, 0), (3, 0), (2, 1), (3, 1)]
-        last = [("wp", 2), ("wp", 3), ("wu", 3)]
+        last = [("wp", 2), ("wu", 2), ("wu", 3)]
         units = [(e, g, t) for e, g in cycles for t in range(PACK)]
 
         def scalar_side(j):
@@ -218,74 +246,101 @@ def tile_autonomyofexpertsnormgate_x1_kernel(tc, x, wdown, rgain, wup, wp, out_0
             elif j < len(a_units) + len(units):
                 u_unit(*units[j - len(a_units)])
 
-        def share_out(n):
+        def share_out(n, share):
             stage(n, "shared")
-            ilv_gpsimd(n, S_SHARE_A)
+            ilv_gpsimd(n, share)
 
-        def scalar_share(n, t):
+        def scalar_share(n, t, share):
             if t >= 2:
-                ilv_scalar(n, 2 * t - 4, S_SHARE_A)
-                ilv_scalar(n, 2 * t - 3, S_SHARE_A)
+                ilv_scalar(n, t - 2, share)
 
-        for j in range(LEAD):
-            scalar_side(j)
-        for i, (e, g, t) in enumerate(a_units):
-            s = i // PACK
-            a_unit(e, g, t)
-            scalar_side(i + LEAD)
+        for t in range(PACK):
+            a_unit(*a_units[t])
             if t == 1:
-                if s == 0:
-                    quant(xc[1], xs[1], xg[1])
-                else:
-                    b_quant(*steps[s - 1])
-                if 0 < s < len(later):
-                    quant_w(later[s - 1])
-                if s < len(later):
-                    share_out(later[s])
-            if s < len(later):
-                scalar_share(later[s], t)
+                x_turn(1, 1)
+            if t == 2:
+                quant(xc[1], xs[1], xg[1])
+                share_out(later[0], S_SHARE_A)
+        for t in range(PACK):
+            scalar_side(t)
+            scalar_share(later[0], t, S_SHARE_A)
+        issued = PACK
+        for i in range(PACK, len(a_units)):
+            s, t = divmod(i, PACK)
+            a_unit(*a_units[i])
+            upto = min(i + max(0, s - len(steps) + 1 + LEAD), len(a_units))
+            for j in range(issued, upto + 1):
+                scalar_side(j)
+            issued = upto + 1
+            if t == 1 and s < len(later):
+                b_quant(*steps[s - 1])
+                quant_w(later[s - 1])
+                share_out(later[s], S_SHARE_A)
+            if s < len(later) - 1:
+                scalar_share(later[s], t, S_SHARE_A)
+            if t == 1 and s == len(later):
+                nc.vector.tensor_reduce(out=top[:, :, 0], in_=score[:], axis=AX.X, op=ALU.max)
+                b_quant(*steps[s - 1])
+                nc.vector.tensor_tensor(out=diff[:], in0=score[:], in1=over_experts(top), op=ALU.subtract)
+                nc.scalar.activation(out=th[:], in_=diff[:], func=ACT.Tanh)
+                nc.scalar.activation(out=rest[:], in_=th[:], func=ACT.Identity, scale=-1.0, bias=1.0)
+                for h in range(2):
+                    ilv_scalar(later[-1], h, S_SHARE_A)
+        for j in range(issued, len(a_units) + LEAD_B):
+            scalar_side(j)
 
-        alone = ("wu", 2)
-        stage(alone, "head")
-        dst, rows = ilv_views(alone)
-        nc.vector.tensor_reduce(out=top[:, :, 0], in_=score[:], axis=AX.X, op=ALU.max)
-        nc.vector.tensor_copy(out=dst[:, 0:2], in_=rows[:, 0:2])
-        nc.vector.tensor_tensor(out=diff[:], in0=score[:], in1=over_experts(top), op=ALU.subtract)
-        nc.scalar.activation(out=th[:], in_=diff[:], func=ACT.Tanh)
-        nc.scalar.activation(out=rest[:], in_=th[:], func=ACT.Identity, scale=-1.0, bias=1.0)
-        nc.vector.tensor_copy(out=dst[:, 2:4], in_=rows[:, 2:4])
+        b_codes(*steps[-1])
+        last_b = (bc[steps[-1]], bs[steps[-1]], bgrp[steps[-1]])
+        last_w = (wc[later[-1]], ws[later[-1]], grp[later[-1]])
         nc.vector.reciprocal(out=quot[:], in_=rest[:])
-        b_quant(*steps[-1])
+        quant_cols(*last_b, 0, 2 * P)
         nc.vector.tensor_reduce(out=total[:, :, 0], in_=quot[:], axis=AX.X, op=ALU.add)
-        quant_w(alone)
+        quant_cols(*last_b, 2 * P, 4 * P)
         nc.vector.tensor_scalar(out=den[:], in0=total[:], scalar1=-0.5 * E, scalar2=None, op0=ALU.add)
+        quant_cols(*last_w, 0, 2 * P)
         nc.vector.reciprocal(out=inv[:], in_=den[:])
         nc.vector.scalar_tensor_tensor(out=gate[:], in0=quot[:], scalar=-0.5, in1=over_experts(inv), op0=ALU.add, op1=ALU.mult)
-        quant_w(later[-1])
+        quant_cols(*last_w, 2 * P, 4 * P)
 
+        alone = ("wp", 3)
         for i, (e, g, t) in enumerate(units):
             c = i // PACK
             if t == 0 and c < len(last):
                 if c > 0:
                     quant_w(last[c - 1])
-                share_out(last[c])
-            if c == len(last) and t == PACK - 1:
+                share_out(last[c], S_SHARE_B)
+            if t == 0 and c == len(last):
+                stage(alone, "head")
+            if c == len(last) + 1 and t == PACK - 1:
                 quant_w(last[-1])
+                quant_w(alone)
                 b_add(nc.vector, e, g, 0)
+                scalar_side(len(a_units) + i - 1 + LEAD_B)
             b_unit(e, g, t)
-            scalar_side(len(a_units) + i + LEAD)
+            if (c, t) != (len(last) + 1, PACK - 2):
+                scalar_side(len(a_units) + i + LEAD_B)
             if c < len(last):
-                scalar_share(last[c], t)
-            if e > 0 and t == PACK - 1:
-                if c != len(last):
+                scalar_share(last[c], t, S_SHARE_B)
+            if c == len(last):
+                dst, rows = ilv_views(alone)
+                nc.scalar.copy(out=dst[:, t], in_=rows[:, t])
+            if e > 0 and t == PACK - 1 and c < len(cycles) - 1:
+                if c != len(last) + 1:
                     b_add(nc.vector, e, g, 0)
-                b_add(nc.gpsimd if c < len(cycles) - 1 else nc.vector, e, g, 1)
+                b_add(nc.gpsimd, e, g, 1)
             if c == len(cycles) - 1:
                 dst, rows = o_views(0, P * t, P * (t + 1))
                 nc.scalar.copy(out=dst, in_=rows)
-        o_quant(0)
-        dst, rows = o_views(1, V_SHARE_TAIL, F)
-        nc.scalar.copy(out=dst, in_=rows)
-        dst, rows = o_views(1, 0, V_SHARE_TAIL)
+        halves = (slice(0, F // 2), slice(F // 2, F))
+        for cs in halves:
+            nc.vector.tensor_tensor(out=res[1][:, :, cs], in0=res[1][:, :, cs], in1=last_term[:, :, cs], op=ALU.add)
+            nc.sync.dma_start(out=tokens(out_0, 1)[:, :, cs], in_=res[1][:, :, cs])
+            if cs.start == 0:
+                dst, rows = o_views(1, cs.start, cs.stop)
+                nc.scalar.copy(out=dst, in_=rows)
+        o_quant(0, 0, F)
+        dst, rows = o_views(1, F // 2, F)
         nc.vector.tensor_copy(out=dst, in_=rows)
-        o_quant(1)
+        for cs in halves:
+            o_quant(1, cs.start, cs.stop)
+        o_scales()

@@ -20,8 +20,8 @@ P = 128
 PACK = 4
 GROUP = 512
 G = T // GROUP
-S_SHARE_A = 36
-S_SHARE_B = 28
+S_SHARE_A = 40
+S_SHARE_B = 40
 S_SHARE_HEAD = 40
 LEAD = 4
 LEAD_B = 2
@@ -38,6 +38,7 @@ def tile_autonomyofexpertsnormgate_x1_kernel(tc, x, wdown, rgain, wup, wp, out_0
         gain_rows = keep.tile([P, R], BF16, name="gain_rows")
         gain = keep.tile([P, E, PACK], BF16, name="gain")
         ident = keep.tile([P, P], F32, name="ident")
+        ident_b = keep.tile([P, P], BF16, name="ident_b")
         warm = keep.tile([P, 1], F32, name="warm")
         x_raw = {(g, h): keep.tile([P, 2 * D], BF16, name="x_raw%d%d" % (g, h), align_bytes=64)
                  for g in range(G) for h in range(2)}
@@ -80,6 +81,7 @@ def tile_autonomyofexpertsnormgate_x1_kernel(tc, x, wdown, rgain, wup, wp, out_0
         nc.vector.memset(warm[:], 0.0)
         nc.scalar.activation(out=warm[:], in_=warm[:], func=ACT.Sqrt)
         make_identity(nc, ident[:])
+        nc.gpsimd.tensor_copy(out=ident_b[:], in_=ident[:])
 
         def cols(t):
             return slice(P * t, P * (t + 1))
@@ -97,6 +99,23 @@ def tile_autonomyofexpertsnormgate_x1_kernel(tc, x, wdown, rgain, wup, wp, out_0
             dst, rows = ilv_views(n)
             nc.gpsimd.tensor_scalar(out=dst[:, :, share:P, :], in0=rows[:, :, share:P, :], scalar1=1.0, scalar2=0.0,
                                     op0=ALU.mult, op1=ALU.add)
+
+        def ilv_tensor(n, h):
+            bank = psum.tile([P, 2, P, PACK], BF16, name="pw", tag="ps")
+            for q in range(2):
+                nc.tensor.matmul(out=bank[:, q].rearrange("p m j -> p j m"), lhsT=ident_b[:],
+                                 rhs=raw[n][:, :, cols(2 * h + q)], start=True, stop=True)
+            nc.scalar.copy(out=grp[n][:, 2 * P * h:2 * P * (h + 1), :].rearrange("p c j -> p (c j)"),
+                           in_=bank[:].rearrange("p q m j -> p (q m j)"))
+
+        def ilv_share(n, share):
+            bank = psum.tile([P, 4, share, PACK], BF16, name="pw", tag="ps")
+            dst, rows = ilv_views(n)
+            order = "p q m j -> p j m q" if n[0] == "wd" else "p q m j -> p j q m"
+            for u in range(2):
+                nc.tensor.matmul(out=bank[:, :, :, 2 * u:2 * u + 2].rearrange(order), lhsT=ident_b[:],
+                                 rhs=rows[:, :, 0:share, 2 * u:2 * u + 2].rearrange(order), start=True, stop=True)
+            nc.scalar.copy(out=dst[:, :, 0:share, :], in_=bank[:])
 
         def ilv_scalar(n, h, share):
             dst, rows = ilv_views(n)
@@ -251,8 +270,8 @@ def tile_autonomyofexpertsnormgate_x1_kernel(tc, x, wdown, rgain, wup, wp, out_0
             ilv_gpsimd(n, share)
 
         def scalar_share(n, t, share):
-            if t >= 2:
-                ilv_scalar(n, t - 2, share)
+            if t == 2:
+                ilv_share(n, share)
 
         for t in range(PACK):
             a_unit(*a_units[t])
@@ -284,8 +303,7 @@ def tile_autonomyofexpertsnormgate_x1_kernel(tc, x, wdown, rgain, wup, wp, out_0
                 nc.vector.tensor_tensor(out=diff[:], in0=score[:], in1=over_experts(top), op=ALU.subtract)
                 nc.scalar.activation(out=th[:], in_=diff[:], func=ACT.Tanh)
                 nc.scalar.activation(out=rest[:], in_=th[:], func=ACT.Identity, scale=-1.0, bias=1.0)
-                for h in range(2):
-                    ilv_scalar(later[-1], h, S_SHARE_A)
+                ilv_share(later[-1], S_SHARE_A)
         for j in range(issued, len(a_units) + LEAD_B):
             scalar_side(j)
 
@@ -321,9 +339,8 @@ def tile_autonomyofexpertsnormgate_x1_kernel(tc, x, wdown, rgain, wup, wp, out_0
                 scalar_side(len(a_units) + i + LEAD_B)
             if c < len(last):
                 scalar_share(last[c], t, S_SHARE_B)
-            if c == len(last):
-                dst, rows = ilv_views(alone)
-                nc.scalar.copy(out=dst[:, t], in_=rows[:, t])
+            if c == len(last) and t % 2 == 0:
+                ilv_tensor(alone, t // 2)
             if e > 0 and t == PACK - 1 and c < len(cycles) - 1:
                 if c != len(last) + 1:
                     b_add(nc.vector, e, g, 0)

@@ -20,8 +20,9 @@ P = 128
 PACK = 4
 GROUP = 512
 G = T // GROUP
-S_SHARE_A = 40
-S_SHARE_B = 40
+S_SHARE_A = 48
+S_SHARE_B = 48
+V_SUM = 1216
 S_SHARE_HEAD = 40
 LEAD = 4
 LEAD_B = 2
@@ -210,17 +211,18 @@ def tile_autonomyofexpertsnormgate_x1_kernel(tc, x, wdown, rgain, wup, wp, out_0
             elif e == 0:
                 dst = res[g][:, t, :]
             else:
-                if t % 2 == 0:
-                    term[e, g, t // 2] = work.tile([P, 2, F], F32, name="term", tag="term%d" % (t // 2), bufs=2)
-                dst = term[e, g, t // 2][:, t % 2, :]
+                if t == 0:
+                    term[e, g] = work.tile([P, PACK, F], F32, name="term", bufs=2)
+                dst = term[e, g][:, t, :]
             nc.vector.scalar_tensor_tensor(out=dst, in0=lin[:], scalar=gate[:, PACK * g + t, e:e + 1], in1=acts[e, g, t][:],
                                            op0=ALU.mult, op1=ALU.mult)
 
         def b_add(engine, e, g, h):
-            dst = res[g][:, 2 * h:2 * h + 2, :]
-            engine.tensor_tensor(out=dst, in0=dst, in1=term[e, g, h][:], op=ALU.add)
+            span = (slice(0, V_SUM), slice(V_SUM, PACK * F))[h]
+            dst = res[g][:].rearrange("p t f -> p (t f)")[:, span]
+            engine.tensor_tensor(out=dst, in0=dst, in1=term[e, g][:].rearrange("p t f -> p (t f)")[:, span], op=ALU.add)
             if e == E - 1:
-                nc.sync.dma_start(out=tokens(out_0, g)[:, 2 * h:2 * h + 2, :], in_=dst)
+                nc.sync.dma_start(out=tokens(out_0, g)[:, 2 * h:2 * h + 2, :], in_=res[g][:, 2 * h:2 * h + 2, :])
 
         og = [keep.tile([P, F, PACK], BF16, name="og%d" % g, align_bytes=64) for g in range(G)]
         oc = [keep.tile([P, F], U32, name="oc%d" % g, align_bytes=64) for g in range(G)]

@@ -20,12 +20,13 @@ P = 128
 PACK = 4
 GROUP = 512
 G = T // GROUP
+BANK = 2048
 S_SHARE_A = 48
 S_SHARE_B = 48
 V_SUM = 1216
 S_SHARE_HEAD = 40
 LEAD = 4
-LEAD_B = 2
+LEAD_B = 4
 
 
 def tile_autonomyofexpertsnormgate_x1_kernel(tc, x, wdown, rgain, wup, wp, out_0, out_1, out_2):
@@ -48,9 +49,13 @@ def tile_autonomyofexpertsnormgate_x1_kernel(tc, x, wdown, rgain, wup, wp, out_0
             src["wd", e], src["wp", e], src["wu", e] = wdown[e], wp[e], wup[e]
         raw = {n: keep.tile([P, PACK, 512], BF16, name="raw_%s%d" % n, align_bytes=64) for n in src}
         grp = {}
-        wc = {n: keep.tile([P, 512], U32, name="wc_%s%d" % n, align_bytes=64) for n in src}
-        ws = {n: keep.tile([P, 512], U8, name="ws_%s%d" % n, align_bytes=64) for n in src}
-        xg = [work.tile([P, GROUP, PACK], BF16, name="xg", tag=tag, align_bytes=64, bufs=1) for tag in ("x0", "shared")]
+        wc, ws = {}, {}
+        joint = keep.tile([P, 3 * 512 * PACK], BF16, name="joint", align_bytes=64)
+
+        def part(i):
+            return joint[:, 512 * PACK * i:512 * PACK * (i + 1)].rearrange("p (c j) -> p c j", j=PACK)
+
+        xg = [keep.tile([P, GROUP, PACK], BF16, name="xg0", align_bytes=64)[:], part(1)]
         xc = [keep.tile([P, GROUP], U32, name="xc%d" % g, align_bytes=64) for g in range(G)]
         xs = [keep.tile([P, GROUP], U8, name="xs%d" % g, align_bytes=64) for g in range(G)]
         sumsq = keep.tile([P, G * PACK, E], F32, name="sumsq")
@@ -84,6 +89,14 @@ def tile_autonomyofexpertsnormgate_x1_kernel(tc, x, wdown, rgain, wup, wp, out_0
         make_identity(nc, ident[:])
         nc.gpsimd.tensor_copy(out=ident_b[:], in_=ident[:])
 
+        late = []
+
+        def bank_of(reader):
+            at = BANK * (0 if reader == "v" else 4)
+            if late:
+                return {"tag": reader + "3", "bufs": 3, "offset": at}
+            return {"tag": reader + "4", "bufs": 4, "offset": at}
+
         def cols(t):
             return slice(P * t, P * (t + 1))
 
@@ -93,24 +106,18 @@ def tile_autonomyofexpertsnormgate_x1_kernel(tc, x, wdown, rgain, wup, wp, out_0
                 return dst, raw[n][:].rearrange("p j (m q) -> p q m j", q=4)
             return dst, raw[n][:].rearrange("p j (q m) -> p q m j", q=4)
 
+        solo = keep.tile([P, 512, PACK], BF16, name="solo", align_bytes=64)
+
         def stage(n, tag):
-            grp[n] = work.tile([P, 512, PACK], BF16, name="grp", tag=tag, align_bytes=64, bufs=1)
+            grp[n] = part(1) if tag == "shared" else solo[:]
 
         def ilv_gpsimd(n, share):
             dst, rows = ilv_views(n)
             nc.gpsimd.tensor_scalar(out=dst[:, :, share:P, :], in0=rows[:, :, share:P, :], scalar1=1.0, scalar2=0.0,
                                     op0=ALU.mult, op1=ALU.add)
 
-        def ilv_tensor(n, h):
-            bank = psum.tile([P, 2, P, PACK], BF16, name="pw", tag="ps")
-            for q in range(2):
-                nc.tensor.matmul(out=bank[:, q].rearrange("p m j -> p j m"), lhsT=ident_b[:],
-                                 rhs=raw[n][:, :, cols(2 * h + q)], start=True, stop=True)
-            nc.scalar.copy(out=grp[n][:, 2 * P * h:2 * P * (h + 1), :].rearrange("p c j -> p (c j)"),
-                           in_=bank[:].rearrange("p q m j -> p (q m j)"))
-
         def ilv_share(n, share):
-            bank = psum.tile([P, 4, share, PACK], BF16, name="pw", tag="ps")
+            bank = psum.tile([P, 4, share, PACK], BF16, name="pw", **bank_of("s"))
             dst, rows = ilv_views(n)
             order = "p q m j -> p j m q" if n[0] == "wd" else "p q m j -> p j q m"
             for u in range(2):
@@ -133,13 +140,18 @@ def tile_autonomyofexpertsnormgate_x1_kernel(tc, x, wdown, rgain, wup, wp, out_0
             nc.vector.quantize_mx(out=codes[:, lo:hi].bitcast(FP8X4), scales=scales[:, lo:hi],
                                   in_=grouped[:, lo:hi, :].rearrange("p c j -> p (c j)"))
 
+        def planes(name, width):
+            return (keep.tile([P, width], U32, name="codes_" + name, align_bytes=64)[:],
+                    keep.tile([P, width], U8, name="scales_" + name, align_bytes=64)[:])
+
         def quant_w(n):
+            wc[n], ws[n] = planes("%s%d" % n, 512)
             quant(wc[n], ws[n], grp[n])
 
         def x_turn(g, h):
             words = x_raw[g, h][:].bitcast(F32)
             dstw = xg[g][:].rearrange("p c j -> p (c j)").bitcast(F32).rearrange("p (s r u) -> p s r u", r=P, u=2)
-            bank = psum.tile([P, 512], F32, name="pt", tag="ps")
+            bank = psum.tile([P, 512], F32, name="pt", **bank_of("s"))
             view = bank[:].rearrange("p (s u r) -> p s u r", s=2, u=2)
             for s in range(2):
                 for u in range(2):
@@ -148,7 +160,7 @@ def tile_autonomyofexpertsnormgate_x1_kernel(tc, x, wdown, rgain, wup, wp, out_0
 
         def gain_turn():
             words = gain_rows[:].bitcast(F32)
-            bank = psum.tile([P, 2, P], F32, name="pg", tag="ps")
+            bank = psum.tile([P, 2, P], F32, name="pg", **bank_of("s"))
             for u in range(2):
                 nc.tensor.transpose(bank[:, u, :], words[:, u::2], ident[:])
             nc.scalar.copy(out=gain[:].rearrange("p e j -> p (e j)").bitcast(F32).rearrange("p (e u) -> p e u", u=2),
@@ -158,26 +170,33 @@ def tile_autonomyofexpertsnormgate_x1_kernel(tc, x, wdown, rgain, wup, wp, out_0
 
         def a_unit(e, g, t):
             n = ("wd", e)
-            ranks = psum.tile([P, 512], F32, name="pa", tag="pv")
+            ranks = psum.tile([P, 512], F32, name="pa", **bank_of("v"))
             for k in range(PACK):
                 nc.tensor.matmul_mx(out=ranks[:, cols(k)], lhsT=wc[n][:, cols(k)].bitcast(FP8X4), lhsT_scale=ws[n][:, cols(k)],
                                     rhs=xc[g][:, cols(t)].bitcast(FP8X4), rhs_scale=xs[g][:, cols(t)], start=True, stop=True)
             if t == 0:
-                bgrp[e, g] = work.tile([P, GROUP, PACK], BF16, name="bgrp", align_bytes=64, bufs=2)
+                bgrp[e, g] = part(2 * (len(bgrp) % 2))
             nc.vector.tensor_tensor(out=bgrp[e, g][:, cols(t), :], in0=ranks[:].rearrange("p (k n) -> p n k", k=PACK),
                                     in1=gain[:, e, :].unsqueeze(1).to_broadcast([P, P, PACK]), op=ALU.mult)
 
         def sq_unit(e, g, t):
             n = ("wd", e)
-            toks = psum.tile([P, 512], F32, name="pb", tag="ps")
+            toks = psum.tile([P, 512], F32, name="pb", **bank_of("s"))
             nc.tensor.matmul_mx(out=toks[:], lhsT=xc[g][:, cols(t)].bitcast(FP8X4), lhsT_scale=xs[g][:, cols(t)],
                                 rhs=wc[n][:].bitcast(FP8X4), rhs_scale=ws[n][:], start=True, stop=True)
             sq = work.tile([P, 512], BF16, name="sq", bufs=2)
             nc.scalar.activation(out=sq[:], in_=toks[:], func=ACT.Square, scale=0.5, accum_out=sumsq[:, PACK * g + t, e:e + 1])
 
         def b_codes(e, g):
-            bc[e, g] = keep.tile([P, GROUP], U32, name="bc%d%d" % (e, g), align_bytes=64)
-            bs[e, g] = keep.tile([P, GROUP], U8, name="bs%d%d" % (e, g), align_bytes=64)
+            bc[e, g], bs[e, g] = planes("b%d%d" % (e, g), GROUP)
+
+        def joint_quant(s, key, n):
+            codes, scales = planes("joint%d" % s, 1024)
+            first = s % 2
+            nc.vector.quantize_mx(out=codes.bitcast(FP8X4), scales=scales, in_=joint[:, 2048 * first:2048 * (first + 2)])
+            b_at, w_at = slice(512 * first, 512 * (first + 1)), slice(512 * (1 - first), 512 * (2 - first))
+            bc[key], bs[key] = codes[:, b_at], scales[:, b_at]
+            wc[n], ws[n] = codes[:, w_at], scales[:, w_at]
 
         def b_quant(e, g):
             b_codes(e, g)
@@ -194,31 +213,56 @@ def tile_autonomyofexpertsnormgate_x1_kernel(tc, x, wdown, rgain, wup, wp, out_0
         last_term = keep.tile([P, PACK, F], F32, name="last_term")
 
         acts = {}
+        kept = [keep.tile([P, 2, F], F32, name="kept%d" % e) for e in range(E)]
+        turned = keep.tile([P, 2, F], F32, name="turned")
+        sums = {}
+
+        def sum_turn(e):
+            for t in range(2):
+                if e == 0:
+                    sums[t] = psum.tile([P, F], F32, name="psum_sum", tag="sum%d" % t, bufs=1, offset=BANK * (3 + 4 * t))
+                for c in range(4):
+                    nc.tensor.matmul(out=sums[t][:, cols(c)], lhsT=kept[e][:, t, cols(c)], rhs=ident[:], is_transpose=True,
+                                     start=(e, c) == (0, 0), stop=(e, c) == (E - 1, 3))
+            if e == E - 1:
+                for t in range(2):
+                    nc.scalar.copy(out=turned[:, t, :], in_=sums[t][:])
+
+        def sum_back():
+            for t in range(2):
+                back = psum.tile([P, F], F32, name="psum_back", tag="sum%d" % t, bufs=1, offset=BANK * (3 + 4 * t))
+                for c in range(4):
+                    nc.tensor.transpose(back[:, cols(c)], turned[:, t, cols(c)], ident[:])
+                nc.scalar.copy(out=res[0][:, t, :], in_=back[:])
+            nc.sync.dma_start(out=tokens(out_0, 0)[:, 0:2, :], in_=res[0][:, 0:2, :])
 
         def u_unit(e, g, t):
-            up = psum.tile([P, 512], F32, name="pu", tag="ps")
+            up = psum.tile([P, 512], F32, name="pu", **bank_of("s"))
             nc.tensor.matmul_mx(out=up[:], lhsT=bc[e, g][:, cols(t)].bitcast(FP8X4), lhsT_scale=bs[e, g][:, cols(t)],
                                 rhs=wc["wu", e][:].bitcast(FP8X4), rhs_scale=ws["wu", e][:], start=True, stop=True)
-            acts[e, g, t] = work.tile([P, F], F32, name="act", bufs=4)
+            acts[e, g, t] = work.tile([P, F], F32, name="act", bufs=7)
             nc.scalar.activation(out=acts[e, g, t][:], in_=up[:], func=ACT.Silu)
 
         def b_unit(e, g, t):
-            lin = psum.tile([P, 512], F32, name="pp", tag="pv")
+            lin = psum.tile([P, 512], F32, name="pp", **bank_of("v"))
             nc.tensor.matmul_mx(out=lin[:], lhsT=xc[g][:, cols(t)].bitcast(FP8X4), lhsT_scale=xs[g][:, cols(t)],
                                 rhs=wc["wp", e][:].bitcast(FP8X4), rhs_scale=ws["wp", e][:], start=True, stop=True)
             if (e, g) == (E - 1, G - 1):
                 dst = last_term[:, t, :]
+            elif g == 0 and t < 2:
+                dst = kept[e][:, t, :]
             elif e == 0:
                 dst = res[g][:, t, :]
             else:
-                if t == 0:
+                if (e, g) not in term:
                     term[e, g] = work.tile([P, PACK, F], F32, name="term", bufs=2)
                 dst = term[e, g][:, t, :]
             nc.vector.scalar_tensor_tensor(out=dst, in0=lin[:], scalar=gate[:, PACK * g + t, e:e + 1], in1=acts[e, g, t][:],
                                            op0=ALU.mult, op1=ALU.mult)
 
         def b_add(engine, e, g, h):
-            span = (slice(0, V_SUM), slice(V_SUM, PACK * F))[h]
+            cut = V_SUM if g else 2 * F
+            span = (slice(0, cut), slice(cut, PACK * F))[h]
             dst = res[g][:].rearrange("p t f -> p (t f)")[:, span]
             engine.tensor_tensor(out=dst, in0=dst, in1=term[e, g][:].rearrange("p t f -> p (t f)")[:, span], op=ALU.add)
             if e == E - 1:
@@ -256,7 +300,7 @@ def tile_autonomyofexpertsnormgate_x1_kernel(tc, x, wdown, rgain, wup, wp, out_0
         later = [("wd", 1), ("wd", 2), ("wd", 3), ("wp", 0), ("wu", 0), ("wp", 1), ("wu", 1)]
         a_units = [(e, g, t) for e, g in steps for t in range(PACK)]
         cycles = [(0, 0), (0, 1), (1, 0), (1, 1), (2, 0), (3, 0), (2, 1), (3, 1)]
-        last = [("wp", 2), ("wu", 2), ("wu", 3)]
+        last = [("wu", 2), ("wu", 3), ("wp", 2)]
         units = [(e, g, t) for e, g in cycles for t in range(PACK)]
 
         def scalar_side(j):
@@ -294,8 +338,7 @@ def tile_autonomyofexpertsnormgate_x1_kernel(tc, x, wdown, rgain, wup, wp, out_0
                 scalar_side(j)
             issued = upto + 1
             if t == 1 and s < len(later):
-                b_quant(*steps[s - 1])
-                quant_w(later[s - 1])
+                joint_quant(s - 1, steps[s - 1], later[s - 1])
                 share_out(later[s], S_SHARE_A)
             if s < len(later) - 1:
                 scalar_share(later[s], t, S_SHARE_A)
@@ -311,6 +354,7 @@ def tile_autonomyofexpertsnormgate_x1_kernel(tc, x, wdown, rgain, wup, wp, out_0
 
         b_codes(*steps[-1])
         last_b = (bc[steps[-1]], bs[steps[-1]], bgrp[steps[-1]])
+        wc[later[-1]], ws[later[-1]] = planes("wu1", 512)
         last_w = (wc[later[-1]], ws[later[-1]], grp[later[-1]])
         nc.vector.reciprocal(out=quot[:], in_=rest[:])
         quant_cols(*last_b, 0, 2 * P)
@@ -331,22 +375,30 @@ def tile_autonomyofexpertsnormgate_x1_kernel(tc, x, wdown, rgain, wup, wp, out_0
                 share_out(last[c], S_SHARE_B)
             if t == 0 and c == len(last):
                 stage(alone, "head")
-            if c == len(last) + 1 and t == PACK - 1:
+            if c == len(last) and t == PACK - 1:
                 quant_w(last[-1])
-                quant_w(alone)
                 b_add(nc.vector, e, g, 0)
-                scalar_side(len(a_units) + i - 1 + LEAD_B)
+            if c == len(last) + 1 and t == PACK - 1:
+                quant_w(alone)
             b_unit(e, g, t)
-            if (c, t) != (len(last) + 1, PACK - 2):
-                scalar_side(len(a_units) + i + LEAD_B)
+            scalar_side(len(a_units) + i + LEAD_B)
             if c < len(last):
                 scalar_share(last[c], t, S_SHARE_B)
-            if c == len(last) and t % 2 == 0:
-                ilv_tensor(alone, t // 2)
+            if c == len(last):
+                dst, rows = ilv_views(alone)
+                nc.scalar.copy(out=dst[:, t], in_=rows[:, t])
             if e > 0 and t == PACK - 1 and c < len(cycles) - 1:
-                if c != len(last) + 1:
+                if g == 1 and c != len(last):
                     b_add(nc.vector, e, g, 0)
                 b_add(nc.gpsimd, e, g, 1)
+            if (c, t) == (len(last), 0):
+                late.append(True)
+            if c == len(last) and t % 2 == 1:
+                sum_turn(t // 2)
+            if g == 0 and e >= 2 and t == PACK - 1:
+                sum_turn(e)
+            if (e, g, t) == (2, 1, PACK - 1):
+                sum_back()
             if c == len(cycles) - 1:
                 dst, rows = o_views(0, P * t, P * (t + 1))
                 nc.scalar.copy(out=dst, in_=rows)
@@ -357,9 +409,9 @@ def tile_autonomyofexpertsnormgate_x1_kernel(tc, x, wdown, rgain, wup, wp, out_0
             if cs.start == 0:
                 dst, rows = o_views(1, cs.start, cs.stop)
                 nc.scalar.copy(out=dst, in_=rows)
-        o_quant(0, 0, F)
         dst, rows = o_views(1, F // 2, F)
         nc.vector.tensor_copy(out=dst, in_=rows)
-        for cs in halves:
+        o_quant(0, 0, F)
+        for cs in reversed(halves):
             o_quant(1, cs.start, cs.stop)
         o_scales()

@@ -24,8 +24,8 @@ BANK = 2048
 S_SHARE_A = 48
 S_SHARE_B = 48
 V_SUM = 1216
-S_SHARE_HEAD = 40
-LEAD = 4
+S_SHARE_HEAD = 32
+LEAD = 3
 LEAD_B = 4
 
 
@@ -185,7 +185,7 @@ def tile_autonomyofexpertsnormgate_x1_kernel(tc, x, wdown, rgain, wup, wp, out_0
             nc.tensor.matmul_mx(out=toks[:], lhsT=xc[g][:, cols(t)].bitcast(FP8X4), lhsT_scale=xs[g][:, cols(t)],
                                 rhs=wc[n][:].bitcast(FP8X4), rhs_scale=ws[n][:], start=True, stop=True)
             sq = work.tile([P, 512], BF16, name="sq", bufs=2)
-            nc.scalar.activation(out=sq[:], in_=toks[:], func=ACT.Square, scale=0.5, accum_out=sumsq[:, PACK * g + t, e:e + 1])
+            nc.scalar.activation(out=sq[:], in_=toks[:], func=ACT.Square, accum_out=sumsq[:, PACK * g + t, e:e + 1])
 
         def b_codes(e, g):
             bc[e, g], bs[e, g] = planes("b%d%d" % (e, g), GROUP)
@@ -202,9 +202,9 @@ def tile_autonomyofexpertsnormgate_x1_kernel(tc, x, wdown, rgain, wup, wp, out_0
             b_codes(e, g)
             quant(bc[e, g], bs[e, g], bgrp[e, g])
 
-        score, diff, th, rest, quot = (keep.tile([P, G * PACK, E], F32, name=name)
-                                       for name in ("score", "diff", "th", "rest", "quot"))
-        top, total, den, inv = (keep.tile([P, G * PACK, 1], F32, name=name) for name in ("top", "total", "den", "inv"))
+        score, z, sz, rest, quot, ex = (keep.tile([P, G * PACK, E], F32, name=name)
+                                        for name in ("score", "z", "sz", "rest", "quot", "ex"))
+        top, total, inv = (keep.tile([P, G * PACK, 1], F32, name=name) for name in ("top", "total", "inv"))
 
         def over_experts(tile):
             return tile[:].to_broadcast([P, G * PACK, E])
@@ -286,11 +286,11 @@ def tile_autonomyofexpertsnormgate_x1_kernel(tc, x, wdown, rgain, wup, wp, out_0
 
         stage(("wd", 0), "head")
         x_turn(0, 0)
-        gain_turn()
         for h in range(2):
             ilv_scalar(("wd", 0), h, S_SHARE_HEAD)
         ilv_vector(("wd", 0), S_SHARE_HEAD)
         quant_cols(xc[0], xs[0], xg[0], 0, 2 * P)
+        gain_turn()
         x_turn(0, 1)
         quant_w(("wd", 0))
         quant_cols(xc[0], xs[0], xg[0], 2 * P, 4 * P)
@@ -315,40 +315,40 @@ def tile_autonomyofexpertsnormgate_x1_kernel(tc, x, wdown, rgain, wup, wp, out_0
             stage(n, "shared")
             ilv_gpsimd(n, share)
 
-        def scalar_share(n, t, share):
-            if t == 2:
-                ilv_share(n, share)
-
         for t in range(PACK):
             a_unit(*a_units[t])
             if t == 1:
                 x_turn(1, 1)
+                scalar_side(0)
             if t == 2:
                 quant(xc[1], xs[1], xg[1])
                 share_out(later[0], S_SHARE_A)
-        for t in range(PACK):
-            scalar_side(t)
-            scalar_share(later[0], t, S_SHARE_A)
+                scalar_side(1)
+        scalar_side(2)
+        ilv_share(later[0], S_SHARE_A)
+        scalar_side(3)
         issued = PACK
         for i in range(PACK, len(a_units)):
             s, t = divmod(i, PACK)
             a_unit(*a_units[i])
-            upto = min(i + max(0, s - len(steps) + 1 + LEAD), len(a_units))
+            upto = min(i + max(0, s - len(steps) + 1 + LEAD), len(a_units) - 1)
             for j in range(issued, upto + 1):
                 scalar_side(j)
             issued = upto + 1
             if t == 1 and s < len(later):
                 joint_quant(s - 1, steps[s - 1], later[s - 1])
                 share_out(later[s], S_SHARE_A)
-            if s < len(later) - 1:
-                scalar_share(later[s], t, S_SHARE_A)
+            if t == PACK - 1 and s < len(later) - 1:
+                ilv_share(later[s], S_SHARE_A)
             if t == 1 and s == len(later):
                 nc.vector.tensor_reduce(out=top[:, :, 0], in_=score[:], axis=AX.X, op=ALU.max)
                 b_quant(*steps[s - 1])
-                nc.vector.tensor_tensor(out=diff[:], in0=score[:], in1=over_experts(top), op=ALU.subtract)
-                nc.scalar.activation(out=th[:], in_=diff[:], func=ACT.Tanh)
-                nc.scalar.activation(out=rest[:], in_=th[:], func=ACT.Identity, scale=-1.0, bias=1.0)
+                nc.vector.scalar_tensor_tensor(out=z[:], in0=score[:], scalar=-1.0, in1=over_experts(top),
+                                               op0=ALU.add, op1=ALU.subtract)
+                nc.scalar.activation(out=sz[:], in_=z[:], func=ACT.Silu)
                 ilv_share(later[-1], S_SHARE_A)
+            if i == len(a_units) - 2:
+                nc.vector.tensor_tensor(out=rest[:], in0=z[:], in1=sz[:], op=ALU.subtract)
         for j in range(issued, len(a_units) + LEAD_B):
             scalar_side(j)
 
@@ -358,12 +358,13 @@ def tile_autonomyofexpertsnormgate_x1_kernel(tc, x, wdown, rgain, wup, wp, out_0
         last_w = (wc[later[-1]], ws[later[-1]], grp[later[-1]])
         nc.vector.reciprocal(out=quot[:], in_=rest[:])
         quant_cols(*last_b, 0, 2 * P)
-        nc.vector.tensor_reduce(out=total[:, :, 0], in_=quot[:], axis=AX.X, op=ALU.add)
+        nc.vector.tensor_tensor(out=ex[:], in0=sz[:], in1=quot[:], op=ALU.mult)
         quant_cols(*last_b, 2 * P, 4 * P)
-        nc.vector.tensor_scalar(out=den[:], in0=total[:], scalar1=-0.5 * E, scalar2=None, op0=ALU.add)
-        quant_cols(*last_w, 0, 2 * P)
-        nc.vector.reciprocal(out=inv[:], in_=den[:])
-        nc.vector.scalar_tensor_tensor(out=gate[:], in0=quot[:], scalar=-0.5, in1=over_experts(inv), op0=ALU.add, op1=ALU.mult)
+        nc.vector.tensor_reduce(out=total[:, :, 0], in_=ex[:], axis=AX.X, op=ALU.add)
+        quant_cols(*last_w, 0, P)
+        nc.vector.reciprocal(out=inv[:], in_=total[:])
+        quant_cols(*last_w, P, 2 * P)
+        nc.vector.tensor_tensor(out=gate[:], in0=ex[:], in1=over_experts(inv), op=ALU.mult)
         quant_cols(*last_w, 2 * P, 4 * P)
 
         alone = ("wp", 3)
@@ -375,20 +376,19 @@ def tile_autonomyofexpertsnormgate_x1_kernel(tc, x, wdown, rgain, wup, wp, out_0
                 share_out(last[c], S_SHARE_B)
             if t == 0 and c == len(last):
                 stage(alone, "head")
-            if c == len(last) and t == PACK - 1:
-                quant_w(last[-1])
-                b_add(nc.vector, e, g, 0)
             if c == len(last) + 1 and t == PACK - 1:
                 quant_w(alone)
             b_unit(e, g, t)
             scalar_side(len(a_units) + i + LEAD_B)
-            if c < len(last):
-                scalar_share(last[c], t, S_SHARE_B)
+            if c < len(last) and t == 1:
+                ilv_share(last[c], S_SHARE_B)
+            if (c, t) == (len(last) - 1, PACK - 1):
+                quant_w(last[-1])
             if c == len(last):
                 dst, rows = ilv_views(alone)
                 nc.scalar.copy(out=dst[:, t], in_=rows[:, t])
             if e > 0 and t == PACK - 1 and c < len(cycles) - 1:
-                if g == 1 and c != len(last):
+                if g == 1:
                     b_add(nc.vector, e, g, 0)
                 b_add(nc.gpsimd, e, g, 1)
             if (c, t) == (len(last), 0):
@@ -409,9 +409,9 @@ def tile_autonomyofexpertsnormgate_x1_kernel(tc, x, wdown, rgain, wup, wp, out_0
             if cs.start == 0:
                 dst, rows = o_views(1, cs.start, cs.stop)
                 nc.scalar.copy(out=dst, in_=rows)
+        o_quant(0, 0, F)
         dst, rows = o_views(1, F // 2, F)
         nc.vector.tensor_copy(out=dst, in_=rows)
-        o_quant(0, 0, F)
-        for cs in reversed(halves):
+        for cs in halves:
             o_quant(1, cs.start, cs.stop)
         o_scales()

@@ -158,6 +158,11 @@ def tile_autonomyofexpertsnormgate_x1_kernel(tc, x, wdown, rgain, wup, wp, out_0
                     nc.tensor.transpose(view[:, s, u, :], words[:, 256 * s + u:256 * (s + 1):2], ident[:])
             nc.scalar.copy(out=dstw[:, 2 * h:2 * h + 2], in_=view.rearrange("p s u r -> p s r u"))
 
+        def warm_up():
+            bank = psum.tile([P, P], F32, name="pz", **bank_of("v"))
+            for i in range(3):
+                nc.tensor.matmul(out=bank[:], lhsT=ident[:], rhs=ident[:], start=True, stop=True)
+
         def gain_turn():
             words = gain_rows[:].bitcast(F32)
             bank = psum.tile([P, 2, P], F32, name="pg", **bank_of("s"))
@@ -285,12 +290,14 @@ def tile_autonomyofexpertsnormgate_x1_kernel(tc, x, wdown, rgain, wup, wp, out_0
                 nc.sync.dma_start(out=out_2[:, 4 * q:4 * q + 4, :].bitcast(I32), in_=osc[32 * q:32 * q + 4 * G, :].bitcast(I32))
 
         stage(("wd", 0), "head")
+        warm_up()
         x_turn(0, 0)
         for h in range(2):
             ilv_scalar(("wd", 0), h, S_SHARE_HEAD)
         ilv_vector(("wd", 0), S_SHARE_HEAD)
         quant_cols(xc[0], xs[0], xg[0], 0, 2 * P)
         gain_turn()
+        warm_up()
         x_turn(0, 1)
         quant_w(("wd", 0))
         quant_cols(xc[0], xs[0], xg[0], 2 * P, 4 * P)

@@ -21,12 +21,13 @@ PACK = 4
 GROUP = 512
 G = T // GROUP
 BANK = 2048
-S_SHARE_A = 48
-S_SHARE_B = 48
-V_SUM = 1216
-S_SHARE_HEAD = 32
-LEAD = 3
-LEAD_B = 4
+WEIGHT_BYTES = PACK * 512 * 2
+HEAD_SHARE = 32
+G_SHARE = 56
+G_SHARE_LATE = 80
+SILU_LEAD = 8
+G_SUM = 832
+GAIN_PITCH = 16
 
 
 def tile_autonomyofexpertsnormgate_x1_kernel(tc, x, wdown, rgain, wup, wp, out_0, out_1, out_2):
@@ -34,30 +35,30 @@ def tile_autonomyofexpertsnormgate_x1_kernel(tc, x, wdown, rgain, wup, wp, out_0
 
     with ExitStack() as ctx:
         keep = ctx.enter_context(tc.tile_pool(name="keep", bufs=1))
-        work = ctx.enter_context(tc.tile_pool(name="work", bufs=3))
+        loads = ctx.enter_context(tc.tile_pool(name="loads", bufs=1))
+        work = ctx.enter_context(tc.tile_pool(name="work", bufs=2))
         psum = ctx.enter_context(tc.psum_pool(name="psum", bufs=4))
         ctx.enter_context(tc.manual_schedule())
-        gain_rows = keep.tile([P, R], BF16, name="gain_rows")
-        gain = keep.tile([P, E, PACK], BF16, name="gain")
+        gain = keep.tile([P, E, GAIN_PITCH], BF16, name="gain")
         ident = keep.tile([P, P], F32, name="ident")
         ident_b = keep.tile([P, P], BF16, name="ident_b")
         warm = keep.tile([P, 1], F32, name="warm")
-        x_raw = {(g, h): keep.tile([P, 2 * D], BF16, name="x_raw%d%d" % (g, h), align_bytes=64)
-                 for g in range(G) for h in range(2)}
+        zeros = keep.tile([P, 512], BF16, name="zeros")
+        x_parts = [(0, 0, 1), (0, 1, 2), (0, 2, 4), (1, 0, 2), (1, 2, 4)]
+        x_raw = {part: keep.tile([P, (part[2] - part[1]) * D], BF16, name="x_raw%d%d%d" % part, align_bytes=64) for part in x_parts}
+        load_order = [("wd", e) for e in range(E)] + [("wu", 0), ("wp", 0), ("wu", 1), ("wp", 1), ("wu", 2), ("wu", 3), ("wp", 2), ("wp", 3)]
         src = {}
         for e in range(E):
             src["wd", e], src["wp", e], src["wu", e] = wdown[e], wp[e], wup[e]
-        raw = {n: keep.tile([P, PACK, 512], BF16, name="raw_%s%d" % n, align_bytes=64) for n in src}
-        grp = {}
-        wc, ws = {}, {}
-        joint = keep.tile([P, 3 * 512 * PACK], BF16, name="joint", align_bytes=64)
-
-        def part(i):
-            return joint[:, 512 * PACK * i:512 * PACK * (i + 1)].rearrange("p (c j) -> p c j", j=PACK)
-
-        xg = [keep.tile([P, GROUP, PACK], BF16, name="xg0", align_bytes=64)[:], part(1)]
-        xc = [keep.tile([P, GROUP], U32, name="xc%d" % g, align_bytes=64) for g in range(G)]
-        xs = [keep.tile([P, GROUP], U8, name="xs%d" % g, align_bytes=64) for g in range(G)]
+        raw = {n: loads.tile([P, PACK, 512], BF16, name="raw_%s%d" % n, offset=WEIGHT_BYTES * i) for i, n in enumerate(load_order)}
+        w_stage = [keep.tile([P, 512, PACK], BF16, name="w_stage%d" % i, align_bytes=64) for i in range(3)]
+        b_stage = [keep.tile([P, 512, PACK], BF16, name="b_stage%d" % g, align_bytes=64) for g in range(G)]
+        xg = [b_stage[1], w_stage[1]]
+        staged = {}
+        codes, scales = {}, {}
+        for n in load_order + [("x", g) for g in range(G)] + [("b%d" % e, g) for e in range(E) for g in range(G)]:
+            codes[n] = keep.tile([P, 512], U32, name="codes_%s%d" % n, align_bytes=64)
+            scales[n] = keep.tile([P, 512], U8, name="scales_%s%d" % n, align_bytes=64)
         sumsq = keep.tile([P, G * PACK, E], F32, name="sumsq")
         gate = keep.tile([P, G * PACK, E], F32, name="gate")
         res = [keep.tile([P, PACK, F], F32, name="res%d" % g) for g in range(G)]
@@ -65,147 +66,106 @@ def tile_autonomyofexpertsnormgate_x1_kernel(tc, x, wdown, rgain, wup, wp, out_0
         def tokens(ap, g):
             return ap[g * GROUP:(g + 1) * GROUP, :].rearrange("(p t) d -> p t d", t=PACK)
 
-        def load_x(g, h):
-            nc.sync.dma_start(out=x_raw[g, h][:].rearrange("p (s d) -> p s d", s=2), in_=tokens(x, g)[:, 2 * h:2 * h + 2, :])
+        def load_x(g, lo, hi):
+            nc.sync.dma_start(out=x_raw[g, lo, hi][:].rearrange("p (s d) -> p s d", d=D), in_=tokens(x, g)[:, lo:hi, :])
 
         def load_w(n):
             nc.sync.dma_start(out=raw[n][:], in_=src[n].rearrange("(p j) c -> p j c", j=PACK))
 
-        nc.vector.memset(gain_rows[:].bitcast(I32), 0)
-        load_x(0, 0)
-        nc.sync.dma_start(out=gain_rows[0:E, :], in_=rgain)
-        load_w(("wd", 0))
-        load_x(0, 1)
-        load_x(1, 0)
-        load_x(1, 1)
-        for e in range(1, E):
-            load_w(("wd", e))
-        for e in range(E):
-            load_w(("wp", e))
-            load_w(("wu", e))
+        load_x(*x_parts[0])
+        load_w(load_order[0])
+        load_x(*x_parts[1])
+        nc.sync.dma_start(out=gain[:, :, 0:PACK], in_=rgain.rearrange("e (p j) -> p e j", j=PACK))
+        load_x(*x_parts[2])
+        load_w(load_order[1])
+        load_x(*x_parts[3])
+        load_x(*x_parts[4])
+        for n in load_order[2:]:
+            load_w(n)
 
         nc.vector.memset(warm[:], 0.0)
+        nc.vector.memset(zeros[:], 0.0)
         nc.scalar.activation(out=warm[:], in_=warm[:], func=ACT.Sqrt)
         make_identity(nc, ident[:])
         nc.gpsimd.tensor_copy(out=ident_b[:], in_=ident[:])
 
-        late = []
+        banks = {"v": [0, 1, 2, 3], "s": [4, 5, 6, 7]}
+
+        def bank_at(b):
+            return {"tag": "bank%d" % b, "bufs": 1, "offset": BANK * b}
 
         def bank_of(reader):
-            at = BANK * (0 if reader == "v" else 4)
-            if late:
-                return {"tag": reader + "3", "bufs": 3, "offset": at}
-            return {"tag": reader + "4", "bufs": 4, "offset": at}
+            banks[reader].append(banks[reader].pop(0))
+            return bank_at(banks[reader][-1])
 
         def cols(t):
             return slice(P * t, P * (t + 1))
 
-        def ilv_views(n):
-            dst = grp[n][:].rearrange("p (q m) j -> p q m j", q=4)
-            if n[0] == "wd":
-                return dst, raw[n][:].rearrange("p j (m q) -> p q m j", q=4)
-            return dst, raw[n][:].rearrange("p j (q m) -> p q m j", q=4)
+        def mx(out, left, left_cols, right, right_cols):
+            nc.tensor.matmul_mx(out=out, lhsT=codes[left][:, left_cols].bitcast(FP8X4), lhsT_scale=scales[left][:, left_cols],
+                                rhs=codes[right][:, right_cols].bitcast(FP8X4), rhs_scale=scales[right][:, right_cols],
+                                start=True, stop=True)
 
-        solo = keep.tile([P, 512, PACK], BF16, name="solo", align_bytes=64)
+        whole = slice(0, 512)
 
-        def stage(n, tag):
-            grp[n] = part(1) if tag == "shared" else solo[:]
+        def lay_views(n, lo, hi):
+            dst = staged[n][:].rearrange("p (q m) j -> p q m j", q=4)
+            rows = raw[n][:].rearrange("p j (m q) -> p q m j" if n[0] == "wd" else "p j (q m) -> p q m j", q=4)
+            return dst[:, :, lo:hi, :], rows[:, :, lo:hi, :]
 
-        def ilv_gpsimd(n, share):
-            dst, rows = ilv_views(n)
-            nc.gpsimd.tensor_scalar(out=dst[:, :, share:P, :], in0=rows[:, :, share:P, :], scalar1=1.0, scalar2=0.0,
-                                    op0=ALU.mult, op1=ALU.add)
+        def lay_gpsimd(n, lo, hi):
+            dst, rows = lay_views(n, lo, hi)
+            nc.gpsimd.tensor_scalar(out=dst, in0=rows, scalar1=1.0, scalar2=0.0, op0=ALU.mult, op1=ALU.add)
 
-        def ilv_share(n, share):
-            bank = psum.tile([P, 4, share, PACK], BF16, name="pw", **bank_of("s"))
-            dst, rows = ilv_views(n)
+        def lay_tensor(n, lo, hi):
+            bank = psum.tile([P, 4, hi - lo, PACK], BF16, name="pw", **bank_of("s"))
+            dst, rows = lay_views(n, lo, hi)
             order = "p q m j -> p j m q" if n[0] == "wd" else "p q m j -> p j q m"
             for u in range(2):
                 nc.tensor.matmul(out=bank[:, :, :, 2 * u:2 * u + 2].rearrange(order), lhsT=ident_b[:],
-                                 rhs=rows[:, :, 0:share, 2 * u:2 * u + 2].rearrange(order), start=True, stop=True)
-            nc.scalar.copy(out=dst[:, :, 0:share, :], in_=bank[:])
+                                 rhs=rows[:, :, :, 2 * u:2 * u + 2].rearrange(order), start=True, stop=True)
+            nc.scalar.copy(out=dst, in_=bank[:])
 
-        def ilv_scalar(n, h, share):
-            dst, rows = ilv_views(n)
-            nc.scalar.copy(out=dst[:, 2 * h:2 * h + 2, 0:share, :], in_=rows[:, 2 * h:2 * h + 2, 0:share, :])
+        def lay_scalar(n, lo, hi):
+            dst, rows = lay_views(n, lo, hi)
+            nc.scalar.copy(out=dst, in_=rows)
 
-        def ilv_vector(n, share):
-            dst, rows = ilv_views(n)
-            nc.vector.tensor_copy(out=dst[:, :, share:P, :], in_=rows[:, :, share:P, :])
+        def lay_vector(n, lo, hi):
+            dst, rows = lay_views(n, lo, hi)
+            nc.vector.tensor_copy(out=dst, in_=rows)
 
-        def quant(codes, scales, grouped):
-            nc.vector.quantize_mx(out=codes[:].bitcast(FP8X4), scales=scales[:], in_=grouped[:].rearrange("p c j -> p (c j)"))
+        def quant(n, lo=0, hi=512):
+            nc.vector.quantize_mx(out=codes[n][:, lo:hi].bitcast(FP8X4), scales=scales[n][:, lo:hi],
+                                  in_=staged[n][:, lo:hi, :].rearrange("p c j -> p (c j)"))
 
-        def quant_cols(codes, scales, grouped, lo, hi):
-            nc.vector.quantize_mx(out=codes[:, lo:hi].bitcast(FP8X4), scales=scales[:, lo:hi],
-                                  in_=grouped[:, lo:hi, :].rearrange("p c j -> p (c j)"))
-
-        def planes(name, width):
-            return (keep.tile([P, width], U32, name="codes_" + name, align_bytes=64)[:],
-                    keep.tile([P, width], U8, name="scales_" + name, align_bytes=64)[:])
-
-        def quant_w(n):
-            wc[n], ws[n] = planes("%s%d" % n, 512)
-            quant(wc[n], ws[n], grp[n])
-
-        def x_turn(g, h):
-            words = x_raw[g, h][:].bitcast(F32)
+        def x_turn(g, lo, hi):
+            words = x_raw[g, lo, hi][:].bitcast(F32)
             dstw = xg[g][:].rearrange("p c j -> p (c j)").bitcast(F32).rearrange("p (s r u) -> p s r u", r=P, u=2)
-            bank = psum.tile([P, 512], F32, name="pt", **bank_of("s"))
-            view = bank[:].rearrange("p (s u r) -> p s u r", s=2, u=2)
-            for s in range(2):
+            bank = psum.tile([P, (hi - lo) * 256], F32, name="pt", **bank_of("s"))
+            view = bank[:].rearrange("p (s u r) -> p s u r", r=P, u=2)
+            for s in range(hi - lo):
                 for u in range(2):
                     nc.tensor.transpose(view[:, s, u, :], words[:, 256 * s + u:256 * (s + 1):2], ident[:])
-            nc.scalar.copy(out=dstw[:, 2 * h:2 * h + 2], in_=view.rearrange("p s u r -> p s r u"))
+            nc.scalar.copy(out=dstw[:, lo:hi], in_=view.rearrange("p s u r -> p s r u"))
 
-        def warm_up():
-            bank = psum.tile([P, P], F32, name="pz", **bank_of("v"))
-            for i in range(3):
-                nc.tensor.matmul(out=bank[:], lhsT=ident[:], rhs=ident[:], start=True, stop=True)
+        def warm_up(count):
+            bank = psum.tile([P, 512], F32, name="pz", **bank_of("v"))
+            for i in range(count):
+                nc.tensor.matmul(out=bank[:], lhsT=zeros[:, 0:P], rhs=zeros[:], start=True, stop=True)
 
-        def gain_turn():
-            words = gain_rows[:].bitcast(F32)
-            bank = psum.tile([P, 2, P], F32, name="pg", **bank_of("s"))
-            for u in range(2):
-                nc.tensor.transpose(bank[:, u, :], words[:, u::2], ident[:])
-            nc.scalar.copy(out=gain[:].rearrange("p e j -> p (e j)").bitcast(F32).rearrange("p (e u) -> p e u", u=2),
-                           in_=bank[:, :, 0:E].rearrange("p u e -> p e u"))
-
-        bgrp, bc, bs = {}, {}, {}
-
-        def a_unit(e, g, t):
-            n = ("wd", e)
+        def b_tile(e, g, t, stage):
             ranks = psum.tile([P, 512], F32, name="pa", **bank_of("v"))
             for k in range(PACK):
-                nc.tensor.matmul_mx(out=ranks[:, cols(k)], lhsT=wc[n][:, cols(k)].bitcast(FP8X4), lhsT_scale=ws[n][:, cols(k)],
-                                    rhs=xc[g][:, cols(t)].bitcast(FP8X4), rhs_scale=xs[g][:, cols(t)], start=True, stop=True)
-            if t == 0:
-                bgrp[e, g] = part(2 * (len(bgrp) % 2))
-            nc.vector.tensor_tensor(out=bgrp[e, g][:, cols(t), :], in0=ranks[:].rearrange("p (k n) -> p n k", k=PACK),
-                                    in1=gain[:, e, :].unsqueeze(1).to_broadcast([P, P, PACK]), op=ALU.mult)
+                mx(ranks[:, cols(k)], ("wd", e), cols(k), ("x", g), cols(t))
+            staged["b%d" % e, g] = stage
+            nc.vector.tensor_tensor(out=stage[:, cols(t), :], in0=ranks[:].rearrange("p (k n) -> p n k", k=PACK),
+                                    in1=gain[:, e, 0:PACK].unsqueeze(1).to_broadcast([P, P, PACK]), op=ALU.mult)
 
-        def sq_unit(e, g, t):
-            n = ("wd", e)
+        def square_tile(e, g, t):
             toks = psum.tile([P, 512], F32, name="pb", **bank_of("s"))
-            nc.tensor.matmul_mx(out=toks[:], lhsT=xc[g][:, cols(t)].bitcast(FP8X4), lhsT_scale=xs[g][:, cols(t)],
-                                rhs=wc[n][:].bitcast(FP8X4), rhs_scale=ws[n][:], start=True, stop=True)
-            sq = work.tile([P, 512], BF16, name="sq", bufs=2)
+            mx(toks[:], ("x", g), cols(t), ("wd", e), whole)
+            sq = work.tile([P, 512], BF16, name="sq")
             nc.scalar.activation(out=sq[:], in_=toks[:], func=ACT.Square, accum_out=sumsq[:, PACK * g + t, e:e + 1])
-
-        def b_codes(e, g):
-            bc[e, g], bs[e, g] = planes("b%d%d" % (e, g), GROUP)
-
-        def joint_quant(s, key, n):
-            codes, scales = planes("joint%d" % s, 1024)
-            first = s % 2
-            nc.vector.quantize_mx(out=codes.bitcast(FP8X4), scales=scales, in_=joint[:, 2048 * first:2048 * (first + 2)])
-            b_at, w_at = slice(512 * first, 512 * (first + 1)), slice(512 * (1 - first), 512 * (2 - first))
-            bc[key], bs[key] = codes[:, b_at], scales[:, b_at]
-            wc[n], ws[n] = codes[:, w_at], scales[:, w_at]
-
-        def b_quant(e, g):
-            b_codes(e, g)
-            quant(bc[e, g], bs[e, g], bgrp[e, g])
 
         score, z, sz, rest, quot, ex = (keep.tile([P, G * PACK, E], F32, name=name)
                                         for name in ("score", "z", "sz", "rest", "quot", "ex"))
@@ -214,20 +174,50 @@ def tile_autonomyofexpertsnormgate_x1_kernel(tc, x, wdown, rgain, wup, wp, out_0
         def over_experts(tile):
             return tile[:].to_broadcast([P, G * PACK, E])
 
-        term = {}
-        last_term = keep.tile([P, PACK, F], F32, name="last_term")
-
         acts = {}
-        kept = [keep.tile([P, 2, F], F32, name="kept%d" % e) for e in range(E)]
+
+        def silu_tile(e, g, t):
+            up = psum.tile([P, 512], F32, name="pu", **bank_of("s"))
+            mx(up[:], ("b%d" % e, g), cols(t), ("wu", e), whole)
+            acts[e, g, t] = work.tile([P, F], F32, name="act", bufs=SILU_LEAD + 3)
+            nc.scalar.activation(out=acts[e, g, t][:], in_=up[:], func=ACT.Silu)
+
+        terms = {}
+
+        def term_of(e, g, t):
+            if e == 0 and (g, t // 2) != (0, 0):
+                return res[g][:, t, :]
+            if (e, g) not in terms:
+                at = 2 * (len(terms) % 4)
+                terms[e, g] = loads.tile([P, PACK, F], F32, name="term%d%d" % (e, g), offset=WEIGHT_BYTES * at)
+            return terms[e, g][:, t, :]
+
+        def product_tile(e, g, t):
+            lin = psum.tile([P, 512], F32, name="pp", **bank_of("v"))
+            mx(lin[:], ("x", g), cols(t), ("wp", e), whole)
+            nc.vector.scalar_tensor_tensor(out=term_of(e, g, t), in0=lin[:], scalar=gate[:, PACK * g + t, e:e + 1],
+                                           in1=acts[e, g, t][:], op0=ALU.mult, op1=ALU.mult)
+
+        def flat(ap):
+            return ap.rearrange("p t f -> p (t f)")
+
+        def add_term(engine, e, g, span):
+            dst = flat(res[g][:])[:, span]
+            engine.tensor_tensor(out=dst, in0=dst, in1=flat(terms[e, g][:])[:, span], op=ALU.add)
+
+        def store_pair(g, h):
+            nc.sync.dma_start(out=tokens(out_0, g)[:, 2 * h:2 * h + 2, :], in_=res[g][:, 2 * h:2 * h + 2, :])
+
         turned = keep.tile([P, 2, F], F32, name="turned")
-        sums = {}
+        sums, held = {}, {}
 
         def sum_turn(e):
             for t in range(2):
                 if e == 0:
-                    sums[t] = psum.tile([P, F], F32, name="psum_sum", tag="sum%d" % t, bufs=1, offset=BANK * (3 + 4 * t))
+                    held[t] = banks["vs"[t]].pop(0)
+                    sums[t] = psum.tile([P, F], F32, name="psum_sum", **bank_at(held[t]))
                 for c in range(4):
-                    nc.tensor.matmul(out=sums[t][:, cols(c)], lhsT=kept[e][:, t, cols(c)], rhs=ident[:], is_transpose=True,
+                    nc.tensor.matmul(out=sums[t][:, cols(c)], lhsT=terms[e, 0][:, t, cols(c)], rhs=ident[:], is_transpose=True,
                                      start=(e, c) == (0, 0), stop=(e, c) == (E - 1, 3))
             if e == E - 1:
                 for t in range(2):
@@ -235,45 +225,13 @@ def tile_autonomyofexpertsnormgate_x1_kernel(tc, x, wdown, rgain, wup, wp, out_0
 
         def sum_back():
             for t in range(2):
-                back = psum.tile([P, F], F32, name="psum_back", tag="sum%d" % t, bufs=1, offset=BANK * (3 + 4 * t))
+                back = psum.tile([P, F], F32, name="psum_back", **bank_at(held[t]))
                 for c in range(4):
                     nc.tensor.transpose(back[:, cols(c)], turned[:, t, cols(c)], ident[:])
                 nc.scalar.copy(out=res[0][:, t, :], in_=back[:])
-            nc.sync.dma_start(out=tokens(out_0, 0)[:, 0:2, :], in_=res[0][:, 0:2, :])
+            store_pair(0, 0)
 
-        def u_unit(e, g, t):
-            up = psum.tile([P, 512], F32, name="pu", **bank_of("s"))
-            nc.tensor.matmul_mx(out=up[:], lhsT=bc[e, g][:, cols(t)].bitcast(FP8X4), lhsT_scale=bs[e, g][:, cols(t)],
-                                rhs=wc["wu", e][:].bitcast(FP8X4), rhs_scale=ws["wu", e][:], start=True, stop=True)
-            acts[e, g, t] = work.tile([P, F], F32, name="act", bufs=7)
-            nc.scalar.activation(out=acts[e, g, t][:], in_=up[:], func=ACT.Silu)
-
-        def b_unit(e, g, t):
-            lin = psum.tile([P, 512], F32, name="pp", **bank_of("v"))
-            nc.tensor.matmul_mx(out=lin[:], lhsT=xc[g][:, cols(t)].bitcast(FP8X4), lhsT_scale=xs[g][:, cols(t)],
-                                rhs=wc["wp", e][:].bitcast(FP8X4), rhs_scale=ws["wp", e][:], start=True, stop=True)
-            if (e, g) == (E - 1, G - 1):
-                dst = last_term[:, t, :]
-            elif g == 0 and t < 2:
-                dst = kept[e][:, t, :]
-            elif e == 0:
-                dst = res[g][:, t, :]
-            else:
-                if (e, g) not in term:
-                    term[e, g] = work.tile([P, PACK, F], F32, name="term", bufs=2)
-                dst = term[e, g][:, t, :]
-            nc.vector.scalar_tensor_tensor(out=dst, in0=lin[:], scalar=gate[:, PACK * g + t, e:e + 1], in1=acts[e, g, t][:],
-                                           op0=ALU.mult, op1=ALU.mult)
-
-        def b_add(engine, e, g, h):
-            cut = V_SUM if g else 2 * F
-            span = (slice(0, cut), slice(cut, PACK * F))[h]
-            dst = res[g][:].rearrange("p t f -> p (t f)")[:, span]
-            engine.tensor_tensor(out=dst, in0=dst, in1=term[e, g][:].rearrange("p t f -> p (t f)")[:, span], op=ALU.add)
-            if e == E - 1:
-                nc.sync.dma_start(out=tokens(out_0, g)[:, 2 * h:2 * h + 2, :], in_=res[g][:, 2 * h:2 * h + 2, :])
-
-        og = [keep.tile([P, F, PACK], BF16, name="og%d" % g, align_bytes=64) for g in range(G)]
+        og = b_stage
         oc = [keep.tile([P, F], U32, name="oc%d" % g, align_bytes=64) for g in range(G)]
         osc = keep.tile([P, F], U8, name="osc", align_bytes=64)
 
@@ -289,133 +247,139 @@ def tile_autonomyofexpertsnormgate_x1_kernel(tc, x, wdown, rgain, wup, wp, out_0
             for q in range(4):
                 nc.sync.dma_start(out=out_2[:, 4 * q:4 * q + 4, :].bitcast(I32), in_=osc[32 * q:32 * q + 4 * G, :].bitcast(I32))
 
-        stage(("wd", 0), "head")
-        warm_up()
-        x_turn(0, 0)
-        for h in range(2):
-            ilv_scalar(("wd", 0), h, S_SHARE_HEAD)
-        ilv_vector(("wd", 0), S_SHARE_HEAD)
-        quant_cols(xc[0], xs[0], xg[0], 0, 2 * P)
-        gain_turn()
-        warm_up()
-        x_turn(0, 1)
-        quant_w(("wd", 0))
-        quant_cols(xc[0], xs[0], xg[0], 2 * P, 4 * P)
-        x_turn(1, 0)
+        staged["x", 0], staged["x", 1], staged["wd", 0], staged["wd", 1] = xg[0], xg[1], w_stage[2], w_stage[0]
+        warm_up(3)
+        x_turn(*x_parts[0])
+        lay_scalar(("wd", 0), 0, HEAD_SHARE)
+        lay_vector(("wd", 0), HEAD_SHARE, P)
+        quant(("x", 0), 0, P)
+        warm_up(2)
+        x_turn(*x_parts[1])
+        quant(("wd", 0))
+        x_turn(*x_parts[2])
+        quant(("x", 0), P, 2 * P)
+        lay_vector(("wd", 1), HEAD_SHARE, P)
+        lay_scalar(("wd", 1), 0, HEAD_SHARE)
 
-        steps = [(0, 0), (0, 1), (1, 0), (1, 1), (2, 0), (3, 0), (2, 1), (3, 1)]
-        later = [("wd", 1), ("wd", 2), ("wd", 3), ("wp", 0), ("wu", 0), ("wp", 1), ("wu", 1)]
-        a_units = [(e, g, t) for e, g in steps for t in range(PACK)]
-        cycles = [(0, 0), (0, 1), (1, 0), (1, 1), (2, 0), (3, 0), (2, 1), (3, 1)]
-        last = [("wu", 2), ("wu", 3), ("wp", 2)]
-        units = [(e, g, t) for e, g in cycles for t in range(PACK)]
+        cycles = [[(e, g, t) for t in range(PACK)] for e, g in ((0, 0), (0, 1), (1, 0), (2, 0), (3, 0), (1, 1))]
+        cycles += [[(e, 1, 2 * h + s) for e in (2, 3) for s in range(2)] for h in range(2)]
+        units = [unit for cycle in cycles for unit in cycle]
+        steps = [(0, 0), (1, 0), (0, 1), (1, 1), (2, 0), (2, 1), (3, 0), (3, 1)]
 
-        def scalar_side(j):
-            if j < len(a_units):
-                sq_unit(*a_units[j])
-                if j == len(a_units) - 1:
-                    nc.scalar.activation(out=score[:], in_=sumsq[:], func=ACT.Sqrt)
-            elif j < len(a_units) + len(units):
-                u_unit(*units[j - len(a_units)])
+        def squares(e, g):
+            return [lambda t=t: square_tile(e, g, t) for t in range(PACK)]
 
-        def share_out(n, share):
-            stage(n, "shared")
-            ilv_gpsimd(n, share)
+        def through_tensor(n, lo):
+            mid = (lo + P) // 2
+            return [lambda: lay_tensor(n, lo, mid), lambda: lay_tensor(n, mid, P)]
 
-        for t in range(PACK):
-            a_unit(*a_units[t])
-            if t == 1:
-                x_turn(1, 1)
-                scalar_side(0)
-            if t == 2:
-                quant(xc[1], xs[1], xg[1])
-                share_out(later[0], S_SHARE_A)
-                scalar_side(1)
-        scalar_side(2)
-        ilv_share(later[0], S_SHARE_A)
-        scalar_side(3)
-        issued = PACK
-        for i in range(PACK, len(a_units)):
-            s, t = divmod(i, PACK)
-            a_unit(*a_units[i])
-            upto = min(i + max(0, s - len(steps) + 1 + LEAD), len(a_units) - 1)
-            for j in range(issued, upto + 1):
-                scalar_side(j)
-            issued = upto + 1
-            if t == 1 and s < len(later):
-                joint_quant(s - 1, steps[s - 1], later[s - 1])
-                share_out(later[s], S_SHARE_A)
-            if t == PACK - 1 and s < len(later) - 1:
-                ilv_share(later[s], S_SHARE_A)
-            if t == 1 and s == len(later):
-                nc.vector.tensor_reduce(out=top[:, :, 0], in_=score[:], axis=AX.X, op=ALU.max)
-                b_quant(*steps[s - 1])
-                nc.vector.scalar_tensor_tensor(out=z[:], in0=score[:], scalar=-1.0, in1=over_experts(top),
-                                               op0=ALU.add, op1=ALU.subtract)
-                nc.scalar.activation(out=sz[:], in_=z[:], func=ACT.Silu)
-                ilv_share(later[-1], S_SHARE_A)
-            if i == len(a_units) - 2:
-                nc.vector.tensor_tensor(out=rest[:], in0=z[:], in1=sz[:], op=ALU.subtract)
-        for j in range(issued, len(a_units) + LEAD_B):
-            scalar_side(j)
+        def gate_root():
+            nc.scalar.activation(out=score[:], in_=sumsq[:], func=ACT.Sqrt)
 
-        b_codes(*steps[-1])
-        last_b = (bc[steps[-1]], bs[steps[-1]], bgrp[steps[-1]])
-        wc[later[-1]], ws[later[-1]] = planes("wu1", 512)
-        last_w = (wc[later[-1]], ws[later[-1]], grp[later[-1]])
-        nc.vector.reciprocal(out=quot[:], in_=rest[:])
-        quant_cols(*last_b, 0, 2 * P)
-        nc.vector.tensor_tensor(out=ex[:], in0=sz[:], in1=quot[:], op=ALU.mult)
-        quant_cols(*last_b, 2 * P, 4 * P)
-        nc.vector.tensor_reduce(out=total[:, :, 0], in_=ex[:], axis=AX.X, op=ALU.add)
-        quant_cols(*last_w, 0, P)
-        nc.vector.reciprocal(out=inv[:], in_=total[:])
-        quant_cols(*last_w, P, 2 * P)
-        nc.vector.tensor_tensor(out=gate[:], in0=ex[:], in1=over_experts(inv), op=ALU.mult)
-        quant_cols(*last_w, 2 * P, 4 * P)
+        own = [("wd", 2), ("wd", 3), ("wp", 0), ("wp", 1)]
+        shared = [("x", 1), ("wu", 0), ("wu", 1), ("wu", 2)]
+        for w, slot in enumerate((0, 0, 1, 0)):
+            staged[own[w]], staged[shared[w]] = w_stage[slot], w_stage[1 - slot]
+        sq = [job for e, g in steps for job in squares(e, g)]
+        jobs = (sq[0:2] + [lambda: x_turn(*x_parts[3]), None] + sq[2:4] + [lambda: x_turn(*x_parts[4]), None] + sq[4:5] + sq[5:9]
+                + sq[9:17] + through_tensor(shared[1], G_SHARE) + sq[17:19]
+                + sq[19:27] + through_tensor(shared[2], G_SHARE) + sq[27:29]
+                + sq[29:32] + [gate_root, lambda: silu_tile(*units[0]), None] + through_tensor(shared[3], G_SHARE)
+                + [lambda i=i: silu_tile(*units[i]) for i in range(1, SILU_LEAD)])
 
-        alone = ("wp", 3)
-        for i, (e, g, t) in enumerate(units):
-            c = i // PACK
-            if t == 0 and c < len(last):
-                if c > 0:
-                    quant_w(last[c - 1])
-                share_out(last[c], S_SHARE_B)
-            if t == 0 and c == len(last):
-                stage(alone, "head")
-            if c == len(last) + 1 and t == PACK - 1:
-                quant_w(alone)
-            b_unit(e, g, t)
-            scalar_side(len(a_units) + i + LEAD_B)
-            if c < len(last) and t == 1:
-                ilv_share(last[c], S_SHARE_B)
-            if (c, t) == (len(last) - 1, PACK - 1):
-                quant_w(last[-1])
-            if c == len(last):
-                dst, rows = ilv_views(alone)
-                nc.scalar.copy(out=dst[:, t], in_=rows[:, t])
-            if e > 0 and t == PACK - 1 and c < len(cycles) - 1:
-                if g == 1:
-                    b_add(nc.vector, e, g, 0)
-                b_add(nc.gpsimd, e, g, 1)
-            if (c, t) == (len(last), 0):
-                late.append(True)
-            if c == len(last) and t % 2 == 1:
-                sum_turn(t // 2)
-            if g == 0 and e >= 2 and t == PACK - 1:
+        def beside():
+            if jobs:
+                job = jobs.pop(0)
+                if job:
+                    job()
+
+        for w in range(E):
+            for i in range(2 * PACK):
+                s, t = divmod(i, PACK)
+                if i == 0 and w > 0:
+                    lay_gpsimd(own[w], 0, P)
+                    lay_gpsimd(shared[w], 0, G_SHARE)
+                b_tile(*steps[2 * w + s], t, b_stage[s])
+                beside()
+                if (w, i) == (0, 0):
+                    quant(("x", 0), 2 * P, 4 * P)
+                if (w, i) == (0, 1):
+                    quant(("wd", 1))
+                    lay_gpsimd(own[0], 0, P)
+                    beside()
+            if w < E - 1:
+                first, final = (shared[w], own[w]) if w == 0 else (own[w], shared[w])
+                for n in [first] + [("b%d" % e, g) for e, g in steps[2 * w:2 * w + 2]] + [final]:
+                    quant(n)
+                    beside()
+
+        fill = [(n, lo, lo + 2 * P) for n in (own[-1], ("b3", 0), ("b3", 1), shared[-1]) for lo in (0, 2 * P)]
+        chain = [
+            lambda: nc.vector.tensor_reduce(out=top[:, :, 0], in_=score[:], axis=AX.X, op=ALU.max),
+            lambda: nc.vector.scalar_tensor_tensor(out=z[:], in0=score[:], scalar=-1.0, in1=over_experts(top), op0=ALU.add, op1=ALU.subtract),
+            lambda: nc.scalar.activation(out=sz[:], in_=z[:], func=ACT.Silu),
+            None,
+            lambda: nc.vector.tensor_tensor(out=rest[:], in0=z[:], in1=sz[:], op=ALU.subtract),
+            lambda: nc.vector.reciprocal(out=quot[:], in_=rest[:]),
+            lambda: nc.vector.tensor_tensor(out=ex[:], in0=sz[:], in1=quot[:], op=ALU.mult),
+            lambda: nc.vector.tensor_reduce(out=total[:, :, 0], in_=ex[:], axis=AX.X, op=ALU.add),
+            lambda: nc.vector.reciprocal(out=inv[:], in_=total[:]),
+            lambda: nc.vector.tensor_tensor(out=gate[:], in0=ex[:], in1=over_experts(inv), op=ALU.mult),
+        ]
+        for i, link in enumerate(chain):
+            if link:
+                link()
+            if i not in (2, 7):
+                quant(*fill.pop(0))
+            if i != 1:
+                beside()
+        while jobs:
+            beside()
+
+        late = [("wu", 3), ("wp", 2), ("wp", 3)]
+        ahead = units[SILU_LEAD:]
+        turns = {2: (0, 1), 3: (2,), 4: (3,)}
+        spent = {0: 1, 1: 1, 2: 1, 3: 1, 4: 1}
+        for c, cycle in enumerate(cycles):
+            for k, (e, g, t) in enumerate(cycle):
+                if k == 0 and c < len(late):
+                    staged[late[c]] = staged[shared[-1]]
+                    lay_gpsimd(late[c], 0, G_SHARE_LATE)
+                product_tile(e, g, t)
+                if k == 0 and c < len(late):
+                    lay_scalar(late[c], G_SHARE_LATE, P)
+                if ahead and k >= spent.get(c, 0):
+                    silu_tile(*ahead.pop(0))
+                if c == len(cycles) - 1:
+                    dst, rows = o_views(0, P * k, P * (k + 1))
+                    nc.scalar.copy(out=dst, in_=rows)
+            if c < len(late):
+                quant(late[c])
+            for e in turns.get(c, ()):
                 sum_turn(e)
-            if (e, g, t) == (2, 1, PACK - 1):
+            if c in (2, 3, 4):
+                add_term(nc.gpsimd, c - 1, 0, slice(2 * F, PACK * F))
+            if c == 4:
+                store_pair(0, 1)
+            if c == 5:
+                add_term(nc.vector, 1, 1, slice(0, PACK * F - G_SUM))
+                add_term(nc.gpsimd, 1, 1, slice(PACK * F - G_SUM, PACK * F))
                 sum_back()
-            if c == len(cycles) - 1:
-                dst, rows = o_views(0, P * t, P * (t + 1))
-                nc.scalar.copy(out=dst, in_=rows)
+            if c == 6:
+                cut = 2 * F - G_SUM // 2
+                nc.vector.tensor_tensor(out=flat(terms[2, 1][:])[:, 0:cut], in0=flat(terms[2, 1][:])[:, 0:cut], in1=flat(terms[3, 1][:])[:, 0:cut], op=ALU.add)
+                for e in (3, 2):
+                    add_term(nc.gpsimd, e, 1, slice(cut, 2 * F))
         halves = (slice(0, F // 2), slice(F // 2, F))
-        for cs in halves:
-            nc.vector.tensor_tensor(out=res[1][:, :, cs], in0=res[1][:, :, cs], in1=last_term[:, :, cs], op=ALU.add)
-            nc.sync.dma_start(out=tokens(out_0, 1)[:, :, cs], in_=res[1][:, :, cs])
-            if cs.start == 0:
-                dst, rows = o_views(1, cs.start, cs.stop)
-                nc.scalar.copy(out=dst, in_=rows)
+        add_term(nc.vector, 2, 1, slice(0, cut))
+        store_pair(1, 0)
+        for e in (2, 3):
+            for cs in halves:
+                nc.vector.tensor_tensor(out=res[1][:, 2:4, cs], in0=res[1][:, 2:4, cs], in1=terms[e, 1][:, 2:4, cs], op=ALU.add)
+                if (e, cs.start) == (3, 0):
+                    dst, rows = o_views(1, cs.start, cs.stop)
+                    nc.scalar.copy(out=dst, in_=rows)
+        store_pair(1, 1)
         o_quant(0, 0, F)
         dst, rows = o_views(1, F // 2, F)
         nc.vector.tensor_copy(out=dst, in_=rows)

@@ -22,10 +22,11 @@ GROUP = 512
 G = T // GROUP
 BANK = 2048
 WEIGHT_BYTES = PACK * 512 * 2
-HEAD_SHARE = 32
+HEAD_SHARE = 40
 G_SHARE = 56
+G_SHARE_GATE = 48
 G_SHARE_LATE = 80
-SILU_LEAD = 8
+SILU_LEAD = int(10)
 G_SUM = 832
 GAIN_PITCH = 16
 
@@ -46,7 +47,7 @@ def tile_autonomyofexpertsnormgate_x1_kernel(tc, x, wdown, rgain, wup, wp, out_0
         zeros = keep.tile([P, 512], BF16, name="zeros")
         x_parts = [(0, 0, 1), (0, 1, 2), (0, 2, 4), (1, 0, 2), (1, 2, 4)]
         x_raw = {part: keep.tile([P, (part[2] - part[1]) * D], BF16, name="x_raw%d%d%d" % part, align_bytes=64) for part in x_parts}
-        load_order = [("wd", e) for e in range(E)] + [("wu", 0), ("wp", 0), ("wu", 1), ("wp", 1), ("wu", 2), ("wu", 3), ("wp", 2), ("wp", 3)]
+        load_order = [("wd", 0), ("wd", 1), ("wd", 2), ("wu", 0), ("wd", 3), ("wp", 0), ("wu", 1), ("wp", 1), ("wu", 2), ("wu", 3), ("wp", 2), ("wp", 3)]
         src = {}
         for e in range(E):
             src["wd", e], src["wp", e], src["wu", e] = wdown[e], wp[e], wup[e]
@@ -72,15 +73,16 @@ def tile_autonomyofexpertsnormgate_x1_kernel(tc, x, wdown, rgain, wup, wp, out_0
         def load_w(n):
             nc.sync.dma_start(out=raw[n][:], in_=src[n].rearrange("(p j) c -> p j c", j=PACK))
 
-        load_x(*x_parts[0])
         load_w(load_order[0])
+        load_x(*x_parts[0])
         load_x(*x_parts[1])
         nc.sync.dma_start(out=gain[:, :, 0:PACK], in_=rgain.rearrange("e (p j) -> p e j", j=PACK))
         load_x(*x_parts[2])
-        load_w(load_order[1])
+        for n in load_order[1:4]:
+            load_w(n)
         load_x(*x_parts[3])
         load_x(*x_parts[4])
-        for n in load_order[2:]:
+        for n in load_order[4:]:
             load_w(n)
 
         nc.vector.memset(warm[:], 0.0)
@@ -245,26 +247,28 @@ def tile_autonomyofexpertsnormgate_x1_kernel(tc, x, wdown, rgain, wup, wp, out_0
 
         def o_scales():
             for q in range(4):
-                nc.sync.dma_start(out=out_2[:, 4 * q:4 * q + 4, :].bitcast(I32), in_=osc[32 * q:32 * q + 4 * G, :].bitcast(I32))
+                (nc.sync, nc.scalar)[q % 2].dma_start(out=out_2[:, 4 * q:4 * q + 4, :].bitcast(I32), in_=osc[32 * q:32 * q + 4 * G, :].bitcast(I32))
 
         staged["x", 0], staged["x", 1], staged["wd", 0], staged["wd", 1] = xg[0], xg[1], w_stage[2], w_stage[0]
-        warm_up(3)
-        x_turn(*x_parts[0])
+        warm_up(4)
         lay_scalar(("wd", 0), 0, HEAD_SHARE)
         lay_vector(("wd", 0), HEAD_SHARE, P)
-        quant(("x", 0), 0, P)
-        warm_up(2)
+        x_turn(*x_parts[0])
         x_turn(*x_parts[1])
         quant(("wd", 0))
         x_turn(*x_parts[2])
+        warm_up(2)
+        quant(("x", 0), 0, P)
         quant(("x", 0), P, 2 * P)
-        lay_vector(("wd", 1), HEAD_SHARE, P)
+        lay_vector(("wd", 1), HEAD_SHARE, (HEAD_SHARE + P) // 2)
+        quant(("x", 0), 2 * P, 4 * P)
+        lay_vector(("wd", 1), (HEAD_SHARE + P) // 2, P)
         lay_scalar(("wd", 1), 0, HEAD_SHARE)
 
         cycles = [[(e, g, t) for t in range(PACK)] for e, g in ((0, 0), (0, 1), (1, 0), (2, 0), (3, 0), (1, 1))]
         cycles += [[(e, 1, 2 * h + s) for e in (2, 3) for s in range(2)] for h in range(2)]
         units = [unit for cycle in cycles for unit in cycle]
-        steps = [(0, 0), (1, 0), (0, 1), (1, 1), (2, 0), (2, 1), (3, 0), (3, 1)]
+        steps = [(0, 0), (1, 0), (2, 0), (0, 1), (3, 0), (1, 1), (2, 1), (3, 1)]
 
         def squares(e, g):
             return [lambda t=t: square_tile(e, g, t) for t in range(PACK)]
@@ -278,17 +282,18 @@ def tile_autonomyofexpertsnormgate_x1_kernel(tc, x, wdown, rgain, wup, wp, out_0
 
         own = [("wd", 2), ("wd", 3), ("wp", 0), ("wp", 1)]
         shared = [("x", 1), ("wu", 0), ("wu", 1), ("wu", 2)]
-        for w, slot in enumerate((0, 0, 1, 0)):
-            staged[own[w]], staged[shared[w]] = w_stage[slot], w_stage[1 - slot]
-        sq = [job for e, g in steps for job in squares(e, g)]
-        jobs = (sq[0:2] + [lambda: x_turn(*x_parts[3]), None] + sq[2:4] + [lambda: x_turn(*x_parts[4]), None] + sq[4:5] + sq[5:9]
-                + sq[9:17] + through_tensor(shared[1], G_SHARE) + sq[17:19]
-                + sq[19:27] + through_tensor(shared[2], G_SHARE) + sq[27:29]
-                + sq[29:32] + [gate_root, lambda: silu_tile(*units[0]), None] + through_tensor(shared[3], G_SHARE)
-                + [lambda i=i: silu_tile(*units[i]) for i in range(1, SILU_LEAD)])
+        for w, (mine, other) in enumerate(((0, 1), (1, 2), (2, 0), (0, 1))):
+            staged[own[w]], staged[shared[w]] = w_stage[mine], w_stage[other]
+        sq = [job for e, g in ((0, 0), (1, 0), (2, 0), (0, 1), (1, 1), (3, 0), (2, 1), (3, 1)) for job in squares(e, g)]
+        silus = [lambda i=i: silu_tile(*units[i]) for i in range(SILU_LEAD)]
+        last_share = through_tensor(shared[3], G_SHARE_GATE)
+        jobs = (sq[0:4] + [lambda: lay_scalar(shared[1], G_SHARE, P)] + sq[4:6]
+                + [lambda: x_turn(*x_parts[3]), lambda: x_turn(*x_parts[4])] + sq[6:30]
+                + through_tensor(shared[2], G_SHARE) + sq[30:32]
+                + last_share[:1] + [gate_root, None, None, silus[0]] + last_share[1:] + silus[1:])
 
-        def beside():
-            if jobs:
+        def beside(count=1):
+            for i in range(min(count, len(jobs))):
                 job = jobs.pop(0)
                 if job:
                     job()
@@ -298,65 +303,64 @@ def tile_autonomyofexpertsnormgate_x1_kernel(tc, x, wdown, rgain, wup, wp, out_0
                 s, t = divmod(i, PACK)
                 if i == 0 and w > 0:
                     lay_gpsimd(own[w], 0, P)
-                    lay_gpsimd(shared[w], 0, G_SHARE)
+                    if w < E - 1:
+                        lay_gpsimd(shared[w], 0, G_SHARE)
                 b_tile(*steps[2 * w + s], t, b_stage[s])
-                beside()
-                if (w, i) == (0, 0):
-                    quant(("x", 0), 2 * P, 4 * P)
+                beside({(0, 7): 2}.get((w, i), 1))
+                if (w, i) == (E - 1, 2):
+                    nc.vector.tensor_reduce(out=top[:, :, 0], in_=score[:], axis=AX.X, op=ALU.max)
+                    nc.gpsimd.tensor_tensor(out=z[:], in0=score[:], in1=over_experts(top), op=ALU.subtract)
+                    lay_gpsimd(shared[w], 0, G_SHARE_GATE)
+                if (w, i) == (E - 1, 6):
+                    nc.scalar.activation(out=sz[:], in_=z[:], func=ACT.Silu, bias=-1.0)
                 if (w, i) == (0, 1):
                     quant(("wd", 1))
                     lay_gpsimd(own[0], 0, P)
-                    beside()
             if w < E - 1:
-                first, final = (shared[w], own[w]) if w == 0 else (own[w], shared[w])
-                for n in [first] + [("b%d" % e, g) for e, g in steps[2 * w:2 * w + 2]] + [final]:
+                for n in [own[w]] + [("b%d" % e, g) for e, g in steps[2 * w:2 * w + 2]] + [shared[w]]:
                     quant(n)
                     beside()
 
-        fill = [(n, lo, lo + 2 * P) for n in (own[-1], ("b3", 0), ("b3", 1), shared[-1]) for lo in (0, 2 * P)]
+        fill = [(own[-1],), (("b2", 1),)] + [(n, lo, lo + 2 * P) for n in (("b3", 1), shared[-1]) for lo in (0, 2 * P)]
         chain = [
-            lambda: nc.vector.tensor_reduce(out=top[:, :, 0], in_=score[:], axis=AX.X, op=ALU.max),
-            lambda: nc.vector.scalar_tensor_tensor(out=z[:], in0=score[:], scalar=-1.0, in1=over_experts(top), op0=ALU.add, op1=ALU.subtract),
-            lambda: nc.scalar.activation(out=sz[:], in_=z[:], func=ACT.Silu),
-            None,
-            lambda: nc.vector.tensor_tensor(out=rest[:], in0=z[:], in1=sz[:], op=ALU.subtract),
+            lambda: nc.vector.scalar_tensor_tensor(out=rest[:], in0=z[:], scalar=-1.0, in1=sz[:], op0=ALU.add, op1=ALU.subtract),
             lambda: nc.vector.reciprocal(out=quot[:], in_=rest[:]),
             lambda: nc.vector.tensor_tensor(out=ex[:], in0=sz[:], in1=quot[:], op=ALU.mult),
             lambda: nc.vector.tensor_reduce(out=total[:, :, 0], in_=ex[:], axis=AX.X, op=ALU.add),
             lambda: nc.vector.reciprocal(out=inv[:], in_=total[:]),
             lambda: nc.vector.tensor_tensor(out=gate[:], in0=ex[:], in1=over_experts(inv), op=ALU.mult),
         ]
-        for i, link in enumerate(chain):
-            if link:
-                link()
-            if i not in (2, 7):
-                quant(*fill.pop(0))
-            if i != 1:
-                beside()
+        for link, call in zip(chain, fill):
+            link()
+            quant(*call)
+            beside()
         while jobs:
             beside()
 
         late = [("wu", 3), ("wp", 2), ("wp", 3)]
         ahead = units[SILU_LEAD:]
-        turns = {2: (0, 1), 3: (2,), 4: (3,)}
-        spent = {0: 1, 1: 1, 2: 1, 3: 1, 4: 1}
+        turns = [{3: (0, 1), 4: (2,), 5: (3,)}, {1: (0,), 3: (1,), 4: (2,), 5: (3,)}, {2: (0,), 3: (1,), 4: (2,), 5: (3,)}][2]
+        spent = dict(enumerate([1, 1, 1, 1, 2, 1]))
         for c, cycle in enumerate(cycles):
             for k, (e, g, t) in enumerate(cycle):
                 if k == 0 and c < len(late):
                     staged[late[c]] = staged[shared[-1]]
                     lay_gpsimd(late[c], 0, G_SHARE_LATE)
                 product_tile(e, g, t)
-                if k == 0 and c < len(late):
+                if k == 1 and c < len(late):
                     lay_scalar(late[c], G_SHARE_LATE, P)
-                if ahead and k >= spent.get(c, 0):
+                if k == 1:
+                    for e in turns.get(c, ()):
+                        sum_turn(e)
+                    if c == 6:
+                        sum_back()
+                if ahead and k not in range(0, 0 + spent.get(c, 0)):
                     silu_tile(*ahead.pop(0))
                 if c == len(cycles) - 1:
                     dst, rows = o_views(0, P * k, P * (k + 1))
                     nc.scalar.copy(out=dst, in_=rows)
             if c < len(late):
                 quant(late[c])
-            for e in turns.get(c, ()):
-                sum_turn(e)
             if c in (2, 3, 4):
                 add_term(nc.gpsimd, c - 1, 0, slice(2 * F, PACK * F))
             if c == 4:
@@ -364,22 +368,20 @@ def tile_autonomyofexpertsnormgate_x1_kernel(tc, x, wdown, rgain, wup, wp, out_0
             if c == 5:
                 add_term(nc.vector, 1, 1, slice(0, PACK * F - G_SUM))
                 add_term(nc.gpsimd, 1, 1, slice(PACK * F - G_SUM, PACK * F))
-                sum_back()
             if c == 6:
-                cut = 2 * F - G_SUM // 2
-                nc.vector.tensor_tensor(out=flat(terms[2, 1][:])[:, 0:cut], in0=flat(terms[2, 1][:])[:, 0:cut], in1=flat(terms[3, 1][:])[:, 0:cut], op=ALU.add)
-                for e in (3, 2):
-                    add_term(nc.gpsimd, e, 1, slice(cut, 2 * F))
+                add_term(nc.vector, 2, 1, slice(0, 2 * F))
+                add_term(nc.gpsimd, 3, 1, slice(0, G_SUM))
         halves = (slice(0, F // 2), slice(F // 2, F))
-        add_term(nc.vector, 2, 1, slice(0, cut))
+        add_term(nc.vector, 3, 1, slice(G_SUM, 2 * F))
         store_pair(1, 0)
         for e in (2, 3):
             for cs in halves:
                 nc.vector.tensor_tensor(out=res[1][:, 2:4, cs], in0=res[1][:, 2:4, cs], in1=terms[e, 1][:, 2:4, cs], op=ALU.add)
+                if e == 3:
+                    nc.sync.dma_start(out=tokens(out_0, 1)[:, 2:4, cs], in_=res[1][:, 2:4, cs])
                 if (e, cs.start) == (3, 0):
                     dst, rows = o_views(1, cs.start, cs.stop)
                     nc.scalar.copy(out=dst, in_=rows)
-        store_pair(1, 1)
         o_quant(0, 0, F)
         dst, rows = o_views(1, F // 2, F)
         nc.vector.tensor_copy(out=dst, in_=rows)

@@ -23,11 +23,13 @@ G = T // GROUP
 BANK = 2048
 WEIGHT_BYTES = PACK * 512 * 2
 HEAD_SHARE = 40
+NEXT_SHARE = 32
 G_SHARE = 56
 G_SHARE_GATE = 48
-G_SHARE_LATE = 80
-SILU_LEAD = int(10)
-G_SUM = 832
+G_SHARE_LATE = 72
+SILU_LEAD = int(7)
+G_THIRD = 512
+G_SUM = 768
 GAIN_PITCH = 16
 
 
@@ -89,7 +91,7 @@ def tile_autonomyofexpertsnormgate_x1_kernel(tc, x, wdown, rgain, wup, wp, out_0
         nc.vector.memset(zeros[:], 0.0)
         nc.scalar.activation(out=warm[:], in_=warm[:], func=ACT.Sqrt)
         make_identity(nc, ident[:])
-        nc.gpsimd.tensor_copy(out=ident_b[:], in_=ident[:])
+        nc.scalar.copy(out=ident_b[:], in_=ident[:])
 
         banks = {"v": [0, 1, 2, 3], "s": [4, 5, 6, 7]}
 
@@ -260,10 +262,10 @@ def tile_autonomyofexpertsnormgate_x1_kernel(tc, x, wdown, rgain, wup, wp, out_0
         warm_up(2)
         quant(("x", 0), 0, P)
         quant(("x", 0), P, 2 * P)
-        lay_vector(("wd", 1), HEAD_SHARE, (HEAD_SHARE + P) // 2)
+        lay_vector(("wd", 1), NEXT_SHARE, (NEXT_SHARE + P) // 2)
         quant(("x", 0), 2 * P, 4 * P)
-        lay_vector(("wd", 1), (HEAD_SHARE + P) // 2, P)
-        lay_scalar(("wd", 1), 0, HEAD_SHARE)
+        lay_vector(("wd", 1), (NEXT_SHARE + P) // 2, P)
+        lay_scalar(("wd", 1), 0, NEXT_SHARE)
 
         cycles = [[(e, g, t) for t in range(PACK)] for e, g in ((0, 0), (0, 1), (1, 0), (2, 0), (3, 0), (1, 1))]
         cycles += [[(e, 1, 2 * h + s) for e in (2, 3) for s in range(2)] for h in range(2)]
@@ -287,10 +289,23 @@ def tile_autonomyofexpertsnormgate_x1_kernel(tc, x, wdown, rgain, wup, wp, out_0
         sq = [job for e, g in ((0, 0), (1, 0), (2, 0), (0, 1), (1, 1), (3, 0), (2, 1), (3, 1)) for job in squares(e, g)]
         silus = [lambda i=i: silu_tile(*units[i]) for i in range(SILU_LEAD)]
         last_share = through_tensor(shared[3], G_SHARE_GATE)
-        jobs = (sq[0:4] + [lambda: lay_scalar(shared[1], G_SHARE, P)] + sq[4:6]
-                + [lambda: x_turn(*x_parts[3]), lambda: x_turn(*x_parts[4])] + sq[6:30]
-                + through_tensor(shared[2], G_SHARE) + sq[30:32]
-                + last_share[:1] + [gate_root, None, None, silus[0]] + last_share[1:] + silus[1:])
+        turn_x = [lambda: x_turn(*x_parts[3]), lambda: x_turn(*x_parts[4])]
+        if 3 == 0:
+            jobs = (sq[0:4] + [lambda: lay_scalar(shared[1], G_SHARE, P)] + sq[4:6] + turn_x + sq[6:30]
+                    + through_tensor(shared[2], G_SHARE) + sq[30:32]
+                    + last_share[:1] + [gate_root, None, None, silus[0]] + last_share[1:] + silus[1:])
+        elif 3 == 1:
+            jobs = (sq[0:4] + [lambda: lay_scalar(shared[1], G_SHARE, P)] + sq[4:6] + turn_x + sq[6:9] + [None] + sq[9:17] + sq[17:20] + [None]
+                    + sq[20:27] + through_tensor(shared[2], G_SHARE) + sq[27:32]
+                    + last_share[:1] + [gate_root, None, silus[0]] + last_share[1:] + silus[1:])
+        elif 3 == 2:
+            jobs = (sq[0:4] + [None] + sq[4:6] + turn_x + sq[6:10] + sq[10:18] + through_tensor(shared[1], G_SHARE) + sq[18:20]
+                    + sq[20:28] + through_tensor(shared[2], G_SHARE) + sq[28:32]
+                    + last_share[:1] + [gate_root, None, silus[0]] + last_share[1:] + silus[1:])
+        elif 3 == 3:
+            jobs = (sq[0:7] + turn_x + sq[7:11] + sq[11:18] + [None] + through_tensor(shared[1], G_SHARE) + sq[18:20]
+                    + sq[20:27] + [None] + through_tensor(shared[2], G_SHARE) + sq[27:32]
+                    + last_share[:1] + [gate_root, None, None, silus[0]] + last_share[1:] + silus[1:])
 
         def beside(count=1):
             for i in range(min(count, len(jobs))):
@@ -307,7 +322,7 @@ def tile_autonomyofexpertsnormgate_x1_kernel(tc, x, wdown, rgain, wup, wp, out_0
                         lay_gpsimd(shared[w], 0, G_SHARE)
                 b_tile(*steps[2 * w + s], t, b_stage[s])
                 beside({(0, 7): 2}.get((w, i), 1))
-                if (w, i) == (E - 1, 2):
+                if (w, i) == (E - 1, 4):
                     nc.vector.tensor_reduce(out=top[:, :, 0], in_=score[:], axis=AX.X, op=ALU.max)
                     nc.gpsimd.tensor_tensor(out=z[:], in0=score[:], in1=over_experts(top), op=ALU.subtract)
                     lay_gpsimd(shared[w], 0, G_SHARE_GATE)
@@ -321,7 +336,7 @@ def tile_autonomyofexpertsnormgate_x1_kernel(tc, x, wdown, rgain, wup, wp, out_0
                     quant(n)
                     beside()
 
-        fill = [(own[-1],), (("b2", 1),)] + [(n, lo, lo + 2 * P) for n in (("b3", 1), shared[-1]) for lo in (0, 2 * P)]
+        fill = [(own[-1],)] + [(n, lo, lo + 2 * P) for n in (("b2", 1), ("b3", 1), shared[-1]) for lo in (0, 2 * P)]
         chain = [
             lambda: nc.vector.scalar_tensor_tensor(out=rest[:], in0=z[:], scalar=-1.0, in1=sz[:], op0=ALU.add, op1=ALU.subtract),
             lambda: nc.vector.reciprocal(out=quot[:], in_=rest[:]),
@@ -330,6 +345,8 @@ def tile_autonomyofexpertsnormgate_x1_kernel(tc, x, wdown, rgain, wup, wp, out_0
             lambda: nc.vector.reciprocal(out=inv[:], in_=total[:]),
             lambda: nc.vector.tensor_tensor(out=gate[:], in0=ex[:], in1=over_experts(inv), op=ALU.mult),
         ]
+        quant(*fill.pop(0))
+        beside()
         for link, call in zip(chain, fill):
             link()
             quant(*call)
@@ -339,8 +356,8 @@ def tile_autonomyofexpertsnormgate_x1_kernel(tc, x, wdown, rgain, wup, wp, out_0
 
         late = [("wu", 3), ("wp", 2), ("wp", 3)]
         ahead = units[SILU_LEAD:]
-        turns = [{3: (0, 1), 4: (2,), 5: (3,)}, {1: (0,), 3: (1,), 4: (2,), 5: (3,)}, {2: (0,), 3: (1,), 4: (2,), 5: (3,)}][2]
-        spent = dict(enumerate([1, 1, 1, 1, 2, 1]))
+        turns = [{3: (0, 1), 4: (2,), 5: (3,)}, {1: (0,), 3: (1,), 4: (2,), 5: (3,)}, {2: (0,), 3: (1,), 4: (2,), 5: (3,)}, {1: (0,), 2: (1,), 5: (2, 3)}, {2: (0, 1), 5: (2, 3)}, {1: (0,), 2: (1,), 4: (2,), 5: (3,)}][3]
+        spent = dict(enumerate([1, 1, 1, 0, 0, 0]))
         for c, cycle in enumerate(cycles):
             for k, (e, g, t) in enumerate(cycle):
                 if k == 0 and c < len(late):
@@ -348,8 +365,8 @@ def tile_autonomyofexpertsnormgate_x1_kernel(tc, x, wdown, rgain, wup, wp, out_0
                     lay_gpsimd(late[c], 0, G_SHARE_LATE)
                 product_tile(e, g, t)
                 if k == 1 and c < len(late):
-                    lay_scalar(late[c], G_SHARE_LATE, P)
-                if k == 1:
+                    (lay_scalar, lay_tensor)[0](late[c], G_SHARE_LATE, P)
+                if k == 3:
                     for e in turns.get(c, ()):
                         sum_turn(e)
                     if c == 6:
@@ -362,10 +379,10 @@ def tile_autonomyofexpertsnormgate_x1_kernel(tc, x, wdown, rgain, wup, wp, out_0
             if c < len(late):
                 quant(late[c])
             if c in (2, 3, 4):
-                add_term(nc.gpsimd, c - 1, 0, slice(2 * F, PACK * F))
-            if c == 4:
-                store_pair(0, 1)
+                add_term(nc.gpsimd, c - 1, 0, slice(2 * F if c < 4 else PACK * F - G_THIRD, PACK * F))
             if c == 5:
+                add_term(nc.vector, E - 1, 0, slice(2 * F, PACK * F - G_THIRD))
+                store_pair(0, 1)
                 add_term(nc.vector, 1, 1, slice(0, PACK * F - G_SUM))
                 add_term(nc.gpsimd, 1, 1, slice(PACK * F - G_SUM, PACK * F))
             if c == 6:

@@ -249,7 +249,7 @@ def tile_autonomyofexpertsnormgate_x1_kernel(tc, x, wdown, rgain, wup, wp, out_0
 
         def o_scales():
             for q in range(4):
-                (nc.sync, nc.scalar)[q % 2].dma_start(out=out_2[:, 4 * q:4 * q + 4, :].bitcast(I32), in_=osc[32 * q:32 * q + 4 * G, :].bitcast(I32))
+                nc.sync.dma_start(out=out_2[:, 4 * q:4 * q + 4, :].bitcast(I32), in_=osc[32 * q:32 * q + 4 * G, :].bitcast(I32))
 
         staged["x", 0], staged["x", 1], staged["wd", 0], staged["wd", 1] = xg[0], xg[1], w_stage[2], w_stage[0]
         warm_up(4)

@@ -23,13 +23,14 @@ G = T // GROUP
 BANK = 2048
 WEIGHT_BYTES = PACK * 512 * 2
 HEAD_SHARE = 40
-NEXT_SHARE = 32
-G_SHARE = 56
+NEXT_SHARE = 40
+G_SHARE = 64
 G_SHARE_GATE = 48
-G_SHARE_LATE = 72
+G_SHARE_LATE = 80
 SILU_LEAD = int(7)
-G_THIRD = 512
-G_SUM = 768
+A_CUT = 320
+D_CUT = 192
+G_SUM = 832
 GAIN_PITCH = 16
 
 
@@ -54,7 +55,8 @@ def tile_autonomyofexpertsnormgate_x1_kernel(tc, x, wdown, rgain, wup, wp, out_0
         for e in range(E):
             src["wd", e], src["wp", e], src["wu", e] = wdown[e], wp[e], wup[e]
         raw = {n: loads.tile([P, PACK, 512], BF16, name="raw_%s%d" % n, offset=WEIGHT_BYTES * i) for i, n in enumerate(load_order)}
-        w_stage = [keep.tile([P, 512, PACK], BF16, name="w_stage%d" % i, align_bytes=64) for i in range(3)]
+        stage_at = [WEIGHT_BYTES * (len(load_order) + i) for i in range(4)]
+        w_stage = [loads.tile([P, 512, PACK], BF16, name="w_stage%d" % i, align_bytes=64, offset=stage_at[i]) for i in range(4)]
         b_stage = [keep.tile([P, 512, PACK], BF16, name="b_stage%d" % g, align_bytes=64) for g in range(G)]
         xg = [b_stage[1], w_stage[1]]
         staged = {}
@@ -62,6 +64,8 @@ def tile_autonomyofexpertsnormgate_x1_kernel(tc, x, wdown, rgain, wup, wp, out_0
         for n in load_order + [("x", g) for g in range(G)] + [("b%d" % e, g) for e in range(E) for g in range(G)]:
             codes[n] = keep.tile([P, 512], U32, name="codes_%s%d" % n, align_bytes=64)
             scales[n] = keep.tile([P, 512], U8, name="scales_%s%d" % n, align_bytes=64)
+        squared_at = stage_at[-1] + WEIGHT_BYTES
+        squared = loads.tile([P, G * PACK * E, R], BF16, name="squared", offset=squared_at)
         sumsq = keep.tile([P, G * PACK, E], F32, name="sumsq")
         gate = keep.tile([P, G * PACK, E], F32, name="gate")
         res = [keep.tile([P, PACK, F], F32, name="res%d" % g) for g in range(G)]
@@ -150,7 +154,10 @@ def tile_autonomyofexpertsnormgate_x1_kernel(tc, x, wdown, rgain, wup, wp, out_0
             for s in range(hi - lo):
                 for u in range(2):
                     nc.tensor.transpose(view[:, s, u, :], words[:, 256 * s + u:256 * (s + 1):2], ident[:])
-            nc.scalar.copy(out=dstw[:, lo:hi], in_=view.rearrange("p s u r -> p s r u"))
+            if g == 1 and lo // 2 < 0:
+                nc.vector.tensor_copy(out=dstw[:, lo:hi], in_=view.rearrange("p s u r -> p s r u"))
+            else:
+                nc.scalar.copy(out=dstw[:, lo:hi], in_=view.rearrange("p s u r -> p s r u"))
 
         def warm_up(count):
             bank = psum.tile([P, 512], F32, name="pz", **bank_of("v"))
@@ -168,8 +175,7 @@ def tile_autonomyofexpertsnormgate_x1_kernel(tc, x, wdown, rgain, wup, wp, out_0
         def square_tile(e, g, t):
             toks = psum.tile([P, 512], F32, name="pb", **bank_of("s"))
             mx(toks[:], ("x", g), cols(t), ("wd", e), whole)
-            sq = work.tile([P, 512], BF16, name="sq")
-            nc.scalar.activation(out=sq[:], in_=toks[:], func=ACT.Square, accum_out=sumsq[:, PACK * g + t, e:e + 1])
+            nc.scalar.activation(out=squared[:, E * (PACK * g + t) + e, :], in_=toks[:], func=ACT.Square, accum_out=sumsq[:, PACK * g + t, e:e + 1])
 
         score, z, sz, rest, quot, ex = (keep.tile([P, G * PACK, E], F32, name=name)
                                         for name in ("score", "z", "sz", "rest", "quot", "ex"))
@@ -192,8 +198,8 @@ def tile_autonomyofexpertsnormgate_x1_kernel(tc, x, wdown, rgain, wup, wp, out_0
             if e == 0 and (g, t // 2) != (0, 0):
                 return res[g][:, t, :]
             if (e, g) not in terms:
-                at = 2 * (len(terms) % 4)
-                terms[e, g] = loads.tile([P, PACK, F], F32, name="term%d%d" % (e, g), offset=WEIGHT_BYTES * at)
+                at = 2 * (len(terms) % 5)
+                terms[e, g] = loads.tile([P, PACK, F], F32, name="term%d%d" % (e, g), offset=squared_at + WEIGHT_BYTES * at)
             return terms[e, g][:, t, :]
 
         def product_tile(e, g, t):
@@ -208,6 +214,9 @@ def tile_autonomyofexpertsnormgate_x1_kernel(tc, x, wdown, rgain, wup, wp, out_0
         def add_term(engine, e, g, span):
             dst = flat(res[g][:])[:, span]
             engine.tensor_tensor(out=dst, in0=dst, in1=flat(terms[e, g][:])[:, span], op=ALU.add)
+
+        def add(engine, out, left, right):
+            engine.tensor_tensor(out=out, in0=left, in1=right, op=ALU.add)
 
         def store_pair(g, h):
             nc.sync.dma_start(out=tokens(out_0, g)[:, 2 * h:2 * h + 2, :], in_=res[g][:, 2 * h:2 * h + 2, :])
@@ -267,8 +276,13 @@ def tile_autonomyofexpertsnormgate_x1_kernel(tc, x, wdown, rgain, wup, wp, out_0
         lay_vector(("wd", 1), (NEXT_SHARE + P) // 2, P)
         lay_scalar(("wd", 1), 0, NEXT_SHARE)
 
-        cycles = [[(e, g, t) for t in range(PACK)] for e, g in ((0, 0), (0, 1), (1, 0), (2, 0), (3, 0), (1, 1))]
-        cycles += [[(e, 1, 2 * h + s) for e in (2, 3) for s in range(2)] for h in range(2)]
+        def four(e):
+            return [(e, 0, t) for t in range(PACK)]
+
+        def two_by_two(first, h):
+            return [(e, 1, 2 * h + s) for e in (first, first + 1) for s in range(2)]
+
+        cycles = [four(0), four(1), two_by_two(0, 0), four(2), four(3), two_by_two(0, 1), two_by_two(2, 0), two_by_two(2, 1)]
         units = [unit for cycle in cycles for unit in cycle]
         steps = [(0, 0), (1, 0), (2, 0), (0, 1), (3, 0), (1, 1), (2, 1), (3, 1)]
 
@@ -277,6 +291,8 @@ def tile_autonomyofexpertsnormgate_x1_kernel(tc, x, wdown, rgain, wup, wp, out_0
 
         def through_tensor(n, lo):
             mid = (lo + P) // 2
+            if lo >= P // 2:
+                return [lambda: lay_tensor(n, lo, P), None]
             return [lambda: lay_tensor(n, lo, mid), lambda: lay_tensor(n, mid, P)]
 
         def gate_root():
@@ -290,22 +306,12 @@ def tile_autonomyofexpertsnormgate_x1_kernel(tc, x, wdown, rgain, wup, wp, out_0
         silus = [lambda i=i: silu_tile(*units[i]) for i in range(SILU_LEAD)]
         last_share = through_tensor(shared[3], G_SHARE_GATE)
         turn_x = [lambda: x_turn(*x_parts[3]), lambda: x_turn(*x_parts[4])]
-        if 3 == 0:
-            jobs = (sq[0:4] + [lambda: lay_scalar(shared[1], G_SHARE, P)] + sq[4:6] + turn_x + sq[6:30]
-                    + through_tensor(shared[2], G_SHARE) + sq[30:32]
-                    + last_share[:1] + [gate_root, None, None, silus[0]] + last_share[1:] + silus[1:])
-        elif 3 == 1:
-            jobs = (sq[0:4] + [lambda: lay_scalar(shared[1], G_SHARE, P)] + sq[4:6] + turn_x + sq[6:9] + [None] + sq[9:17] + sq[17:20] + [None]
-                    + sq[20:27] + through_tensor(shared[2], G_SHARE) + sq[27:32]
-                    + last_share[:1] + [gate_root, None, silus[0]] + last_share[1:] + silus[1:])
-        elif 3 == 2:
-            jobs = (sq[0:4] + [None] + sq[4:6] + turn_x + sq[6:10] + sq[10:18] + through_tensor(shared[1], G_SHARE) + sq[18:20]
-                    + sq[20:28] + through_tensor(shared[2], G_SHARE) + sq[28:32]
-                    + last_share[:1] + [gate_root, None, silus[0]] + last_share[1:] + silus[1:])
-        elif 3 == 3:
-            jobs = (sq[0:7] + turn_x + sq[7:11] + sq[11:18] + [None] + through_tensor(shared[1], G_SHARE) + sq[18:20]
-                    + sq[20:27] + [None] + through_tensor(shared[2], G_SHARE) + sq[27:32]
-                    + last_share[:1] + [gate_root, None, None, silus[0]] + last_share[1:] + silus[1:])
+        alone = ("wu", 3)
+        staged[alone] = w_stage[3]
+        alone_parts = through_tensor(alone, 0)
+        jobs = (sq[0:7] + turn_x + through_tensor(shared[1], G_SHARE) + sq[7:9] + sq[9:17] + alone_parts[:1] + sq[17:20]
+                + sq[20:27] + [None] + through_tensor(shared[2], G_SHARE) + sq[27:32]
+                + last_share[:1] + [gate_root, None, None, silus[0]] + last_share[1:] + alone_parts[1:] + silus[1:])
 
         def beside(count=1):
             for i in range(min(count, len(jobs))):
@@ -318,15 +324,13 @@ def tile_autonomyofexpertsnormgate_x1_kernel(tc, x, wdown, rgain, wup, wp, out_0
                 s, t = divmod(i, PACK)
                 if i == 0 and w > 0:
                     lay_gpsimd(own[w], 0, P)
-                    if w < E - 1:
-                        lay_gpsimd(shared[w], 0, G_SHARE)
+                    lay_gpsimd(shared[w], 0, G_SHARE if w < E - 1 else G_SHARE_GATE)
                 b_tile(*steps[2 * w + s], t, b_stage[s])
                 beside({(0, 7): 2}.get((w, i), 1))
-                if (w, i) == (E - 1, 4):
+                if (w, i) == (E - 1, 5):
                     nc.vector.tensor_reduce(out=top[:, :, 0], in_=score[:], axis=AX.X, op=ALU.max)
                     nc.gpsimd.tensor_tensor(out=z[:], in0=score[:], in1=over_experts(top), op=ALU.subtract)
-                    lay_gpsimd(shared[w], 0, G_SHARE_GATE)
-                if (w, i) == (E - 1, 6):
+                if (w, i) == (E - 1, 7):
                     nc.scalar.activation(out=sz[:], in_=z[:], func=ACT.Silu, bias=-1.0)
                 if (w, i) == (0, 1):
                     quant(("wd", 1))
@@ -336,7 +340,7 @@ def tile_autonomyofexpertsnormgate_x1_kernel(tc, x, wdown, rgain, wup, wp, out_0
                     quant(n)
                     beside()
 
-        fill = [(own[-1],)] + [(n, lo, lo + 2 * P) for n in (("b2", 1), ("b3", 1), shared[-1]) for lo in (0, 2 * P)]
+        fill = [(own[-1],), (("b2", 1),)] + [(n, lo, lo + 2 * P) for n in (("b3", 1), alone, shared[-1]) for lo in (0, 2 * P)]
         chain = [
             lambda: nc.vector.scalar_tensor_tensor(out=rest[:], in0=z[:], scalar=-1.0, in1=sz[:], op0=ALU.add, op1=ALU.subtract),
             lambda: nc.vector.reciprocal(out=quot[:], in_=rest[:]),
@@ -345,8 +349,9 @@ def tile_autonomyofexpertsnormgate_x1_kernel(tc, x, wdown, rgain, wup, wp, out_0
             lambda: nc.vector.reciprocal(out=inv[:], in_=total[:]),
             lambda: nc.vector.tensor_tensor(out=gate[:], in0=ex[:], in1=over_experts(inv), op=ALU.mult),
         ]
-        quant(*fill.pop(0))
-        beside()
+        for i in range(2):
+            quant(*fill.pop(0))
+            beside()
         for link, call in zip(chain, fill):
             link()
             quant(*call)
@@ -354,10 +359,10 @@ def tile_autonomyofexpertsnormgate_x1_kernel(tc, x, wdown, rgain, wup, wp, out_0
         while jobs:
             beside()
 
-        late = [("wu", 3), ("wp", 2), ("wp", 3)]
+        late = [("wp", 2), ("wp", 3)]
         ahead = units[SILU_LEAD:]
-        turns = [{3: (0, 1), 4: (2,), 5: (3,)}, {1: (0,), 3: (1,), 4: (2,), 5: (3,)}, {2: (0,), 3: (1,), 4: (2,), 5: (3,)}, {1: (0,), 2: (1,), 5: (2, 3)}, {2: (0, 1), 5: (2, 3)}, {1: (0,), 2: (1,), 4: (2,), 5: (3,)}][3]
-        spent = dict(enumerate([1, 1, 1, 0, 0, 0]))
+        turns = [{0: (0,), 1: (1,), 5: (2, 3)}, {1: (0, 1), 5: (2, 3)}, {0: (0,), 1: (1,), 4: (2,), 5: (3,)}][0]
+        spent = dict(enumerate([1, 1, 0, 0, 0, 1]))
         for c, cycle in enumerate(cycles):
             for k, (e, g, t) in enumerate(cycle):
                 if k == 0 and c < len(late):
@@ -365,33 +370,43 @@ def tile_autonomyofexpertsnormgate_x1_kernel(tc, x, wdown, rgain, wup, wp, out_0
                     lay_gpsimd(late[c], 0, G_SHARE_LATE)
                 product_tile(e, g, t)
                 if k == 1 and c < len(late):
-                    (lay_scalar, lay_tensor)[0](late[c], G_SHARE_LATE, P)
-                if k == 3:
-                    for e in turns.get(c, ()):
-                        sum_turn(e)
+                    lay_scalar(late[c], G_SHARE_LATE, P)
+                if k == PACK - 1:
+                    for turn in turns.get(c, ()):
+                        sum_turn(turn)
                     if c == 6:
                         sum_back()
-                if ahead and k not in range(0, 0 + spent.get(c, 0)):
+                if ahead and k >= spent.get(c, 0):
                     silu_tile(*ahead.pop(0))
-                if c == len(cycles) - 1:
-                    dst, rows = o_views(0, P * k, P * (k + 1))
+                if c == len(cycles) - 1 and k % 2:
+                    dst, rows = o_views(0, P * (k - 1), P * (k + 1))
                     nc.scalar.copy(out=dst, in_=rows)
             if c < len(late):
                 quant(late[c])
-            if c in (2, 3, 4):
-                add_term(nc.gpsimd, c - 1, 0, slice(2 * F if c < 4 else PACK * F - G_THIRD, PACK * F))
+            if c == 1:
+                running = loads.tile([P, 2, F], F32, name="running", offset=stage_at[1])
+                add(nc.gpsimd, running[:], res[0][:, 2:4, :], terms[1, 0][:, 2:4, :])
+            if c == 2:
+                add_term(nc.gpsimd, 1, 1, slice(0, 2 * F))
+            if c == 3:
+                add(nc.gpsimd, running[:], running[:], terms[2, 0][:, 2:4, :])
+            if c == 4:
+                add(nc.gpsimd, flat(res[0][:, 2:4, :])[:, A_CUT:], flat(running[:])[:, A_CUT:], flat(terms[3, 0][:, 2:4, :])[:, A_CUT:])
             if c == 5:
-                add_term(nc.vector, E - 1, 0, slice(2 * F, PACK * F - G_THIRD))
+                add_term(nc.vector, 1, 1, slice(2 * F, 2 * F + D_CUT))
+                add(nc.vector, flat(res[0][:, 2:4, :])[:, :A_CUT], flat(running[:])[:, :A_CUT], flat(terms[3, 0][:, 2:4, :])[:, :A_CUT])
+                add(nc.gpsimd, flat(running[:])[:, D_CUT:], flat(res[1][:, 2:4, :])[:, D_CUT:], flat(terms[1, 1][:, 2:4, :])[:, D_CUT:])
                 store_pair(0, 1)
-                add_term(nc.vector, 1, 1, slice(0, PACK * F - G_SUM))
-                add_term(nc.gpsimd, 1, 1, slice(PACK * F - G_SUM, PACK * F))
             if c == 6:
                 add_term(nc.vector, 2, 1, slice(0, 2 * F))
                 add_term(nc.gpsimd, 3, 1, slice(0, G_SUM))
         halves = (slice(0, F // 2), slice(F // 2, F))
+        last_pair = flat(res[1][:, 2:4, :])
+        add(nc.vector, last_pair[:, :D_CUT], last_pair[:, :D_CUT], flat(terms[2, 1][:, 2:4, :])[:, :D_CUT])
+        add(nc.vector, last_pair[:, D_CUT:], flat(running[:])[:, D_CUT:], flat(terms[2, 1][:, 2:4, :])[:, D_CUT:])
         add_term(nc.vector, 3, 1, slice(G_SUM, 2 * F))
         store_pair(1, 0)
-        for e in (2, 3):
+        for e in (3,):
             for cs in halves:
                 nc.vector.tensor_tensor(out=res[1][:, 2:4, cs], in0=res[1][:, 2:4, cs], in1=terms[e, 1][:, 2:4, cs], op=ALU.add)
                 if e == 3:

@@ -24,12 +24,12 @@ BANK = 2048
 WEIGHT_BYTES = PACK * 512 * 2
 HEAD_SHARE = 40
 NEXT_SHARE = 40
-G_SHARE = 64
+G_SHARE = 72
 G_SHARE_GATE = 48
 G_SHARE_LATE = 80
 SILU_LEAD = int(7)
-A_CUT = 320
-D_CUT = 192
+A_CUT = 384
+D_CUT = 128
 G_SUM = 832
 GAIN_PITCH = 16
 
@@ -57,13 +57,20 @@ def tile_autonomyofexpertsnormgate_x1_kernel(tc, x, wdown, rgain, wup, wp, out_0
         raw = {n: loads.tile([P, PACK, 512], BF16, name="raw_%s%d" % n, offset=WEIGHT_BYTES * i) for i, n in enumerate(load_order)}
         stage_at = [WEIGHT_BYTES * (len(load_order) + i) for i in range(4)]
         w_stage = [loads.tile([P, 512, PACK], BF16, name="w_stage%d" % i, align_bytes=64, offset=stage_at[i]) for i in range(4)]
-        b_stage = [keep.tile([P, 512, PACK], BF16, name="b_stage%d" % g, align_bytes=64) for g in range(G)]
+        b_both = keep.tile([P, 2 * 512, PACK], BF16, name="b_both", align_bytes=64)
+        b_stage = [b_both[:, 512 * s:512 * (s + 1), :] for s in range(2)]
         xg = [b_stage[1], w_stage[1]]
         staged = {}
         codes, scales = {}, {}
-        for n in load_order + [("x", g) for g in range(G)] + [("b%d" % e, g) for e in range(E) for g in range(G)]:
+        for n in load_order + [("x", g) for g in range(G)]:
             codes[n] = keep.tile([P, 512], U32, name="codes_%s%d" % n, align_bytes=64)
             scales[n] = keep.tile([P, 512], U8, name="scales_%s%d" % n, align_bytes=64)
+        steps = [(0, 0), (1, 0), (2, 0), (0, 1), (3, 0), (1, 1), (2, 1), (3, 1)]
+        b_codes = [keep.tile([P, 2 * 512], U32, name="codes_b%d" % w, align_bytes=64) for w in range(E)]
+        b_scales = [keep.tile([P, 2 * 512], U8, name="scales_b%d" % w, align_bytes=64) for w in range(E)]
+        for i, (e, g) in enumerate(steps):
+            half = slice(512 * (i % 2), 512 * (i % 2 + 1))
+            codes["b%d" % e, g], scales["b%d" % e, g] = b_codes[i // 2][:, half], b_scales[i // 2][:, half]
         squared_at = stage_at[-1] + WEIGHT_BYTES
         squared = loads.tile([P, G * PACK * E, R], BF16, name="squared", offset=squared_at)
         sumsq = keep.tile([P, G * PACK, E], F32, name="sumsq")
@@ -145,6 +152,9 @@ def tile_autonomyofexpertsnormgate_x1_kernel(tc, x, wdown, rgain, wup, wp, out_0
         def quant(n, lo=0, hi=512):
             nc.vector.quantize_mx(out=codes[n][:, lo:hi].bitcast(FP8X4), scales=scales[n][:, lo:hi],
                                   in_=staged[n][:, lo:hi, :].rearrange("p c j -> p (c j)"))
+
+        def quant_b(w):
+            nc.vector.quantize_mx(out=b_codes[w][:].bitcast(FP8X4), scales=b_scales[w][:], in_=b_both[:].rearrange("p c j -> p (c j)"))
 
         def x_turn(g, lo, hi):
             words = x_raw[g, lo, hi][:].bitcast(F32)
@@ -269,8 +279,7 @@ def tile_autonomyofexpertsnormgate_x1_kernel(tc, x, wdown, rgain, wup, wp, out_0
         quant(("wd", 0))
         x_turn(*x_parts[2])
         warm_up(2)
-        quant(("x", 0), 0, P)
-        quant(("x", 0), P, 2 * P)
+        quant(("x", 0), 0, 2 * P)
         lay_vector(("wd", 1), NEXT_SHARE, (NEXT_SHARE + P) // 2)
         quant(("x", 0), 2 * P, 4 * P)
         lay_vector(("wd", 1), (NEXT_SHARE + P) // 2, P)
@@ -282,9 +291,8 @@ def tile_autonomyofexpertsnormgate_x1_kernel(tc, x, wdown, rgain, wup, wp, out_0
         def two_by_two(first, h):
             return [(e, 1, 2 * h + s) for e in (first, first + 1) for s in range(2)]
 
-        cycles = [four(0), four(1), two_by_two(0, 0), four(2), four(3), two_by_two(0, 1), two_by_two(2, 0), two_by_two(2, 1)]
+        cycles = [four(0), four(1), two_by_two(0, 0), four(2), four(3), two_by_two(2, 0), two_by_two(0, 1), two_by_two(2, 1)]
         units = [unit for cycle in cycles for unit in cycle]
-        steps = [(0, 0), (1, 0), (2, 0), (0, 1), (3, 0), (1, 1), (2, 1), (3, 1)]
 
         def squares(e, g):
             return [lambda t=t: square_tile(e, g, t) for t in range(PACK)]
@@ -336,9 +344,12 @@ def tile_autonomyofexpertsnormgate_x1_kernel(tc, x, wdown, rgain, wup, wp, out_0
                     quant(("wd", 1))
                     lay_gpsimd(own[0], 0, P)
             if w < E - 1:
-                for n in [own[w]] + [("b%d" % e, g) for e, g in steps[2 * w:2 * w + 2]] + [shared[w]]:
-                    quant(n)
-                    beside()
+                quant(own[w])
+                beside()
+                quant_b(w)
+                beside(2)
+                quant(shared[w])
+                beside()
 
         fill = [(own[-1],), (("b2", 1),)] + [(n, lo, lo + 2 * P) for n in (("b3", 1), alone, shared[-1]) for lo in (0, 2 * P)]
         chain = [
@@ -361,8 +372,8 @@ def tile_autonomyofexpertsnormgate_x1_kernel(tc, x, wdown, rgain, wup, wp, out_0
 
         late = [("wp", 2), ("wp", 3)]
         ahead = units[SILU_LEAD:]
-        turns = [{0: (0,), 1: (1,), 5: (2, 3)}, {1: (0, 1), 5: (2, 3)}, {0: (0,), 1: (1,), 4: (2,), 5: (3,)}][0]
-        spent = dict(enumerate([1, 1, 0, 0, 0, 1]))
+        turns = {0: (0,), 1: (1,), 5: (2, 3)}
+        spent = dict(enumerate([1, 1, 0, 0, 0, 0]))
         for c, cycle in enumerate(cycles):
             for k, (e, g, t) in enumerate(cycle):
                 if k == 0 and c < len(late):
@@ -378,8 +389,8 @@ def tile_autonomyofexpertsnormgate_x1_kernel(tc, x, wdown, rgain, wup, wp, out_0
                         sum_back()
                 if ahead and k >= spent.get(c, 0):
                     silu_tile(*ahead.pop(0))
-                if c == len(cycles) - 1 and k % 2:
-                    dst, rows = o_views(0, P * (k - 1), P * (k + 1))
+                if c == len(cycles) - 1 and k == 1:
+                    dst, rows = o_views(0, 0, F)
                     nc.scalar.copy(out=dst, in_=rows)
             if c < len(late):
                 quant(late[c])
@@ -393,29 +404,26 @@ def tile_autonomyofexpertsnormgate_x1_kernel(tc, x, wdown, rgain, wup, wp, out_0
             if c == 4:
                 add(nc.gpsimd, flat(res[0][:, 2:4, :])[:, A_CUT:], flat(running[:])[:, A_CUT:], flat(terms[3, 0][:, 2:4, :])[:, A_CUT:])
             if c == 5:
-                add_term(nc.vector, 1, 1, slice(2 * F, 2 * F + D_CUT))
                 add(nc.vector, flat(res[0][:, 2:4, :])[:, :A_CUT], flat(running[:])[:, :A_CUT], flat(terms[3, 0][:, 2:4, :])[:, :A_CUT])
-                add(nc.gpsimd, flat(running[:])[:, D_CUT:], flat(res[1][:, 2:4, :])[:, D_CUT:], flat(terms[1, 1][:, 2:4, :])[:, D_CUT:])
                 store_pair(0, 1)
-            if c == 6:
                 add_term(nc.vector, 2, 1, slice(0, 2 * F))
                 add_term(nc.gpsimd, 3, 1, slice(0, G_SUM))
-        halves = (slice(0, F // 2), slice(F // 2, F))
-        last_pair = flat(res[1][:, 2:4, :])
-        add(nc.vector, last_pair[:, :D_CUT], last_pair[:, :D_CUT], flat(terms[2, 1][:, 2:4, :])[:, :D_CUT])
-        add(nc.vector, last_pair[:, D_CUT:], flat(running[:])[:, D_CUT:], flat(terms[2, 1][:, 2:4, :])[:, D_CUT:])
-        add_term(nc.vector, 3, 1, slice(G_SUM, 2 * F))
-        store_pair(1, 0)
-        for e in (3,):
-            for cs in halves:
-                nc.vector.tensor_tensor(out=res[1][:, 2:4, cs], in0=res[1][:, 2:4, cs], in1=terms[e, 1][:, 2:4, cs], op=ALU.add)
-                if e == 3:
-                    nc.sync.dma_start(out=tokens(out_0, 1)[:, 2:4, cs], in_=res[1][:, 2:4, cs])
-                if (e, cs.start) == (3, 0):
-                    dst, rows = o_views(1, cs.start, cs.stop)
-                    nc.scalar.copy(out=dst, in_=rows)
+            if c == 6:
+                add_term(nc.vector, 3, 1, slice(G_SUM, 2 * F))
+                store_pair(1, 0)
+                add(nc.vector, res[1][:, 2:4, :D_CUT], res[1][:, 2:4, :D_CUT], terms[1, 1][:, 2:4, :D_CUT])
+                add(nc.gpsimd, terms[3, 1][:, 0:2, D_CUT:], res[1][:, 2:4, D_CUT:], terms[1, 1][:, 2:4, D_CUT:])
+        halves = (slice(F // 2, F), slice(0, F // 2))
+        add(nc.vector, res[1][:, 2:4, D_CUT:], terms[3, 1][:, 0:2, D_CUT:], terms[2, 1][:, 2:4, D_CUT:])
+        add(nc.vector, res[1][:, 2:4, :D_CUT], res[1][:, 2:4, :D_CUT], terms[2, 1][:, 2:4, :D_CUT])
+        for cs in halves:
+            add(nc.vector, res[1][:, 2:4, cs], res[1][:, 2:4, cs], terms[3, 1][:, 2:4, cs])
+            nc.sync.dma_start(out=tokens(out_0, 1)[:, 2:4, cs], in_=res[1][:, 2:4, cs])
+            if cs == halves[0]:
+                dst, rows = o_views(1, cs.start, cs.stop)
+                nc.scalar.copy(out=dst, in_=rows)
         o_quant(0, 0, F)
-        dst, rows = o_views(1, F // 2, F)
+        dst, rows = o_views(1, halves[1].start, halves[1].stop)
         nc.vector.tensor_copy(out=dst, in_=rows)
         for cs in halves:
             o_quant(1, cs.start, cs.stop)

@@ -47,7 +47,6 @@ def tile_autonomyofexpertsnormgate_x1_kernel(tc, x, wdown, rgain, wup, wp, out_0
         ident = keep.tile([P, P], F32, name="ident")
         ident_b = keep.tile([P, P], BF16, name="ident_b")
         warm = keep.tile([P, 1], F32, name="warm")
-        zeros = keep.tile([P, 512], BF16, name="zeros")
         x_parts = [(0, 0, 1), (0, 1, 2), (0, 2, 4), (1, 0, 2), (1, 2, 4)]
         x_raw = {part: keep.tile([P, (part[2] - part[1]) * D], BF16, name="x_raw%d%d%d" % part, align_bytes=64) for part in x_parts}
         load_order = [("wd", 0), ("wd", 1), ("wd", 2), ("wu", 0), ("wd", 3), ("wp", 0), ("wu", 1), ("wp", 1), ("wu", 2), ("wu", 3), ("wp", 2), ("wp", 3)]
@@ -99,7 +98,6 @@ def tile_autonomyofexpertsnormgate_x1_kernel(tc, x, wdown, rgain, wup, wp, out_0
             load_w(n)
 
         nc.vector.memset(warm[:], 0.0)
-        nc.vector.memset(zeros[:], 0.0)
         nc.scalar.activation(out=warm[:], in_=warm[:], func=ACT.Sqrt)
         make_identity(nc, ident[:])
         nc.scalar.copy(out=ident_b[:], in_=ident[:])
@@ -168,11 +166,6 @@ def tile_autonomyofexpertsnormgate_x1_kernel(tc, x, wdown, rgain, wup, wp, out_0
                 nc.vector.tensor_copy(out=dstw[:, lo:hi], in_=view.rearrange("p s u r -> p s r u"))
             else:
                 nc.scalar.copy(out=dstw[:, lo:hi], in_=view.rearrange("p s u r -> p s r u"))
-
-        def warm_up(count):
-            bank = psum.tile([P, 512], F32, name="pz", **bank_of("v"))
-            for i in range(count):
-                nc.tensor.matmul(out=bank[:], lhsT=zeros[:, 0:P], rhs=zeros[:], start=True, stop=True)
 
         def b_tile(e, g, t, stage):
             ranks = psum.tile([P, 512], F32, name="pa", **bank_of("v"))
@@ -271,14 +264,12 @@ def tile_autonomyofexpertsnormgate_x1_kernel(tc, x, wdown, rgain, wup, wp, out_0
                 nc.sync.dma_start(out=out_2[:, 4 * q:4 * q + 4, :].bitcast(I32), in_=osc[32 * q:32 * q + 4 * G, :].bitcast(I32))
 
         staged["x", 0], staged["x", 1], staged["wd", 0], staged["wd", 1] = xg[0], xg[1], w_stage[2], w_stage[0]
-        warm_up(4)
         lay_scalar(("wd", 0), 0, HEAD_SHARE)
         lay_vector(("wd", 0), HEAD_SHARE, P)
         x_turn(*x_parts[0])
         x_turn(*x_parts[1])
         quant(("wd", 0))
         x_turn(*x_parts[2])
-        warm_up(2)
         quant(("x", 0), 0, 2 * P)
         lay_vector(("wd", 1), NEXT_SHARE, (NEXT_SHARE + P) // 2)
         quant(("x", 0), 2 * P, 4 * P)

@@ -122,12 +122,24 @@ def tile_autonomyofexpertsnormgate_x1_kernel(tc, x, wdown, rgain, wup, wp, out_0
         whole = slice(0, 512)
 
         def lay_views(n, lo, hi):
-            dst = staged[n][:].rearrange("p (q m) j -> p q m j", q=4)
-            rows = raw[n][:].rearrange("p j (m q) -> p q m j" if n[0] == "wd" else "p j (q m) -> p q m j", q=4)
-            return dst[:, :, lo:hi, :], rows[:, :, lo:hi, :]
+            if n[0] == "wd":
+                dst = staged[n][:].rearrange("p (q m) j -> p q m j", q=4)
+                rows = raw[n][:].rearrange("p j (m q) -> p q m j", q=4)
+                return dst[:, :, lo:hi, :], rows[:, :, lo:hi, :]
+            return (staged[n][:, 4 * lo:4 * hi, :].rearrange("p (q m) j -> p q m j", q=4),
+                    raw[n][:, :, 4 * lo:4 * hi].rearrange("p j (q m) -> p q m j", q=4))
+
+        def run_views(n, lo, hi):
+            if n[0] == "wd":
+                dst = staged[n][:].rearrange("p (q m) j -> p m j q", q=4)
+                rows = raw[n][:].rearrange("p j (m q) -> p m j q", q=4)
+            else:
+                dst = staged[n][:].rearrange("p (m q) j -> p m j q", q=4)
+                rows = raw[n][:].rearrange("p j (m q) -> p m j q", q=4)
+            return dst[:, lo:hi], rows[:, lo:hi]
 
         def lay_gpsimd(n, lo, hi):
-            dst, rows = lay_views(n, lo, hi)
+            dst, rows = run_views(n, lo, hi)
             nc.gpsimd.tensor_scalar(out=dst, in0=rows, scalar1=1.0, scalar2=0.0, op0=ALU.mult, op1=ALU.add)
 
         def lay_tensor(n, lo, hi):
@@ -140,11 +152,11 @@ def tile_autonomyofexpertsnormgate_x1_kernel(tc, x, wdown, rgain, wup, wp, out_0
             nc.scalar.copy(out=dst, in_=bank[:])
 
         def lay_scalar(n, lo, hi):
-            dst, rows = lay_views(n, lo, hi)
+            dst, rows = run_views(n, lo, hi)
             nc.scalar.copy(out=dst, in_=rows)
 
         def lay_vector(n, lo, hi):
-            dst, rows = lay_views(n, lo, hi)
+            dst, rows = run_views(n, lo, hi)
             nc.vector.tensor_copy(out=dst, in_=rows)
 
         def quant(n, lo=0, hi=512):
@@ -252,7 +264,8 @@ def tile_autonomyofexpertsnormgate_x1_kernel(tc, x, wdown, rgain, wup, wp, out_0
         osc = keep.tile([P, F], U8, name="osc", align_bytes=64)
 
         def o_views(g, lo, hi):
-            return og[g][:, lo:hi, :], res[g][:].rearrange("p t f -> p f t")[:, lo:hi, :]
+            return (og[g][:, lo:hi, :].rearrange("p (m q) t -> p m t q", q=4),
+                    res[g][:, :, lo:hi].rearrange("p t (m q) -> p m t q", q=4))
 
         def o_quant(g, lo, hi):
             nc.vector.quantize_mx(out=oc[g][:, lo:hi].bitcast(FP8X4), scales=osc[4 * g:P, lo:hi],

@@ -21,16 +21,18 @@ PACK = 4
 GROUP = 512
 G = T // GROUP
 BANK = 2048
-WEIGHT_BYTES = PACK * 512 * 2
-HEAD_SHARE = 40
-NEXT_SHARE = 40
-G_SHARE = 72
-G_SHARE_GATE = 48
-G_SHARE_LATE = 80
-SILU_LEAD = int(7)
-A_CUT = 384
-D_CUT = 128
-G_SUM = 832
+SLOT = PACK * 512 * 2
+RUNS = 128
+FIRST_SCALAR = 40
+SECOND_SCALAR = 48
+EARLY_GPSIMD = 16
+SHARED_GPSIMD = 88
+GATE_GPSIMD = 64
+LATE_GPSIMD = 100
+SILU_LEAD = 7
+CUT_A = 384
+CUT_B = 832
+CUT_C = 128
 GAIN_PITCH = 16
 
 
@@ -39,7 +41,7 @@ def tile_autonomyofexpertsnormgate_x1_kernel(tc, x, wdown, rgain, wup, wp, out_0
 
     with ExitStack() as ctx:
         keep = ctx.enter_context(tc.tile_pool(name="keep", bufs=1))
-        loads = ctx.enter_context(tc.tile_pool(name="loads", bufs=1))
+        slots = ctx.enter_context(tc.tile_pool(name="slots", bufs=1))
         work = ctx.enter_context(tc.tile_pool(name="work", bufs=2))
         psum = ctx.enter_context(tc.psum_pool(name="psum", bufs=4))
         ctx.enter_context(tc.manual_schedule())
@@ -49,19 +51,18 @@ def tile_autonomyofexpertsnormgate_x1_kernel(tc, x, wdown, rgain, wup, wp, out_0
         warm = keep.tile([P, 1], F32, name="warm")
         x_parts = [(0, 0, 1), (0, 1, 2), (0, 2, 4), (1, 0, 2), (1, 2, 4)]
         x_raw = {part: keep.tile([P, (part[2] - part[1]) * D], BF16, name="x_raw%d%d%d" % part, align_bytes=64) for part in x_parts}
-        load_order = [("wd", 0), ("wd", 1), ("wd", 2), ("wu", 0), ("wd", 3), ("wp", 0), ("wu", 1), ("wp", 1), ("wu", 2), ("wu", 3), ("wp", 2), ("wp", 3)]
+        weights = [("wd", 0), ("wd", 1), ("wd", 2), ("wu", 0), ("wd", 3), ("wu", 3), ("wp", 0), ("wu", 1), ("wp", 1), ("wu", 2), ("wp", 2), ("wp", 3)]
         src = {}
         for e in range(E):
             src["wd", e], src["wp", e], src["wu", e] = wdown[e], wp[e], wup[e]
-        raw = {n: loads.tile([P, PACK, 512], BF16, name="raw_%s%d" % n, offset=WEIGHT_BYTES * i) for i, n in enumerate(load_order)}
-        stage_at = [WEIGHT_BYTES * (len(load_order) + i) for i in range(4)]
-        w_stage = [loads.tile([P, 512, PACK], BF16, name="w_stage%d" % i, align_bytes=64, offset=stage_at[i]) for i in range(4)]
+        raw = {n: slots.tile([P, PACK, 512], BF16, name="raw_%s%d" % n, offset=SLOT * i) for i, n in enumerate(weights)}
+        stage_at = [SLOT * (len(weights) + i) for i in range(4)]
+        stage = [slots.tile([P, 512, PACK], BF16, name="stage%d" % i, align_bytes=64, offset=at) for i, at in enumerate(stage_at)]
         b_both = keep.tile([P, 2 * 512, PACK], BF16, name="b_both", align_bytes=64)
         b_stage = [b_both[:, 512 * s:512 * (s + 1), :] for s in range(2)]
-        xg = [b_stage[1], w_stage[1]]
         staged = {}
         codes, scales = {}, {}
-        for n in load_order + [("x", g) for g in range(G)]:
+        for n in weights + [("x", g) for g in range(G)]:
             codes[n] = keep.tile([P, 512], U32, name="codes_%s%d" % n, align_bytes=64)
             scales[n] = keep.tile([P, 512], U8, name="scales_%s%d" % n, align_bytes=64)
         steps = [(0, 0), (1, 0), (2, 0), (0, 1), (3, 0), (1, 1), (2, 1), (3, 1)]
@@ -70,8 +71,7 @@ def tile_autonomyofexpertsnormgate_x1_kernel(tc, x, wdown, rgain, wup, wp, out_0
         for i, (e, g) in enumerate(steps):
             half = slice(512 * (i % 2), 512 * (i % 2 + 1))
             codes["b%d" % e, g], scales["b%d" % e, g] = b_codes[i // 2][:, half], b_scales[i // 2][:, half]
-        squared_at = stage_at[-1] + WEIGHT_BYTES
-        squared = loads.tile([P, G * PACK * E, R], BF16, name="squared", offset=squared_at)
+        squared = keep.tile([P, 2 * PACK, R], BF16, name="squared")
         sumsq = keep.tile([P, G * PACK, E], F32, name="sumsq")
         gate = keep.tile([P, G * PACK, E], F32, name="gate")
         res = [keep.tile([P, PACK, F], F32, name="res%d" % g) for g in range(G)]
@@ -85,16 +85,16 @@ def tile_autonomyofexpertsnormgate_x1_kernel(tc, x, wdown, rgain, wup, wp, out_0
         def load_w(n):
             nc.sync.dma_start(out=raw[n][:], in_=src[n].rearrange("(p j) c -> p j c", j=PACK))
 
-        load_w(load_order[0])
+        load_w(weights[0])
         load_x(*x_parts[0])
         load_x(*x_parts[1])
+        load_w(weights[1])
         nc.sync.dma_start(out=gain[:, :, 0:PACK], in_=rgain.rearrange("e (p j) -> p e j", j=PACK))
         load_x(*x_parts[2])
-        for n in load_order[1:4]:
-            load_w(n)
+        load_w(weights[2])
         load_x(*x_parts[3])
         load_x(*x_parts[4])
-        for n in load_order[4:]:
+        for n in weights[3:]:
             load_w(n)
 
         nc.vector.memset(warm[:], 0.0)
@@ -121,35 +121,13 @@ def tile_autonomyofexpertsnormgate_x1_kernel(tc, x, wdown, rgain, wup, wp, out_0
 
         whole = slice(0, 512)
 
-        def lay_views(n, lo, hi):
-            if n[0] == "wd":
-                dst = staged[n][:].rearrange("p (q m) j -> p q m j", q=4)
-                rows = raw[n][:].rearrange("p j (m q) -> p q m j", q=4)
-                return dst[:, :, lo:hi, :], rows[:, :, lo:hi, :]
-            return (staged[n][:, 4 * lo:4 * hi, :].rearrange("p (q m) j -> p q m j", q=4),
-                    raw[n][:, :, 4 * lo:4 * hi].rearrange("p j (q m) -> p q m j", q=4))
-
         def run_views(n, lo, hi):
-            if n[0] == "wd":
-                dst = staged[n][:].rearrange("p (q m) j -> p m j q", q=4)
-                rows = raw[n][:].rearrange("p j (m q) -> p m j q", q=4)
-            else:
-                dst = staged[n][:].rearrange("p (m q) j -> p m j q", q=4)
-                rows = raw[n][:].rearrange("p j (m q) -> p m j q", q=4)
-            return dst[:, lo:hi], rows[:, lo:hi]
+            dst = staged[n][:].rearrange("p (q m) j -> p m j q" if n[0] == "wd" else "p (m q) j -> p m j q", q=4)
+            return dst[:, lo:hi], raw[n][:].rearrange("p j (m q) -> p m j q", q=4)[:, lo:hi]
 
         def lay_gpsimd(n, lo, hi):
             dst, rows = run_views(n, lo, hi)
             nc.gpsimd.tensor_scalar(out=dst, in0=rows, scalar1=1.0, scalar2=0.0, op0=ALU.mult, op1=ALU.add)
-
-        def lay_tensor(n, lo, hi):
-            bank = psum.tile([P, 4, hi - lo, PACK], BF16, name="pw", **bank_of("s"))
-            dst, rows = lay_views(n, lo, hi)
-            order = "p q m j -> p j m q" if n[0] == "wd" else "p q m j -> p j q m"
-            for u in range(2):
-                nc.tensor.matmul(out=bank[:, :, :, 2 * u:2 * u + 2].rearrange(order), lhsT=ident_b[:],
-                                 rhs=rows[:, :, :, 2 * u:2 * u + 2].rearrange(order), start=True, stop=True)
-            nc.scalar.copy(out=dst, in_=bank[:])
 
         def lay_scalar(n, lo, hi):
             dst, rows = run_views(n, lo, hi)
@@ -158,6 +136,13 @@ def tile_autonomyofexpertsnormgate_x1_kernel(tc, x, wdown, rgain, wup, wp, out_0
         def lay_vector(n, lo, hi):
             dst, rows = run_views(n, lo, hi)
             nc.vector.tensor_copy(out=dst, in_=rows)
+
+        def lay_tensor(n, lo, hi):
+            bank = psum.tile([P, 4 * (hi - lo), PACK], BF16, name="pw", **bank_of("s"))
+            for u in range(2):
+                nc.tensor.matmul(out=bank[:, :, 2 * u:2 * u + 2].rearrange("p c j -> p j c"), lhsT=ident_b[:],
+                                 rhs=raw[n][:, 2 * u:2 * u + 2, 4 * lo:4 * hi], start=True, stop=True)
+            nc.scalar.copy(out=staged[n][:, 4 * lo:4 * hi, :], in_=bank[:])
 
         def quant(n, lo=0, hi=512):
             nc.vector.quantize_mx(out=codes[n][:, lo:hi].bitcast(FP8X4), scales=scales[n][:, lo:hi],
@@ -168,29 +153,27 @@ def tile_autonomyofexpertsnormgate_x1_kernel(tc, x, wdown, rgain, wup, wp, out_0
 
         def x_turn(g, lo, hi):
             words = x_raw[g, lo, hi][:].bitcast(F32)
-            dstw = xg[g][:].rearrange("p c j -> p (c j)").bitcast(F32).rearrange("p (s r u) -> p s r u", r=P, u=2)
+            dstw = staged["x", g][:].rearrange("p c j -> p (c j)").bitcast(F32).rearrange("p (s r u) -> p s r u", r=P, u=2)
             bank = psum.tile([P, (hi - lo) * 256], F32, name="pt", **bank_of("s"))
             view = bank[:].rearrange("p (s u r) -> p s u r", r=P, u=2)
             for s in range(hi - lo):
                 for u in range(2):
                     nc.tensor.transpose(view[:, s, u, :], words[:, 256 * s + u:256 * (s + 1):2], ident[:])
-            if g == 1 and lo // 2 < 0:
-                nc.vector.tensor_copy(out=dstw[:, lo:hi], in_=view.rearrange("p s u r -> p s r u"))
-            else:
-                nc.scalar.copy(out=dstw[:, lo:hi], in_=view.rearrange("p s u r -> p s r u"))
+            nc.scalar.copy(out=dstw[:, lo:hi], in_=view.rearrange("p s u r -> p s r u"))
 
-        def b_tile(e, g, t, stage):
+        def b_tile(e, g, t, into):
             ranks = psum.tile([P, 512], F32, name="pa", **bank_of("v"))
             for k in range(PACK):
                 mx(ranks[:, cols(k)], ("wd", e), cols(k), ("x", g), cols(t))
-            staged["b%d" % e, g] = stage
-            nc.vector.tensor_tensor(out=stage[:, cols(t), :], in0=ranks[:].rearrange("p (k n) -> p n k", k=PACK),
+            staged["b%d" % e, g] = into
+            nc.vector.tensor_tensor(out=into[:, cols(t), :], in0=ranks[:].rearrange("p (k n) -> p n k", k=PACK),
                                     in1=gain[:, e, 0:PACK].unsqueeze(1).to_broadcast([P, P, PACK]), op=ALU.mult)
 
         def square_tile(e, g, t):
             toks = psum.tile([P, 512], F32, name="pb", **bank_of("s"))
             mx(toks[:], ("x", g), cols(t), ("wd", e), whole)
-            nc.scalar.activation(out=squared[:, E * (PACK * g + t) + e, :], in_=toks[:], func=ACT.Square, accum_out=sumsq[:, PACK * g + t, e:e + 1])
+            nc.scalar.activation(out=squared[:, PACK * (e % 2) + t, :], in_=toks[:], func=ACT.Square,
+                                 accum_out=sumsq[:, PACK * g + t, e:e + 1])
 
         score, z, sz, rest, quot, ex = (keep.tile([P, G * PACK, E], F32, name=name)
                                         for name in ("score", "z", "sz", "rest", "quot", "ex"))
@@ -199,65 +182,75 @@ def tile_autonomyofexpertsnormgate_x1_kernel(tc, x, wdown, rgain, wup, wp, out_0
         def over_experts(tile):
             return tile[:].to_broadcast([P, G * PACK, E])
 
-        acts = {}
+        cycles = [[(0, 0), (0, 1)], [(1, 0), (1, 1)], [(0, 2), (1, 2)], [(2, 0), (2, 1)], [(3, 0), (3, 1)], [(2, 2), (3, 2)], [(0, 3), (1, 3)], [(2, 3), (3, 3)]]
+        units = [(e, pair, s) for cycle in cycles for e, pair in cycle for s in range(2)]
+        acts, lins, terms = {}, {}, {}
 
-        def silu_tile(e, g, t):
+        def place(pair, s):
+            return pair // 2, 2 * (pair % 2) + s
+
+        def silu_tile(e, pair, s):
+            g, t = place(pair, s)
             up = psum.tile([P, 512], F32, name="pu", **bank_of("s"))
             mx(up[:], ("b%d" % e, g), cols(t), ("wu", e), whole)
-            acts[e, g, t] = work.tile([P, F], F32, name="act", bufs=SILU_LEAD + 3)
-            nc.scalar.activation(out=acts[e, g, t][:], in_=up[:], func=ACT.Silu)
+            acts[e, pair, s] = work.tile([P, F], F32, name="act", bufs=SILU_LEAD + 3)
+            nc.scalar.activation(out=acts[e, pair, s][:], in_=up[:], func=ACT.Silu)
 
-        terms = {}
+        def linear_pass(e, pair, s):
+            g, t = place(pair, s)
+            lins[e, pair, s] = psum.tile([P, 512], F32, name="pp", **bank_of("v"))
+            mx(lins[e, pair, s][:], ("x", g), cols(t), ("wp", e), whole)
 
-        def term_of(e, g, t):
-            if e == 0 and (g, t // 2) != (0, 0):
-                return res[g][:, t, :]
-            if (e, g) not in terms:
-                at = 2 * (len(terms) % 5)
-                terms[e, g] = loads.tile([P, PACK, F], F32, name="term%d%d" % (e, g), offset=squared_at + WEIGHT_BYTES * at)
-            return terms[e, g][:, t, :]
+        TURNED = 0
 
-        def product_tile(e, g, t):
-            lin = psum.tile([P, 512], F32, name="pp", **bank_of("v"))
-            mx(lin[:], ("x", g), cols(t), ("wp", e), whole)
-            nc.vector.scalar_tensor_tensor(out=term_of(e, g, t), in0=lin[:], scalar=gate[:, PACK * g + t, e:e + 1],
-                                           in1=acts[e, g, t][:], op0=ALU.mult, op1=ALU.mult)
+        def pair_res(pair):
+            return res[pair // 2][:, 2 * (pair % 2):2 * (pair % 2) + 2, :]
+
+        def term_of(e, pair):
+            if e == 0 and pair != TURNED:
+                return pair_res(pair)
+            if (e, pair) not in terms:
+                terms[e, pair] = slots.tile([P, 2, F], F32, name="term%d%d" % (e, pair), offset=SLOT * (len(terms) % len(weights)))
+            return terms[e, pair][:]
+
+        def product(e, pair, s):
+            g, t = place(pair, s)
+            nc.vector.scalar_tensor_tensor(out=term_of(e, pair)[:, s, :], in0=lins[e, pair, s][:], scalar=gate[:, PACK * g + t, e:e + 1],
+                                           in1=acts[e, pair, s][:], op0=ALU.mult, op1=ALU.mult)
 
         def flat(ap):
             return ap.rearrange("p t f -> p (t f)")
 
-        def add_term(engine, e, g, span):
-            dst = flat(res[g][:])[:, span]
-            engine.tensor_tensor(out=dst, in0=dst, in1=flat(terms[e, g][:])[:, span], op=ALU.add)
+        def add_term(engine, e, pair, span=slice(0, 2 * F)):
+            dst = flat(pair_res(pair))[:, span]
+            engine.tensor_tensor(out=dst, in0=dst, in1=flat(terms[e, pair][:])[:, span], op=ALU.add)
 
-        def add(engine, out, left, right):
-            engine.tensor_tensor(out=out, in0=left, in1=right, op=ALU.add)
-
-        def store_pair(g, h):
-            nc.sync.dma_start(out=tokens(out_0, g)[:, 2 * h:2 * h + 2, :], in_=res[g][:, 2 * h:2 * h + 2, :])
+        def store_pair(pair, cs=slice(0, F)):
+            h = pair % 2
+            nc.sync.dma_start(out=tokens(out_0, pair // 2)[:, 2 * h:2 * h + 2, cs], in_=pair_res(pair)[:, :, cs])
 
         turned = keep.tile([P, 2, F], F32, name="turned")
         sums, held = {}, {}
 
         def sum_turn(e):
-            for t in range(2):
+            for s in range(2):
                 if e == 0:
-                    held[t] = banks["vs"[t]].pop(0)
-                    sums[t] = psum.tile([P, F], F32, name="psum_sum", **bank_at(held[t]))
+                    held[s] = banks["vs"[s]].pop(0)
+                    sums[s] = psum.tile([P, F], F32, name="psum_sum", **bank_at(held[s]))
                 for c in range(4):
-                    nc.tensor.matmul(out=sums[t][:, cols(c)], lhsT=terms[e, 0][:, t, cols(c)], rhs=ident[:], is_transpose=True,
+                    nc.tensor.matmul(out=sums[s][:, cols(c)], lhsT=terms[e, TURNED][:, s, cols(c)], rhs=ident[:], is_transpose=True,
                                      start=(e, c) == (0, 0), stop=(e, c) == (E - 1, 3))
             if e == E - 1:
-                for t in range(2):
-                    nc.scalar.copy(out=turned[:, t, :], in_=sums[t][:])
+                for s in range(2):
+                    nc.scalar.copy(out=turned[:, s, :], in_=sums[s][:])
 
         def sum_back():
-            for t in range(2):
-                back = psum.tile([P, F], F32, name="psum_back", **bank_at(held[t]))
+            for s in range(2):
+                back = psum.tile([P, F], F32, name="psum_back", **bank_at(held[s]))
                 for c in range(4):
-                    nc.tensor.transpose(back[:, cols(c)], turned[:, t, cols(c)], ident[:])
-                nc.scalar.copy(out=res[0][:, t, :], in_=back[:])
-            store_pair(0, 0)
+                    nc.tensor.transpose(back[:, cols(c)], turned[:, s, cols(c)], ident[:])
+                nc.scalar.copy(out=pair_res(TURNED)[:, s, :], in_=back[:])
+            store_pair(TURNED)
 
         og = b_stage
         oc = [keep.tile([P, F], U32, name="oc%d" % g, align_bytes=64) for g in range(G)]
@@ -276,77 +269,66 @@ def tile_autonomyofexpertsnormgate_x1_kernel(tc, x, wdown, rgain, wup, wp, out_0
             for q in range(4):
                 nc.sync.dma_start(out=out_2[:, 4 * q:4 * q + 4, :].bitcast(I32), in_=osc[32 * q:32 * q + 4 * G, :].bitcast(I32))
 
-        staged["x", 0], staged["x", 1], staged["wd", 0], staged["wd", 1] = xg[0], xg[1], w_stage[2], w_stage[0]
-        lay_scalar(("wd", 0), 0, HEAD_SHARE)
-        lay_vector(("wd", 0), HEAD_SHARE, P)
+        staged["x", 0], staged["x", 1], staged["wd", 0], staged["wd", 1] = stage[3], stage[1], stage[2], stage[0]
+        lay_scalar(("wd", 0), 0, FIRST_SCALAR)
+        lay_vector(("wd", 0), FIRST_SCALAR, RUNS)
         x_turn(*x_parts[0])
         x_turn(*x_parts[1])
         quant(("wd", 0))
-        x_turn(*x_parts[2])
-        quant(("x", 0), 0, 2 * P)
-        lay_vector(("wd", 1), NEXT_SHARE, (NEXT_SHARE + P) // 2)
-        quant(("x", 0), 2 * P, 4 * P)
-        lay_vector(("wd", 1), (NEXT_SHARE + P) // 2, P)
-        lay_scalar(("wd", 1), 0, NEXT_SHARE)
+        quant(("x", 0), 0, P)
+        quant(("x", 0), P, 2 * P)
+        lay_scalar(("wd", 1), 0, SECOND_SCALAR)
+        lay_vector(("wd", 1), SECOND_SCALAR, RUNS)
 
-        def four(e):
-            return [(e, 0, t) for t in range(PACK)]
-
-        def two_by_two(first, h):
-            return [(e, 1, 2 * h + s) for e in (first, first + 1) for s in range(2)]
-
-        cycles = [four(0), four(1), two_by_two(0, 0), four(2), four(3), two_by_two(2, 0), two_by_two(0, 1), two_by_two(2, 1)]
-        units = [unit for cycle in cycles for unit in cycle]
-
-        def squares(e, g):
-            return [lambda t=t: square_tile(e, g, t) for t in range(PACK)]
-
-        def through_tensor(n, lo):
-            mid = (lo + P) // 2
-            if lo >= P // 2:
-                return [lambda: lay_tensor(n, lo, P), None]
-            return [lambda: lay_tensor(n, lo, mid), lambda: lay_tensor(n, mid, P)]
+        own = [("wd", 2), ("wd", 3), ("wp", 0), ("wp", 1)]
+        shared = [("x", 1), ("wu", 0), ("wu", 1), ("wu", 2)]
+        for w, (mine, other) in enumerate(((3, 1), (1, 2), (2, 0), (0, 1))):
+            staged[own[w]], staged[shared[w]] = stage[mine], stage[other]
+        alone, late = ("wu", 3), [("wp", 2), ("wp", 3)]
+        staged[alone], staged[late[0]], staged[late[1]] = stage[3], stage[1], stage[1]
+        opening = [(e, 0, 2 * h + s) for h in range(2) for e in range(2) for s in range(2)]
 
         def gate_root():
             nc.scalar.activation(out=score[:], in_=sumsq[:], func=ACT.Sqrt)
 
-        own = [("wd", 2), ("wd", 3), ("wp", 0), ("wp", 1)]
-        shared = [("x", 1), ("wu", 0), ("wu", 1), ("wu", 2)]
-        for w, (mine, other) in enumerate(((0, 1), (1, 2), (2, 0), (0, 1))):
-            staged[own[w]], staged[shared[w]] = w_stage[mine], w_stage[other]
-        sq = [job for e, g in ((0, 0), (1, 0), (2, 0), (0, 1), (1, 1), (3, 0), (2, 1), (3, 1)) for job in squares(e, g)]
-        silus = [lambda i=i: silu_tile(*units[i]) for i in range(SILU_LEAD)]
-        last_share = through_tensor(shared[3], G_SHARE_GATE)
-        turn_x = [lambda: x_turn(*x_parts[3]), lambda: x_turn(*x_parts[4])]
-        alone = ("wu", 3)
-        staged[alone] = w_stage[3]
-        alone_parts = through_tensor(alone, 0)
-        jobs = (sq[0:7] + turn_x + through_tensor(shared[1], G_SHARE) + sq[7:9] + sq[9:17] + alone_parts[:1] + sq[17:20]
-                + sq[20:27] + [None] + through_tensor(shared[2], G_SHARE) + sq[27:32]
-                + last_share[:1] + [gate_root, None, None, silus[0]] + last_share[1:] + alone_parts[1:] + silus[1:])
+        def job(call, *args):
+            return lambda: call(*args)
+
+        order = opening + [(e, g, t) for e, g in ((2, 0), (0, 1), (1, 1), (3, 0), (2, 1), (3, 1)) for t in range(PACK)]
+        sq = [job(square_tile, *tile) for tile in order]
+        silus = [job(silu_tile, *unit) for unit in units[:SILU_LEAD]]
+        turn_x = [job(x_turn, *part) for part in x_parts[2:]]
+        HALF = RUNS // 2
+        jobs = ([None, turn_x[0]] + sq[0:7] + turn_x[1:] + sq[7:10]
+                + [job(lay_scalar, shared[1], EARLY_GPSIMD + SHARED_GPSIMD, RUNS)] + sq[10:17] + [job(lay_tensor, alone, 0, HALF)] + sq[17:20]
+                + sq[20:27] + [None, job(lay_tensor, shared[2], SHARED_GPSIMD, RUNS), None] + sq[27:32]
+                + [job(lay_tensor, shared[3], GATE_GPSIMD, RUNS), gate_root, None, None, silus[0], job(lay_tensor, alone, HALF, RUNS)] + silus[1:])
 
         def beside(count=1):
             for i in range(min(count, len(jobs))):
-                job = jobs.pop(0)
-                if job:
-                    job()
+                call = jobs.pop(0)
+                if call:
+                    call()
 
         for w in range(E):
             for i in range(2 * PACK):
-                s, t = divmod(i, PACK)
+                s, t = (opening[i][0], opening[i][2]) if w == 0 else divmod(i, PACK)
                 if i == 0 and w > 0:
-                    lay_gpsimd(own[w], 0, P)
-                    lay_gpsimd(shared[w], 0, G_SHARE if w < E - 1 else G_SHARE_GATE)
+                    lay_gpsimd(own[w], 0, RUNS)
+                    lay_gpsimd(shared[w], *((EARLY_GPSIMD, EARLY_GPSIMD + SHARED_GPSIMD), (0, SHARED_GPSIMD), (0, GATE_GPSIMD))[w - 1])
                 b_tile(*steps[2 * w + s], t, b_stage[s])
-                beside({(0, 7): 2}.get((w, i), 1))
+                beside({(0, 1): 3}.get((w, i), 1))
+                if (w, i) == (0, 0):
+                    quant(("wd", 1))
+                if (w, i) == (0, 1):
+                    quant(("x", 0), 2 * P, 4 * P)
+                    lay_gpsimd(own[0], 0, RUNS)
+                    lay_gpsimd(shared[1], 0, EARLY_GPSIMD)
                 if (w, i) == (E - 1, 5):
                     nc.vector.tensor_reduce(out=top[:, :, 0], in_=score[:], axis=AX.X, op=ALU.max)
                     nc.gpsimd.tensor_tensor(out=z[:], in0=score[:], in1=over_experts(top), op=ALU.subtract)
                 if (w, i) == (E - 1, 7):
                     nc.scalar.activation(out=sz[:], in_=z[:], func=ACT.Silu, bias=-1.0)
-                if (w, i) == (0, 1):
-                    quant(("wd", 1))
-                    lay_gpsimd(own[0], 0, P)
             if w < E - 1:
                 quant(own[w])
                 beside()
@@ -374,55 +356,52 @@ def tile_autonomyofexpertsnormgate_x1_kernel(tc, x, wdown, rgain, wup, wp, out_0
         while jobs:
             beside()
 
-        late = [("wp", 2), ("wp", 3)]
         ahead = units[SILU_LEAD:]
-        turns = {0: (0,), 1: (1,), 5: (2, 3)}
-        spent = dict(enumerate([1, 1, 0, 0, 0, 0]))
-        for c, cycle in enumerate(cycles):
-            for k, (e, g, t) in enumerate(cycle):
-                if k == 0 and c < len(late):
-                    staged[late[c]] = staged[shared[-1]]
-                    lay_gpsimd(late[c], 0, G_SHARE_LATE)
-                product_tile(e, g, t)
-                if k == 1 and c < len(late):
-                    lay_scalar(late[c], G_SHARE_LATE, P)
-                if k == PACK - 1:
-                    for turn in turns.get(c, ()):
-                        sum_turn(turn)
-                    if c == 6:
-                        sum_back()
-                if ahead and k >= spent.get(c, 0):
-                    silu_tile(*ahead.pop(0))
-                if c == len(cycles) - 1 and k == 1:
-                    dst, rows = o_views(0, 0, F)
-                    nc.scalar.copy(out=dst, in_=rows)
-            if c < len(late):
-                quant(late[c])
-            if c == 1:
-                running = loads.tile([P, 2, F], F32, name="running", offset=stage_at[1])
-                add(nc.gpsimd, running[:], res[0][:, 2:4, :], terms[1, 0][:, 2:4, :])
-            if c == 2:
-                add_term(nc.gpsimd, 1, 1, slice(0, 2 * F))
-            if c == 3:
-                add(nc.gpsimd, running[:], running[:], terms[2, 0][:, 2:4, :])
-            if c == 4:
-                add(nc.gpsimd, flat(res[0][:, 2:4, :])[:, A_CUT:], flat(running[:])[:, A_CUT:], flat(terms[3, 0][:, 2:4, :])[:, A_CUT:])
-            if c == 5:
-                add(nc.vector, flat(res[0][:, 2:4, :])[:, :A_CUT], flat(running[:])[:, :A_CUT], flat(terms[3, 0][:, 2:4, :])[:, :A_CUT])
-                store_pair(0, 1)
-                add_term(nc.vector, 2, 1, slice(0, 2 * F))
-                add_term(nc.gpsimd, 3, 1, slice(0, G_SUM))
-            if c == 6:
-                add_term(nc.vector, 3, 1, slice(G_SUM, 2 * F))
-                store_pair(1, 0)
-                add(nc.vector, res[1][:, 2:4, :D_CUT], res[1][:, 2:4, :D_CUT], terms[1, 1][:, 2:4, :D_CUT])
-                add(nc.gpsimd, terms[3, 1][:, 0:2, D_CUT:], res[1][:, 2:4, D_CUT:], terms[1, 1][:, 2:4, D_CUT:])
+        turns = {3: (0,), 7: (1,), 23: (2, 3)}
+        skips = (0, 4)
+        for i, unit in enumerate(units):
+            if i in (0, 4):
+                lay_gpsimd(late[i // 4], 0, LATE_GPSIMD)
+            linear_pass(*unit)
+            product(*unit)
+            if i in (1, 5):
+                lay_scalar(late[i // 4], LATE_GPSIMD, RUNS)
+            for e in turns.get(i, ()):
+                sum_turn(e)
+            if i == 27:
+                sum_back()
+            if ahead and i not in skips:
+                silu_tile(*ahead.pop(0))
+            if i == 29:
+                dst, rows = o_views(0, 0, F)
+                nc.scalar.copy(out=dst, in_=rows)
+            if i in (3, 7):
+                quant(late[i // 4])
+            if i == 7:
+                running = slots.tile([P, 2, F], F32, name="running", offset=stage_at[1])
+                nc.gpsimd.tensor_tensor(out=running[:], in0=pair_res(1), in1=terms[1, 1][:], op=ALU.add)
+            if i == 11:
+                add_term(nc.gpsimd, 1, 2)
+            if i == 15:
+                nc.gpsimd.tensor_tensor(out=running[:], in0=running[:], in1=terms[2, 1][:], op=ALU.add)
+            if i == 19:
+                nc.gpsimd.tensor_tensor(out=flat(pair_res(1))[:, CUT_A:], in0=flat(running[:])[:, CUT_A:], in1=flat(terms[3, 1][:])[:, CUT_A:], op=ALU.add)
+            if i == 23:
+                nc.vector.tensor_tensor(out=flat(pair_res(1))[:, :CUT_A], in0=flat(running[:])[:, :CUT_A], in1=flat(terms[3, 1][:])[:, :CUT_A], op=ALU.add)
+                store_pair(1)
+                add_term(nc.vector, 2, 2)
+                add_term(nc.gpsimd, 3, 2, slice(0, CUT_B))
+            if i == 27:
+                add_term(nc.vector, 3, 2, slice(CUT_B, 2 * F))
+                store_pair(2)
+                nc.vector.tensor_tensor(out=pair_res(3)[:, :, :CUT_C], in0=pair_res(3)[:, :, :CUT_C], in1=terms[1, 3][:, :, :CUT_C], op=ALU.add)
+                nc.gpsimd.tensor_tensor(out=terms[3, 2][:, :, CUT_C:], in0=pair_res(3)[:, :, CUT_C:], in1=terms[1, 3][:, :, CUT_C:], op=ALU.add)
+        nc.vector.tensor_tensor(out=pair_res(3)[:, :, CUT_C:], in0=terms[3, 2][:, :, CUT_C:], in1=terms[2, 3][:, :, CUT_C:], op=ALU.add)
+        nc.vector.tensor_tensor(out=pair_res(3)[:, :, :CUT_C], in0=pair_res(3)[:, :, :CUT_C], in1=terms[2, 3][:, :, :CUT_C], op=ALU.add)
         halves = (slice(F // 2, F), slice(0, F // 2))
-        add(nc.vector, res[1][:, 2:4, D_CUT:], terms[3, 1][:, 0:2, D_CUT:], terms[2, 1][:, 2:4, D_CUT:])
-        add(nc.vector, res[1][:, 2:4, :D_CUT], res[1][:, 2:4, :D_CUT], terms[2, 1][:, 2:4, :D_CUT])
         for cs in halves:
-            add(nc.vector, res[1][:, 2:4, cs], res[1][:, 2:4, cs], terms[3, 1][:, 2:4, cs])
-            nc.sync.dma_start(out=tokens(out_0, 1)[:, 2:4, cs], in_=res[1][:, 2:4, cs])
+            nc.vector.tensor_tensor(out=pair_res(3)[:, :, cs], in0=pair_res(3)[:, :, cs], in1=terms[3, 3][:, :, cs], op=ALU.add)
+            store_pair(3, cs)
             if cs == halves[0]:
                 dst, rows = o_views(1, cs.start, cs.stop)
                 nc.scalar.copy(out=dst, in_=rows)

@@ -26,9 +26,8 @@ RUNS = 128
 FIRST_SCALAR = 40
 SECOND_SCALAR = 48
 EARLY_GPSIMD = 16
-SHARED_GPSIMD = 88
-GATE_GPSIMD = 64
-LATE_GPSIMD = 100
+SHARES = (84, 104, 88)
+LATE_GPSIMD = 116
 SILU_LEAD = 7
 CUT_A = 384
 CUT_B = 832
@@ -101,6 +100,13 @@ def tile_autonomyofexpertsnormgate_x1_kernel(tc, x, wdown, rgain, wup, wp, out_0
         nc.scalar.activation(out=warm[:], in_=warm[:], func=ACT.Sqrt)
         make_identity(nc, ident[:])
         nc.scalar.copy(out=ident_b[:], in_=ident[:])
+        idle = psum.tile([P, P], F32, name="idle", tag="bank3", bufs=1, offset=3 * BANK)
+
+        def warm_up(count):
+            for i in range(count):
+                nc.tensor.matmul(out=idle[:], lhsT=ident[:], rhs=ident[:], start=True, stop=True)
+
+        warm_up(4)
 
         banks = {"v": [0, 1, 2, 3], "s": [4, 5, 6, 7]}
 
@@ -122,8 +128,11 @@ def tile_autonomyofexpertsnormgate_x1_kernel(tc, x, wdown, rgain, wup, wp, out_0
         whole = slice(0, 512)
 
         def run_views(n, lo, hi):
-            dst = staged[n][:].rearrange("p (q m) j -> p m j q" if n[0] == "wd" else "p (m q) j -> p m j q", q=4)
-            return dst[:, lo:hi], raw[n][:].rearrange("p j (m q) -> p m j q", q=4)[:, lo:hi]
+            if n[0] == "wd":
+                return (staged[n][:].rearrange("p (q m) j -> p m j q", q=4)[:, lo:hi],
+                        raw[n][:].rearrange("p j (m q) -> p m j q", q=4)[:, lo:hi])
+            return (staged[n][:, 4 * lo:4 * hi, :].rearrange("p (m q) j -> p m j q", q=2),
+                    raw[n][:, :, 4 * lo:4 * hi].rearrange("p j (m q) -> p m j q", q=2))
 
         def lay_gpsimd(n, lo, hi):
             dst, rows = run_views(n, lo, hi)
@@ -257,8 +266,8 @@ def tile_autonomyofexpertsnormgate_x1_kernel(tc, x, wdown, rgain, wup, wp, out_0
         osc = keep.tile([P, F], U8, name="osc", align_bytes=64)
 
         def o_views(g, lo, hi):
-            return (og[g][:, lo:hi, :].rearrange("p (m q) t -> p m t q", q=4),
-                    res[g][:, :, lo:hi].rearrange("p t (m q) -> p m t q", q=4))
+            return (og[g][:, lo:hi, :].rearrange("p (m q) t -> p m t q", q=2),
+                    res[g][:, :, lo:hi].rearrange("p t (m q) -> p m t q", q=2))
 
         def o_quant(g, lo, hi):
             nc.vector.quantize_mx(out=oc[g][:, lo:hi].bitcast(FP8X4), scales=osc[4 * g:P, lo:hi],
@@ -274,6 +283,7 @@ def tile_autonomyofexpertsnormgate_x1_kernel(tc, x, wdown, rgain, wup, wp, out_0
         lay_vector(("wd", 0), FIRST_SCALAR, RUNS)
         x_turn(*x_parts[0])
         x_turn(*x_parts[1])
+        warm_up(2)
         quant(("wd", 0))
         quant(("x", 0), 0, P)
         quant(("x", 0), P, 2 * P)
@@ -285,7 +295,8 @@ def tile_autonomyofexpertsnormgate_x1_kernel(tc, x, wdown, rgain, wup, wp, out_0
         for w, (mine, other) in enumerate(((3, 1), (1, 2), (2, 0), (0, 1))):
             staged[own[w]], staged[shared[w]] = stage[mine], stage[other]
         alone, late = ("wu", 3), [("wp", 2), ("wp", 3)]
-        staged[alone], staged[late[0]], staged[late[1]] = stage[3], stage[1], stage[1]
+        staged[alone], staged[late[0]], staged[late[1]] = stage[3], stage[3], stage[2]
+        done = {1: EARLY_GPSIMD, 2: 0, 3: 0}
         opening = [(e, 0, 2 * h + s) for h in range(2) for e in range(2) for s in range(2)]
 
         def gate_root():
@@ -299,10 +310,11 @@ def tile_autonomyofexpertsnormgate_x1_kernel(tc, x, wdown, rgain, wup, wp, out_0
         silus = [job(silu_tile, *unit) for unit in units[:SILU_LEAD]]
         turn_x = [job(x_turn, *part) for part in x_parts[2:]]
         HALF = RUNS // 2
+        rests = [job(lay_scalar, shared[w], done[w] + SHARES[w - 1], RUNS) for w in (1, 2)]
         jobs = ([None, turn_x[0]] + sq[0:7] + turn_x[1:] + sq[7:10]
-                + [job(lay_scalar, shared[1], EARLY_GPSIMD + SHARED_GPSIMD, RUNS)] + sq[10:17] + [job(lay_tensor, alone, 0, HALF)] + sq[17:20]
-                + sq[20:27] + [None, job(lay_tensor, shared[2], SHARED_GPSIMD, RUNS), None] + sq[27:32]
-                + [job(lay_tensor, shared[3], GATE_GPSIMD, RUNS), gate_root, None, None, silus[0], job(lay_tensor, alone, HALF, RUNS)] + silus[1:])
+                + sq[10:15] + rests[:1] + sq[15:17] + [job(lay_tensor, alone, 0, HALF)] + sq[17:20]
+                + sq[20:24] + rests[1:] + sq[24:27] + sq[27:29] + [None, None]
+                + sq[29:32] + [gate_root, job(lay_tensor, shared[3], SHARES[2], RUNS), silus[0], None, None, job(lay_tensor, alone, HALF, RUNS)] + silus[1:])
 
         def beside(count=1):
             for i in range(min(count, len(jobs))):
@@ -315,7 +327,7 @@ def tile_autonomyofexpertsnormgate_x1_kernel(tc, x, wdown, rgain, wup, wp, out_0
                 s, t = (opening[i][0], opening[i][2]) if w == 0 else divmod(i, PACK)
                 if i == 0 and w > 0:
                     lay_gpsimd(own[w], 0, RUNS)
-                    lay_gpsimd(shared[w], *((EARLY_GPSIMD, EARLY_GPSIMD + SHARED_GPSIMD), (0, SHARED_GPSIMD), (0, GATE_GPSIMD))[w - 1])
+                    lay_gpsimd(shared[w], done[w], done[w] + SHARES[w - 1])
                 b_tile(*steps[2 * w + s], t, b_stage[s])
                 beside({(0, 1): 3}.get((w, i), 1))
                 if (w, i) == (0, 0):
@@ -329,15 +341,20 @@ def tile_autonomyofexpertsnormgate_x1_kernel(tc, x, wdown, rgain, wup, wp, out_0
                     nc.gpsimd.tensor_tensor(out=z[:], in0=score[:], in1=over_experts(top), op=ALU.subtract)
                 if (w, i) == (E - 1, 7):
                     nc.scalar.activation(out=sz[:], in_=z[:], func=ACT.Silu, bias=-1.0)
-            if w < E - 1:
+            if w == 0:
+                for call in ((own[w],), (("b0", 0),), (("b1", 0), 0, 2 * P), (shared[w],)):
+                    quant(*call)
+                    beside()
+                quant(("b1", 0), 2 * P, 4 * P)
+            elif w < E - 1:
                 quant(own[w])
+                beside()
+                quant(shared[w])
                 beside()
                 quant_b(w)
                 beside(2)
-                quant(shared[w])
-                beside()
 
-        fill = [(own[-1],), (("b2", 1),)] + [(n, lo, lo + 2 * P) for n in (("b3", 1), alone, shared[-1]) for lo in (0, 2 * P)]
+        fill = [(own[-1],), (("b3", 1), 0, 2 * P)] + [(n, lo, lo + 2 * P) for n in (shared[-1], ("b2", 1), alone) for lo in (0, 2 * P)] + [(("b3", 1), 2 * P, 4 * P)]
         chain = [
             lambda: nc.vector.scalar_tensor_tensor(out=rest[:], in0=z[:], scalar=-1.0, in1=sz[:], op0=ALU.add, op1=ALU.subtract),
             lambda: nc.vector.reciprocal(out=quot[:], in_=rest[:]),
@@ -353,19 +370,20 @@ def tile_autonomyofexpertsnormgate_x1_kernel(tc, x, wdown, rgain, wup, wp, out_0
             link()
             quant(*call)
             beside()
+        quant(*fill[-1])
+        lay_gpsimd(late[0], 0, RUNS)
+        lay_gpsimd(late[1], 0, LATE_GPSIMD)
         while jobs:
             beside()
 
         ahead = units[SILU_LEAD:]
-        turns = {3: (0,), 7: (1,), 23: (2, 3)}
-        skips = (0, 4)
+        turns = {9: (0, 1), 23: (2, 3)}
+        skips = (9,)
         for i, unit in enumerate(units):
-            if i in (0, 4):
-                lay_gpsimd(late[i // 4], 0, LATE_GPSIMD)
             linear_pass(*unit)
             product(*unit)
-            if i in (1, 5):
-                lay_scalar(late[i // 4], LATE_GPSIMD, RUNS)
+            if i == 1:
+                lay_scalar(late[1], LATE_GPSIMD, RUNS)
             for e in turns.get(i, ()):
                 sum_turn(e)
             if i == 27:
@@ -375,10 +393,10 @@ def tile_autonomyofexpertsnormgate_x1_kernel(tc, x, wdown, rgain, wup, wp, out_0
             if i == 29:
                 dst, rows = o_views(0, 0, F)
                 nc.scalar.copy(out=dst, in_=rows)
-            if i in (3, 7):
-                quant(late[i // 4])
             if i == 7:
-                running = slots.tile([P, 2, F], F32, name="running", offset=stage_at[1])
+                quant(late[0])
+                quant(late[1])
+                running = slots.tile([P, 2, F], F32, name="running", offset=stage_at[3])
                 nc.gpsimd.tensor_tensor(out=running[:], in0=pair_res(1), in1=terms[1, 1][:], op=ALU.add)
             if i == 11:
                 add_term(nc.gpsimd, 1, 2)

@@ -25,10 +25,10 @@ SLOT = PACK * 512 * 2
 RUNS = 128
 FIRST_SCALAR = 40
 SECOND_SCALAR = 48
-EARLY_GPSIMD = 16
-SHARES = (84, 104, 88)
-LATE_GPSIMD = 116
-SILU_LEAD = 7
+WALK = 4
+SHARES = (72, 84, 72)
+LATE_GPSIMD = 88
+SILU_LEAD = 6
 CUT_A = 384
 CUT_B = 832
 CUT_C = 128
@@ -131,8 +131,8 @@ def tile_autonomyofexpertsnormgate_x1_kernel(tc, x, wdown, rgain, wup, wp, out_0
             if n[0] == "wd":
                 return (staged[n][:].rearrange("p (q m) j -> p m j q", q=4)[:, lo:hi],
                         raw[n][:].rearrange("p j (m q) -> p m j q", q=4)[:, lo:hi])
-            return (staged[n][:, 4 * lo:4 * hi, :].rearrange("p (m q) j -> p m j q", q=2),
-                    raw[n][:, :, 4 * lo:4 * hi].rearrange("p j (m q) -> p m j q", q=2))
+            return (staged[n][:, 4 * lo:4 * hi, :].rearrange("p (m q) j -> p m j q", q=WALK),
+                    raw[n][:, :, 4 * lo:4 * hi].rearrange("p j (m q) -> p m j q", q=WALK))
 
         def lay_gpsimd(n, lo, hi):
             dst, rows = run_views(n, lo, hi)
@@ -266,8 +266,8 @@ def tile_autonomyofexpertsnormgate_x1_kernel(tc, x, wdown, rgain, wup, wp, out_0
         osc = keep.tile([P, F], U8, name="osc", align_bytes=64)
 
         def o_views(g, lo, hi):
-            return (og[g][:, lo:hi, :].rearrange("p (m q) t -> p m t q", q=2),
-                    res[g][:, :, lo:hi].rearrange("p t (m q) -> p m t q", q=2))
+            return (og[g][:, lo:hi, :].rearrange("p (m q) t -> p m t q", q=4),
+                    res[g][:, :, lo:hi].rearrange("p t (m q) -> p m t q", q=4))
 
         def o_quant(g, lo, hi):
             nc.vector.quantize_mx(out=oc[g][:, lo:hi].bitcast(FP8X4), scales=osc[4 * g:P, lo:hi],
@@ -296,7 +296,6 @@ def tile_autonomyofexpertsnormgate_x1_kernel(tc, x, wdown, rgain, wup, wp, out_0
             staged[own[w]], staged[shared[w]] = stage[mine], stage[other]
         alone, late = ("wu", 3), [("wp", 2), ("wp", 3)]
         staged[alone], staged[late[0]], staged[late[1]] = stage[3], stage[3], stage[2]
-        done = {1: EARLY_GPSIMD, 2: 0, 3: 0}
         opening = [(e, 0, 2 * h + s) for h in range(2) for e in range(2) for s in range(2)]
 
         def gate_root():
@@ -310,11 +309,11 @@ def tile_autonomyofexpertsnormgate_x1_kernel(tc, x, wdown, rgain, wup, wp, out_0
         silus = [job(silu_tile, *unit) for unit in units[:SILU_LEAD]]
         turn_x = [job(x_turn, *part) for part in x_parts[2:]]
         HALF = RUNS // 2
-        rests = [job(lay_scalar, shared[w], done[w] + SHARES[w - 1], RUNS) for w in (1, 2)]
-        jobs = ([None, turn_x[0]] + sq[0:7] + turn_x[1:] + sq[7:10]
-                + sq[10:15] + rests[:1] + sq[15:17] + [job(lay_tensor, alone, 0, HALF)] + sq[17:20]
-                + sq[20:24] + rests[1:] + sq[24:27] + sq[27:29] + [None, None]
-                + sq[29:32] + [gate_root, job(lay_tensor, shared[3], SHARES[2], RUNS), silus[0], None, None, job(lay_tensor, alone, HALF, RUNS)] + silus[1:])
+        rests = [job(lay_tensor, shared[w], SHARES[w - 1], RUNS) for w in (1, 2, 3)]
+        jobs = ([None, turn_x[0]] + sq[0:7] + turn_x[1:] + sq[7:9] + rests[0:1]
+                + sq[9:17] + rests[1:2] + sq[17:20]
+                + sq[20:27] + [None, job(lay_tensor, alone, 0, HALF)] + sq[27:28] + [None, None]
+                + sq[28:32] + [gate_root, silus[0], None, None, rests[2], job(lay_tensor, alone, HALF, RUNS)] + silus[1:])
 
         def beside(count=1):
             for i in range(min(count, len(jobs))):
@@ -327,7 +326,7 @@ def tile_autonomyofexpertsnormgate_x1_kernel(tc, x, wdown, rgain, wup, wp, out_0
                 s, t = (opening[i][0], opening[i][2]) if w == 0 else divmod(i, PACK)
                 if i == 0 and w > 0:
                     lay_gpsimd(own[w], 0, RUNS)
-                    lay_gpsimd(shared[w], done[w], done[w] + SHARES[w - 1])
+                    lay_gpsimd(shared[w], 0, SHARES[w - 1])
                 b_tile(*steps[2 * w + s], t, b_stage[s])
                 beside({(0, 1): 3}.get((w, i), 1))
                 if (w, i) == (0, 0):
@@ -335,7 +334,6 @@ def tile_autonomyofexpertsnormgate_x1_kernel(tc, x, wdown, rgain, wup, wp, out_0
                 if (w, i) == (0, 1):
                     quant(("x", 0), 2 * P, 4 * P)
                     lay_gpsimd(own[0], 0, RUNS)
-                    lay_gpsimd(shared[1], 0, EARLY_GPSIMD)
                 if (w, i) == (E - 1, 5):
                     nc.vector.tensor_reduce(out=top[:, :, 0], in_=score[:], axis=AX.X, op=ALU.max)
                     nc.gpsimd.tensor_tensor(out=z[:], in0=score[:], in1=over_experts(top), op=ALU.subtract)
@@ -354,7 +352,7 @@ def tile_autonomyofexpertsnormgate_x1_kernel(tc, x, wdown, rgain, wup, wp, out_0
                 quant_b(w)
                 beside(2)
 
-        fill = [(own[-1],), (("b3", 1), 0, 2 * P)] + [(n, lo, lo + 2 * P) for n in (shared[-1], ("b2", 1), alone) for lo in (0, 2 * P)] + [(("b3", 1), 2 * P, 4 * P)]
+        fill = [(own[-1],), (("b3", 1), 0, 2 * P)] + [(n, lo, lo + 2 * P) for n in (("b2", 1), shared[-1], alone) for lo in (0, 2 * P)] + [(("b3", 1), 2 * P, 4 * P)]
         chain = [
             lambda: nc.vector.scalar_tensor_tensor(out=rest[:], in0=z[:], scalar=-1.0, in1=sz[:], op0=ALU.add, op1=ALU.subtract),
             lambda: nc.vector.reciprocal(out=quot[:], in_=rest[:]),
@@ -378,7 +376,7 @@ def tile_autonomyofexpertsnormgate_x1_kernel(tc, x, wdown, rgain, wup, wp, out_0
 
         ahead = units[SILU_LEAD:]
         turns = {9: (0, 1), 23: (2, 3)}
-        skips = (9,)
+        skips = (1,)
         for i, unit in enumerate(units):
             linear_pass(*unit)
             product(*unit)

@@ -26,11 +26,11 @@ RUNS = 128
 FIRST_SCALAR = 40
 SECOND_SCALAR = 48
 WALK = 4
-SHARES = (72, 84, 72)
-LATE_GPSIMD = 88
+SHARES = (72, 88, 72)
+LATE_GPSIMD = 96
 SILU_LEAD = 6
-CUT_A = 384
-CUT_B = 832
+CUT_A = 288
+CUT_B = 864
 CUT_C = 128
 GAIN_PITCH = 16
 
@@ -57,8 +57,8 @@ def tile_autonomyofexpertsnormgate_x1_kernel(tc, x, wdown, rgain, wup, wp, out_0
         raw = {n: slots.tile([P, PACK, 512], BF16, name="raw_%s%d" % n, offset=SLOT * i) for i, n in enumerate(weights)}
         stage_at = [SLOT * (len(weights) + i) for i in range(4)]
         stage = [slots.tile([P, 512, PACK], BF16, name="stage%d" % i, align_bytes=64, offset=at) for i, at in enumerate(stage_at)]
-        b_both = keep.tile([P, 2 * 512, PACK], BF16, name="b_both", align_bytes=64)
-        b_stage = [b_both[:, 512 * s:512 * (s + 1), :] for s in range(2)]
+        b_both = [keep.tile([P, 2 * 512, PACK], BF16, name="b_both%d" % i, align_bytes=64) for i in range(2)]
+        b_stage = [[both[:, 512 * s:512 * (s + 1), :] for s in range(2)] for both in b_both]
         staged = {}
         codes, scales = {}, {}
         for n in weights + [("x", g) for g in range(G)]:
@@ -70,7 +70,9 @@ def tile_autonomyofexpertsnormgate_x1_kernel(tc, x, wdown, rgain, wup, wp, out_0
         for i, (e, g) in enumerate(steps):
             half = slice(512 * (i % 2), 512 * (i % 2 + 1))
             codes["b%d" % e, g], scales["b%d" % e, g] = b_codes[i // 2][:, half], b_scales[i // 2][:, half]
-        squared = keep.tile([P, 2 * PACK, R], BF16, name="squared")
+        squared_at = stage_at[-1] + SLOT
+        squared = slots.tile([P, 2 * PACK, R], BF16, name="squared", offset=squared_at)
+        spare_at = squared_at + 2 * SLOT
         sumsq = keep.tile([P, G * PACK, E], F32, name="sumsq")
         gate = keep.tile([P, G * PACK, E], F32, name="gate")
         res = [keep.tile([P, PACK, F], F32, name="res%d" % g) for g in range(G)]
@@ -100,13 +102,6 @@ def tile_autonomyofexpertsnormgate_x1_kernel(tc, x, wdown, rgain, wup, wp, out_0
         nc.scalar.activation(out=warm[:], in_=warm[:], func=ACT.Sqrt)
         make_identity(nc, ident[:])
         nc.scalar.copy(out=ident_b[:], in_=ident[:])
-        idle = psum.tile([P, P], F32, name="idle", tag="bank3", bufs=1, offset=3 * BANK)
-
-        def warm_up(count):
-            for i in range(count):
-                nc.tensor.matmul(out=idle[:], lhsT=ident[:], rhs=ident[:], start=True, stop=True)
-
-        warm_up(4)
 
         banks = {"v": [0, 1, 2, 3], "s": [4, 5, 6, 7]}
 
@@ -158,7 +153,7 @@ def tile_autonomyofexpertsnormgate_x1_kernel(tc, x, wdown, rgain, wup, wp, out_0
                                   in_=staged[n][:, lo:hi, :].rearrange("p c j -> p (c j)"))
 
         def quant_b(w):
-            nc.vector.quantize_mx(out=b_codes[w][:].bitcast(FP8X4), scales=b_scales[w][:], in_=b_both[:].rearrange("p c j -> p (c j)"))
+            nc.vector.quantize_mx(out=b_codes[w][:].bitcast(FP8X4), scales=b_scales[w][:], in_=b_both[w % 2][:].rearrange("p c j -> p (c j)"))
 
         def x_turn(g, lo, hi):
             words = x_raw[g, lo, hi][:].bitcast(F32)
@@ -205,9 +200,9 @@ def tile_autonomyofexpertsnormgate_x1_kernel(tc, x, wdown, rgain, wup, wp, out_0
             acts[e, pair, s] = work.tile([P, F], F32, name="act", bufs=SILU_LEAD + 3)
             nc.scalar.activation(out=acts[e, pair, s][:], in_=up[:], func=ACT.Silu)
 
-        def linear_pass(e, pair, s):
+        def linear_pass(e, pair, s, reader):
             g, t = place(pair, s)
-            lins[e, pair, s] = psum.tile([P, 512], F32, name="pp", **bank_of("v"))
+            lins[e, pair, s] = psum.tile([P, 512], F32, name="pp", **bank_of(reader))
             mx(lins[e, pair, s][:], ("x", g), cols(t), ("wp", e), whole)
 
         TURNED = 0
@@ -215,11 +210,15 @@ def tile_autonomyofexpertsnormgate_x1_kernel(tc, x, wdown, rgain, wup, wp, out_0
         def pair_res(pair):
             return res[pair // 2][:, 2 * (pair % 2):2 * (pair % 2) + 2, :]
 
+        term_at = {(0, 0): 0, (2, 0): 0, (1, 3): 0, (1, 0): SLOT, (3, 0): SLOT, (2, 3): SLOT,
+                   (1, 1): squared_at, (3, 3): squared_at, (1, 2): squared_at + SLOT, (2, 1): stage_at[0], (3, 1): stage_at[1],
+                   (2, 2): stage_at[2], (3, 2): spare_at}
+
         def term_of(e, pair):
             if e == 0 and pair != TURNED:
                 return pair_res(pair)
             if (e, pair) not in terms:
-                terms[e, pair] = slots.tile([P, 2, F], F32, name="term%d%d" % (e, pair), offset=SLOT * (len(terms) % len(weights)))
+                terms[e, pair] = slots.tile([P, 2, F], F32, name="term%d%d" % (e, pair), offset=term_at[e, pair])
             return terms[e, pair][:]
 
         def product(e, pair, s):
@@ -261,7 +260,7 @@ def tile_autonomyofexpertsnormgate_x1_kernel(tc, x, wdown, rgain, wup, wp, out_0
                 nc.scalar.copy(out=pair_res(TURNED)[:, s, :], in_=back[:])
             store_pair(TURNED)
 
-        og = b_stage
+        og = b_stage[0]
         oc = [keep.tile([P, F], U32, name="oc%d" % g, align_bytes=64) for g in range(G)]
         osc = keep.tile([P, F], U8, name="osc", align_bytes=64)
 
@@ -283,7 +282,6 @@ def tile_autonomyofexpertsnormgate_x1_kernel(tc, x, wdown, rgain, wup, wp, out_0
         lay_vector(("wd", 0), FIRST_SCALAR, RUNS)
         x_turn(*x_parts[0])
         x_turn(*x_parts[1])
-        warm_up(2)
         quant(("wd", 0))
         quant(("x", 0), 0, P)
         quant(("x", 0), P, 2 * P)
@@ -309,10 +307,9 @@ def tile_autonomyofexpertsnormgate_x1_kernel(tc, x, wdown, rgain, wup, wp, out_0
         silus = [job(silu_tile, *unit) for unit in units[:SILU_LEAD]]
         turn_x = [job(x_turn, *part) for part in x_parts[2:]]
         HALF = RUNS // 2
-        rests = [job(lay_tensor, shared[w], SHARES[w - 1], RUNS) for w in (1, 2, 3)]
-        jobs = ([None, turn_x[0]] + sq[0:7] + turn_x[1:] + sq[7:9] + rests[0:1]
-                + sq[9:17] + rests[1:2] + sq[17:20]
-                + sq[20:27] + [None, job(lay_tensor, alone, 0, HALF)] + sq[27:28] + [None, None]
+        rests = [job(lay, shared[w], SHARES[w - 1], RUNS) for w, lay in ((1, lay_scalar), (2, lay_tensor), (3, lay_tensor))]
+        jobs = (turn_x[:1] + sq[0:7] + turn_x[1:] + sq[7:8] + rests[0:1] + [None]
+                + sq[8:16] + rests[1:2] + sq[16:18] + [None] + sq[18:26] + [job(lay_tensor, alone, 0, HALF)] + sq[26:28] + [None]
                 + sq[28:32] + [gate_root, silus[0], None, None, rests[2], job(lay_tensor, alone, HALF, RUNS)] + silus[1:])
 
         def beside(count=1):
@@ -327,8 +324,8 @@ def tile_autonomyofexpertsnormgate_x1_kernel(tc, x, wdown, rgain, wup, wp, out_0
                 if i == 0 and w > 0:
                     lay_gpsimd(own[w], 0, RUNS)
                     lay_gpsimd(shared[w], 0, SHARES[w - 1])
-                b_tile(*steps[2 * w + s], t, b_stage[s])
-                beside({(0, 1): 3}.get((w, i), 1))
+                b_tile(*steps[2 * w + s], t, b_stage[w % 2][s])
+                beside({(0, 1): 2}.get((w, i), 1))
                 if (w, i) == (0, 0):
                     quant(("wd", 1))
                 if (w, i) == (0, 1):
@@ -339,11 +336,14 @@ def tile_autonomyofexpertsnormgate_x1_kernel(tc, x, wdown, rgain, wup, wp, out_0
                     nc.gpsimd.tensor_tensor(out=z[:], in0=score[:], in1=over_experts(top), op=ALU.subtract)
                 if (w, i) == (E - 1, 7):
                     nc.scalar.activation(out=sz[:], in_=z[:], func=ACT.Silu, bias=-1.0)
+                    nc.scalar.activation(out=rest[:], in_=z[:], func=ACT.Silu, scale=-1.0, bias=1.0)
             if w == 0:
-                for call in ((own[w],), (("b0", 0),), (("b1", 0), 0, 2 * P), (shared[w],)):
-                    quant(*call)
-                    beside()
-                quant(("b1", 0), 2 * P, 4 * P)
+                quant(own[w])
+                beside()
+                quant_b(w)
+                beside(2)
+                quant(shared[w])
+                beside()
             elif w < E - 1:
                 quant(own[w])
                 beside()
@@ -352,9 +352,8 @@ def tile_autonomyofexpertsnormgate_x1_kernel(tc, x, wdown, rgain, wup, wp, out_0
                 quant_b(w)
                 beside(2)
 
-        fill = [(own[-1],), (("b3", 1), 0, 2 * P)] + [(n, lo, lo + 2 * P) for n in (("b2", 1), shared[-1], alone) for lo in (0, 2 * P)] + [(("b3", 1), 2 * P, 4 * P)]
+        fill = [(own[-1],), (("b2", 1),), (shared[-1], 0, 2 * P), (shared[-1], 2 * P, 4 * P), (("b3", 1), 0, 2 * P), (alone, 0, 2 * P), (alone, 2 * P, 4 * P), (("b3", 1), 2 * P, 4 * P)]
         chain = [
-            lambda: nc.vector.scalar_tensor_tensor(out=rest[:], in0=z[:], scalar=-1.0, in1=sz[:], op0=ALU.add, op1=ALU.subtract),
             lambda: nc.vector.reciprocal(out=quot[:], in_=rest[:]),
             lambda: nc.vector.tensor_tensor(out=ex[:], in0=sz[:], in1=quot[:], op=ALU.mult),
             lambda: nc.vector.tensor_reduce(out=total[:, :, 0], in_=ex[:], axis=AX.X, op=ALU.add),
@@ -378,7 +377,7 @@ def tile_autonomyofexpertsnormgate_x1_kernel(tc, x, wdown, rgain, wup, wp, out_0
         turns = {9: (0, 1), 23: (2, 3)}
         skips = (1,)
         for i, unit in enumerate(units):
-            linear_pass(*unit)
+            linear_pass(*unit, "v" if i < len(units) - len(banks["s"]) else "s")
             product(*unit)
             if i == 1:
                 lay_scalar(late[1], LATE_GPSIMD, RUNS)
@@ -410,10 +409,10 @@ def tile_autonomyofexpertsnormgate_x1_kernel(tc, x, wdown, rgain, wup, wp, out_0
             if i == 27:
                 add_term(nc.vector, 3, 2, slice(CUT_B, 2 * F))
                 store_pair(2)
-                nc.vector.tensor_tensor(out=pair_res(3)[:, :, :CUT_C], in0=pair_res(3)[:, :, :CUT_C], in1=terms[1, 3][:, :, :CUT_C], op=ALU.add)
-                nc.gpsimd.tensor_tensor(out=terms[3, 2][:, :, CUT_C:], in0=pair_res(3)[:, :, CUT_C:], in1=terms[1, 3][:, :, CUT_C:], op=ALU.add)
-        nc.vector.tensor_tensor(out=pair_res(3)[:, :, CUT_C:], in0=terms[3, 2][:, :, CUT_C:], in1=terms[2, 3][:, :, CUT_C:], op=ALU.add)
-        nc.vector.tensor_tensor(out=pair_res(3)[:, :, :CUT_C], in0=pair_res(3)[:, :, :CUT_C], in1=terms[2, 3][:, :, :CUT_C], op=ALU.add)
+                add_term(nc.gpsimd, 1, 3)
+        nc.vector.tensor_tensor(out=terms[3, 3][:, 0, :], in0=terms[3, 3][:, 0, :], in1=terms[2, 3][:, 0, :], op=ALU.add)
+        add_term(nc.vector, 2, 3, slice(F + F // 2, 2 * F))
+        add_term(nc.vector, 2, 3, slice(F, F + F // 2))
         halves = (slice(F // 2, F), slice(0, F // 2))
         for cs in halves:
             nc.vector.tensor_tensor(out=pair_res(3)[:, :, cs], in0=pair_res(3)[:, :, cs], in1=terms[3, 3][:, :, cs], op=ALU.add)

@@ -48,6 +48,7 @@ def tile_autonomyofexpertsnormgate_x1_kernel(tc, x, wdown, rgain, wup, wp, out_0
         ident = keep.tile([P, P], F32, name="ident")
         ident_b = keep.tile([P, P], BF16, name="ident_b")
         warm = keep.tile([P, 1], F32, name="warm")
+        ones = keep.tile([P, 512], BF16, name="ones")
         x_parts = [(0, 0, 1), (0, 1, 2), (0, 2, 4), (1, 0, 2), (1, 2, 4)]
         x_raw = {part: keep.tile([P, (part[2] - part[1]) * D], BF16, name="x_raw%d%d%d" % part, align_bytes=64) for part in x_parts}
         weights = [("wd", 0), ("wd", 1), ("wd", 2), ("wu", 0), ("wd", 3), ("wu", 3), ("wp", 0), ("wu", 1), ("wp", 1), ("wu", 2), ("wp", 2), ("wp", 3)]
@@ -98,10 +99,18 @@ def tile_autonomyofexpertsnormgate_x1_kernel(tc, x, wdown, rgain, wup, wp, out_0
         for n in weights[3:]:
             load_w(n)
 
-        nc.vector.memset(warm[:], 0.0)
-        nc.scalar.activation(out=warm[:], in_=warm[:], func=ACT.Sqrt)
+        nc.vector.memset(ones[:], 1.0)
+        nc.scalar.activation(out=warm[:], in_=ones[:, 0:1], func=ACT.Sqrt)
         make_identity(nc, ident[:])
         nc.scalar.copy(out=ident_b[:], in_=ident[:])
+        idle = psum.tile([P, 512], F32, name="idle", tag="bank3", bufs=1, offset=3 * BANK)
+
+        def warm_up(moving, count):
+            for i in range(count):
+                nc.tensor.matmul(out=idle[:], lhsT=ones[:, 0:P], rhs=moving, start=True, stop=True)
+
+        warm_up(ones[:], 3)
+        warm_up(raw["wd", 0][:, 0, :], 1)
 
         banks = {"v": [0, 1, 2, 3], "s": [4, 5, 6, 7]}
 
@@ -282,6 +291,7 @@ def tile_autonomyofexpertsnormgate_x1_kernel(tc, x, wdown, rgain, wup, wp, out_0
         lay_vector(("wd", 0), FIRST_SCALAR, RUNS)
         x_turn(*x_parts[0])
         x_turn(*x_parts[1])
+        warm_up(ones[:], 2)
         quant(("wd", 0))
         quant(("x", 0), 0, P)
         quant(("x", 0), P, 2 * P)

@@ -23,16 +23,17 @@ G = T // GROUP
 BANK = 2048
 SLOT = PACK * 512 * 2
 RUNS = 128
+WALK = 4
+GAIN_PITCH = 16
 FIRST_SCALAR = 40
 SECOND_SCALAR = 48
-WALK = 4
-SHARES = (72, 88, 72)
+SHARES = (64, 72, 64)
 LATE_GPSIMD = 96
-SILU_LEAD = 6
 CUT_A = 288
 CUT_B = 864
-CUT_C = 128
-GAIN_PITCH = 16
+STAGES = 4
+BBUF = 2
+LEAD = 6
 
 
 def tile_autonomyofexpertsnormgate_x1_kernel(tc, x, wdown, rgain, wup, wp, out_0, out_1, out_2):
@@ -41,8 +42,7 @@ def tile_autonomyofexpertsnormgate_x1_kernel(tc, x, wdown, rgain, wup, wp, out_0
     with ExitStack() as ctx:
         keep = ctx.enter_context(tc.tile_pool(name="keep", bufs=1))
         slots = ctx.enter_context(tc.tile_pool(name="slots", bufs=1))
-        work = ctx.enter_context(tc.tile_pool(name="work", bufs=2))
-        psum = ctx.enter_context(tc.psum_pool(name="psum", bufs=4))
+        psum = ctx.enter_context(tc.psum_pool(name="psum", bufs=1))
         ctx.enter_context(tc.manual_schedule())
         gain = keep.tile([P, E, GAIN_PITCH], BF16, name="gain")
         ident = keep.tile([P, P], F32, name="ident")
@@ -56,9 +56,9 @@ def tile_autonomyofexpertsnormgate_x1_kernel(tc, x, wdown, rgain, wup, wp, out_0
         for e in range(E):
             src["wd", e], src["wp", e], src["wu", e] = wdown[e], wp[e], wup[e]
         raw = {n: slots.tile([P, PACK, 512], BF16, name="raw_%s%d" % n, offset=SLOT * i) for i, n in enumerate(weights)}
-        stage_at = [SLOT * (len(weights) + i) for i in range(4)]
+        stage_at = [SLOT * (len(weights) + i) for i in range(STAGES)]
         stage = [slots.tile([P, 512, PACK], BF16, name="stage%d" % i, align_bytes=64, offset=at) for i, at in enumerate(stage_at)]
-        b_both = [keep.tile([P, 2 * 512, PACK], BF16, name="b_both%d" % i, align_bytes=64) for i in range(2)]
+        b_both = [keep.tile([P, 2 * 512, PACK], BF16, name="b_both%d" % i, align_bytes=64) for i in range(BBUF)]
         b_stage = [[both[:, 512 * s:512 * (s + 1), :] for s in range(2)] for both in b_both]
         staged = {}
         codes, scales = {}, {}
@@ -71,9 +71,8 @@ def tile_autonomyofexpertsnormgate_x1_kernel(tc, x, wdown, rgain, wup, wp, out_0
         for i, (e, g) in enumerate(steps):
             half = slice(512 * (i % 2), 512 * (i % 2 + 1))
             codes["b%d" % e, g], scales["b%d" % e, g] = b_codes[i // 2][:, half], b_scales[i // 2][:, half]
-        squared_at = stage_at[-1] + SLOT
-        squared = slots.tile([P, 2 * PACK, R], BF16, name="squared", offset=squared_at)
-        spare_at = squared_at + 2 * SLOT
+            staged["b%d" % e, g] = b_stage[i // 2 % BBUF][i % 2]
+        squared = keep.tile([P, 2 * PACK, R], BF16, name="squared")
         sumsq = keep.tile([P, G * PACK, E], F32, name="sumsq")
         gate = keep.tile([P, G * PACK, E], F32, name="gate")
         res = [keep.tile([P, PACK, F], F32, name="res%d" % g) for g in range(G)]
@@ -103,7 +102,7 @@ def tile_autonomyofexpertsnormgate_x1_kernel(tc, x, wdown, rgain, wup, wp, out_0
         nc.scalar.activation(out=warm[:], in_=ones[:, 0:1], func=ACT.Sqrt)
         make_identity(nc, ident[:])
         nc.scalar.copy(out=ident_b[:], in_=ident[:])
-        idle = psum.tile([P, 512], F32, name="idle", tag="bank3", bufs=1, offset=3 * BANK)
+        idle = psum.tile([P, 512], F32, name="idle", tag="bank3", offset=3 * BANK)
 
         def warm_up(moving, count):
             for i in range(count):
@@ -112,14 +111,10 @@ def tile_autonomyofexpertsnormgate_x1_kernel(tc, x, wdown, rgain, wup, wp, out_0
         warm_up(ones[:], 3)
         warm_up(raw["wd", 0][:, 0, :], 1)
 
-        banks = {"v": [0, 1, 2, 3], "s": [4, 5, 6, 7]}
+        free = {"v": [0, 1, 2, 3], "s": [4, 5, 6, 7]}
 
-        def bank_at(b):
-            return {"tag": "bank%d" % b, "bufs": 1, "offset": BANK * b}
-
-        def bank_of(reader):
-            banks[reader].append(banks[reader].pop(0))
-            return bank_at(banks[reader][-1])
+        def bank_tile(b, shape, dtype):
+            return psum.tile(shape, dtype, name="bank%d" % b, tag="bank%d" % b, offset=BANK * b)
 
         def cols(t):
             return slice(P * t, P * (t + 1))
@@ -142,51 +137,75 @@ def tile_autonomyofexpertsnormgate_x1_kernel(tc, x, wdown, rgain, wup, wp, out_0
             dst, rows = run_views(n, lo, hi)
             nc.gpsimd.tensor_scalar(out=dst, in0=rows, scalar1=1.0, scalar2=0.0, op0=ALU.mult, op1=ALU.add)
 
-        def lay_scalar(n, lo, hi):
+        def lay(copy, n, lo, hi):
             dst, rows = run_views(n, lo, hi)
-            nc.scalar.copy(out=dst, in_=rows)
+            copy(out=dst, in_=rows)
 
-        def lay_vector(n, lo, hi):
-            dst, rows = run_views(n, lo, hi)
-            nc.vector.tensor_copy(out=dst, in_=rows)
+        def plain(call, *args):
+            return (lambda bank: call(*args), None, (), ())
 
-        def lay_tensor(n, lo, hi):
-            bank = psum.tile([P, 4 * (hi - lo), PACK], BF16, name="pw", **bank_of("s"))
-            for u in range(2):
-                nc.tensor.matmul(out=bank[:, :, 2 * u:2 * u + 2].rearrange("p c j -> p j c"), lhsT=ident_b[:],
-                                 rhs=raw[n][:, 2 * u:2 * u + 2, 4 * lo:4 * hi], start=True, stop=True)
-            nc.scalar.copy(out=staged[n][:, 4 * lo:4 * hi, :], in_=bank[:])
+        def made_by(n, lo, hi):
+            return [(n, t) for t in range(lo // P, hi // P)]
 
-        def quant(n, lo=0, hi=512):
+        def quantise(n, lo, hi):
             nc.vector.quantize_mx(out=codes[n][:, lo:hi].bitcast(FP8X4), scales=scales[n][:, lo:hi],
                                   in_=staged[n][:, lo:hi, :].rearrange("p c j -> p (c j)"))
 
+        def quant(n, lo=0, hi=512):
+            return (lambda bank: quantise(n, lo, hi), None, (), made_by(n, lo, hi))
+
         def quant_b(w):
-            nc.vector.quantize_mx(out=b_codes[w][:].bitcast(FP8X4), scales=b_scales[w][:], in_=b_both[w % 2][:].rearrange("p c j -> p (c j)"))
+            def work(bank):
+                nc.vector.quantize_mx(out=b_codes[w][:].bitcast(FP8X4), scales=b_scales[w][:], in_=b_both[w % BBUF][:].rearrange("p c j -> p (c j)"))
+            return (work, None, (), [tile for e, g in steps[2 * w:2 * w + 2] for tile in made_by(("b%d" % e, g), 0, 512)])
+
+        def lay_tensor(copy, n, lo, hi):
+            def front(b):
+                bank = bank_tile(b, [P, 4 * (hi - lo), PACK], BF16)
+                for u in range(2):
+                    nc.tensor.matmul(out=bank[:, :, 2 * u:2 * u + 2].rearrange("p c j -> p j c"), lhsT=ident_b[:],
+                                     rhs=raw[n][:, 2 * u:2 * u + 2, 4 * lo:4 * hi], start=True, stop=True)
+                return bank
+            return (lambda bank: copy(out=staged[n][:, 4 * lo:4 * hi, :], in_=bank[:]), front, (), ())
 
         def x_turn(g, lo, hi):
-            words = x_raw[g, lo, hi][:].bitcast(F32)
-            dstw = staged["x", g][:].rearrange("p c j -> p (c j)").bitcast(F32).rearrange("p (s r u) -> p s r u", r=P, u=2)
-            bank = psum.tile([P, (hi - lo) * 256], F32, name="pt", **bank_of("s"))
-            view = bank[:].rearrange("p (s u r) -> p s u r", r=P, u=2)
-            for s in range(hi - lo):
-                for u in range(2):
-                    nc.tensor.transpose(view[:, s, u, :], words[:, 256 * s + u:256 * (s + 1):2], ident[:])
-            nc.scalar.copy(out=dstw[:, lo:hi], in_=view.rearrange("p s u r -> p s r u"))
+            def front(b):
+                words = x_raw[g, lo, hi][:].bitcast(F32)
+                view = bank_tile(b, [P, (hi - lo) * 256], F32)[:].rearrange("p (s u r) -> p s u r", r=P, u=2)
+                for s in range(hi - lo):
+                    for u in range(2):
+                        nc.tensor.transpose(view[:, s, u, :], words[:, 256 * s + u:256 * (s + 1):2], ident[:])
+                return view
 
-        def b_tile(e, g, t, into):
-            ranks = psum.tile([P, 512], F32, name="pa", **bank_of("v"))
-            for k in range(PACK):
-                mx(ranks[:, cols(k)], ("wd", e), cols(k), ("x", g), cols(t))
-            staged["b%d" % e, g] = into
-            nc.vector.tensor_tensor(out=into[:, cols(t), :], in0=ranks[:].rearrange("p (k n) -> p n k", k=PACK),
-                                    in1=gain[:, e, 0:PACK].unsqueeze(1).to_broadcast([P, P, PACK]), op=ALU.mult)
+            def work(view):
+                dst = staged["x", g][:].rearrange("p c j -> p (c j)").bitcast(F32).rearrange("p (s r u) -> p s r u", r=P, u=2)
+                nc.scalar.copy(out=dst[:, lo:hi], in_=view.rearrange("p s u r -> p s r u"))
+            return (work, front, (), ())
+
+        def b_tile(e, g, t):
+            def front(b):
+                ranks = bank_tile(b, [P, 512], F32)
+                for k in range(PACK):
+                    mx(ranks[:, cols(k)], ("wd", e), cols(k), ("x", g), cols(t))
+                return ranks
+
+            def work(ranks):
+                nc.vector.tensor_tensor(out=staged["b%d" % e, g][:, cols(t), :], in0=ranks[:].rearrange("p (k n) -> p n k", k=PACK),
+                                        in1=gain[:, e, 0:PACK].unsqueeze(1).to_broadcast([P, P, PACK]), op=ALU.mult)
+            return (work, front, made_by(("wd", e), 0, 512) + [(("x", g), t)], ())
+
+        def one_pass(left, t, right):
+            def front(b):
+                bank = bank_tile(b, [P, 512], F32)
+                mx(bank[:], left, cols(t), right, whole)
+                return bank
+            return front, made_by(right, 0, 512) + [(left, t)]
 
         def square_tile(e, g, t):
-            toks = psum.tile([P, 512], F32, name="pb", **bank_of("s"))
-            mx(toks[:], ("x", g), cols(t), ("wd", e), whole)
-            nc.scalar.activation(out=squared[:, PACK * (e % 2) + t, :], in_=toks[:], func=ACT.Square,
-                                 accum_out=sumsq[:, PACK * g + t, e:e + 1])
+            def work(toks):
+                nc.scalar.activation(out=squared[:, PACK * (e % 2) + t, :], in_=toks[:], func=ACT.Square,
+                                     accum_out=sumsq[:, PACK * g + t, e:e + 1])
+            return (work,) + one_pass(("x", g), t, ("wd", e)) + ((),)
 
         score, z, sz, rest, quot, ex = (keep.tile([P, G * PACK, E], F32, name=name)
                                         for name in ("score", "z", "sz", "rest", "quot", "ex"))
@@ -195,52 +214,43 @@ def tile_autonomyofexpertsnormgate_x1_kernel(tc, x, wdown, rgain, wup, wp, out_0
         def over_experts(tile):
             return tile[:].to_broadcast([P, G * PACK, E])
 
-        cycles = [[(0, 0), (0, 1)], [(1, 0), (1, 1)], [(0, 2), (1, 2)], [(2, 0), (2, 1)], [(3, 0), (3, 1)], [(2, 2), (3, 2)], [(0, 3), (1, 3)], [(2, 3), (3, 3)]]
-        units = [(e, pair, s) for cycle in cycles for e, pair in cycle for s in range(2)]
-        acts, lins, terms = {}, {}, {}
+        terms = {}
+        spare = [SLOT * i for i in range(len(weights))]
 
         def place(pair, s):
             return pair // 2, 2 * (pair % 2) + s
 
-        def silu_tile(e, pair, s):
-            g, t = place(pair, s)
-            up = psum.tile([P, 512], F32, name="pu", **bank_of("s"))
-            mx(up[:], ("b%d" % e, g), cols(t), ("wu", e), whole)
-            acts[e, pair, s] = work.tile([P, F], F32, name="act", bufs=SILU_LEAD + 3)
-            nc.scalar.activation(out=acts[e, pair, s][:], in_=up[:], func=ACT.Silu)
-
-        def linear_pass(e, pair, s, reader):
-            g, t = place(pair, s)
-            lins[e, pair, s] = psum.tile([P, 512], F32, name="pp", **bank_of(reader))
-            mx(lins[e, pair, s][:], ("x", g), cols(t), ("wp", e), whole)
-
-        TURNED = 0
-
         def pair_res(pair):
             return res[pair // 2][:, 2 * (pair % 2):2 * (pair % 2) + 2, :]
 
-        term_at = {(0, 0): 0, (2, 0): 0, (1, 3): 0, (1, 0): SLOT, (3, 0): SLOT, (2, 3): SLOT,
-                   (1, 1): squared_at, (3, 3): squared_at, (1, 2): squared_at + SLOT, (2, 1): stage_at[0], (3, 1): stage_at[1],
-                   (2, 2): stage_at[2], (3, 2): spare_at}
-
         def term_of(e, pair):
-            if e == 0 and pair != TURNED:
+            if e == 0:
                 return pair_res(pair)
             if (e, pair) not in terms:
-                terms[e, pair] = slots.tile([P, 2, F], F32, name="term%d%d" % (e, pair), offset=term_at[e, pair])
+                terms[e, pair] = slots.tile([P, 2, F], F32, name="term%d%d" % (e, pair), offset=spare.pop(0))
             return terms[e, pair][:]
+
+        def silu_tile(e, pair, s):
+            g, t = place(pair, s)
+
+            def work(up):
+                nc.scalar.activation(out=term_of(e, pair)[:, s, :], in_=up[:], func=ACT.Silu)
+            return (work,) + one_pass(("b%d" % e, g), t, ("wu", e)) + ((),)
 
         def product(e, pair, s):
             g, t = place(pair, s)
-            nc.vector.scalar_tensor_tensor(out=term_of(e, pair)[:, s, :], in0=lins[e, pair, s][:], scalar=gate[:, PACK * g + t, e:e + 1],
-                                           in1=acts[e, pair, s][:], op0=ALU.mult, op1=ALU.mult)
+
+            def work(lin):
+                tile = term_of(e, pair)[:, s, :]
+                nc.vector.scalar_tensor_tensor(out=tile, in0=lin[:], scalar=gate[:, PACK * g + t, e:e + 1], in1=tile,
+                                               op0=ALU.mult, op1=ALU.mult)
+            return (work,) + one_pass(("x", g), t, ("wp", e)) + ((),)
 
         def flat(ap):
             return ap.rearrange("p t f -> p (t f)")
 
-        def add_term(engine, e, pair, span=slice(0, 2 * F)):
-            dst = flat(pair_res(pair))[:, span]
-            engine.tensor_tensor(out=dst, in0=dst, in1=flat(terms[e, pair][:])[:, span], op=ALU.add)
+        def add(engine, out, in0, in1, span=slice(0, 2 * F)):
+            engine.tensor_tensor(out=flat(out)[:, span], in0=flat(in0)[:, span], in1=flat(in1)[:, span], op=ALU.add)
 
         def store_pair(pair, cs=slice(0, F)):
             h = pair % 2
@@ -249,33 +259,36 @@ def tile_autonomyofexpertsnormgate_x1_kernel(tc, x, wdown, rgain, wup, wp, out_0
         turned = keep.tile([P, 2, F], F32, name="turned")
         sums, held = {}, {}
 
-        def sum_turn(e):
-            for s in range(2):
-                if e == 0:
-                    held[s] = banks["vs"[s]].pop(0)
-                    sums[s] = psum.tile([P, F], F32, name="psum_sum", **bank_at(held[s]))
-                for c in range(4):
-                    nc.tensor.matmul(out=sums[s][:, cols(c)], lhsT=terms[e, TURNED][:, s, cols(c)], rhs=ident[:], is_transpose=True,
-                                     start=(e, c) == (0, 0), stop=(e, c) == (E - 1, 3))
-            if e == E - 1:
+        def sum_turn(pair, experts):
+            for e in experts:
                 for s in range(2):
-                    nc.scalar.copy(out=turned[:, s, :], in_=sums[s][:])
+                    if e == 0:
+                        held["vs"[s]] = free["vs"[s]].pop(0)
+                        sums[s] = bank_tile(held["vs"[s]], [P, F], F32)
+                    for c in range(4):
+                        nc.tensor.matmul(out=sums[s][:, cols(c)], lhsT=term_of(e, pair)[:, s, cols(c)], rhs=ident[:], is_transpose=True,
+                                         start=(e, c) == (0, 0), stop=(e, c) == (E - 1, 3))
+
+        def sum_out(s):
+            nc.scalar.copy(out=turned[:, s, :], in_=sums[s][:])
 
         def sum_back():
             for s in range(2):
-                back = psum.tile([P, F], F32, name="psum_back", **bank_at(held[s]))
+                sums[s] = bank_tile(held["vs"[s]], [P, F], F32)
                 for c in range(4):
-                    nc.tensor.transpose(back[:, cols(c)], turned[:, s, cols(c)], ident[:])
-                nc.scalar.copy(out=pair_res(TURNED)[:, s, :], in_=back[:])
-            store_pair(TURNED)
+                    nc.tensor.transpose(sums[s][:, cols(c)], turned[:, s, cols(c)], ident[:])
+
+        def sum_home(pair, s):
+            nc.scalar.copy(out=pair_res(pair)[:, s, :], in_=sums[s][:])
+            if s == 1:
+                store_pair(pair)
 
         og = b_stage[0]
         oc = [keep.tile([P, F], U32, name="oc%d" % g, align_bytes=64) for g in range(G)]
         osc = keep.tile([P, F], U8, name="osc", align_bytes=64)
 
-        def o_views(g, lo, hi):
-            return (og[g][:, lo:hi, :].rearrange("p (m q) t -> p m t q", q=4),
-                    res[g][:, :, lo:hi].rearrange("p t (m q) -> p m t q", q=4))
+        def rounding(copy, g, lo, hi):
+            copy(out=og[g][:, lo:hi, :].rearrange("p (m q) t -> p m t q", q=4), in_=res[g][:, :, lo:hi].rearrange("p t (m q) -> p m t q", q=4))
 
         def o_quant(g, lo, hi):
             nc.vector.quantize_mx(out=oc[g][:, lo:hi].bitcast(FP8X4), scales=osc[4 * g:P, lo:hi],
@@ -286,83 +299,88 @@ def tile_autonomyofexpertsnormgate_x1_kernel(tc, x, wdown, rgain, wup, wp, out_0
             for q in range(4):
                 nc.sync.dma_start(out=out_2[:, 4 * q:4 * q + 4, :].bitcast(I32), in_=osc[32 * q:32 * q + 4 * G, :].bitcast(I32))
 
-        staged["x", 0], staged["x", 1], staged["wd", 0], staged["wd", 1] = stage[3], stage[1], stage[2], stage[0]
-        lay_scalar(("wd", 0), 0, FIRST_SCALAR)
-        lay_vector(("wd", 0), FIRST_SCALAR, RUNS)
-        x_turn(*x_parts[0])
-        x_turn(*x_parts[1])
-        warm_up(ones[:], 2)
-        quant(("wd", 0))
-        quant(("x", 0), 0, P)
-        quant(("x", 0), P, 2 * P)
-        lay_scalar(("wd", 1), 0, SECOND_SCALAR)
-        lay_vector(("wd", 1), SECOND_SCALAR, RUNS)
+        made = []
+        queue = {"v": [], "s": []}
+        fronted = {"v": [], "s": []}
 
+        def fronts(side, look=0):
+            while len(fronted[side]) < min(len(queue[side]), look + 1):
+                work, front, needs, gives = queue[side][len(fronted[side])]
+                if front is None:
+                    fronted[side].append(None)
+                elif free[side] and all(tile in made for tile in needs):
+                    b = free[side].pop(0)
+                    fronted[side].append((b, front(b)))
+                else:
+                    return
+
+        def run(side):
+            fronts(side)
+            work, front, needs, gives = queue[side].pop(0)
+            bank = fronted[side].pop(0)
+            work(bank[1] if bank else None)
+            if bank:
+                free[side].append(bank[0])
+            return gives
+
+        def turn(beside=1, ahead=None):
+            if ahead:
+                ahead()
+            gives = run("v")
+            for i in range(min(beside, len(queue["s"]))):
+                run("s")
+            made.extend(gives)
+
+        staged["x", 0], staged["x", 1], staged["wd", 0], staged["wd", 1] = stage[3], stage[1], stage[2], stage[0]
         own = [("wd", 2), ("wd", 3), ("wp", 0), ("wp", 1)]
         shared = [("x", 1), ("wu", 0), ("wu", 1), ("wu", 2)]
         for w, (mine, other) in enumerate(((3, 1), (1, 2), (2, 0), (0, 1))):
             staged[own[w]], staged[shared[w]] = stage[mine], stage[other]
         alone, late = ("wu", 3), [("wp", 2), ("wp", 3)]
         staged[alone], staged[late[0]], staged[late[1]] = stage[3], stage[3], stage[2]
+        nothing = plain(lambda: None)
+        scopy, vcopy = nc.scalar.copy, nc.vector.tensor_copy
+
+        lay(scopy, ("wd", 0), 0, FIRST_SCALAR)
+        lay(vcopy, ("wd", 0), FIRST_SCALAR, RUNS)
+        queue["s"] = [x_turn(*part) for part in x_parts[:2]]
+        run("s")
+        run("s")
+        warm_up(ones[:], 2)
+        for n, lo, hi in ((("wd", 0), 0, 512), (("x", 0), 0, P), (("x", 0), P, 2 * P)):
+            quantise(n, lo, hi)
+            made.extend(made_by(n, lo, hi))
+        lay(scopy, ("wd", 1), 0, SECOND_SCALAR)
+        lay(vcopy, ("wd", 1), SECOND_SCALAR, RUNS)
+
         opening = [(e, 0, 2 * h + s) for h in range(2) for e in range(2) for s in range(2)]
+        order = opening + [(e, g, t) for e, g in ((2, 0), (0, 1), (1, 1), (3, 0), (2, 1), (3, 1)) for t in range(PACK)]
+        sq = [square_tile(*tile) for tile in order]
+        cycles = [[(0, 0), (0, 1)], [(1, 0), (1, 1)], [(0, 2), (1, 2)], [(2, 0), (2, 1)], [(3, 0), (3, 1)], [(2, 2), (3, 2)], [(0, 3), (1, 3)], [(2, 3), (3, 3)]]
+        units = [(e, pair, s) for cycle in cycles for e, pair in cycle for s in range(2)]
+        silus = [silu_tile(*unit) for unit in units]
+        HALF = RUNS // 2
 
         def gate_root():
             nc.scalar.activation(out=score[:], in_=sumsq[:], func=ACT.Sqrt)
 
-        def job(call, *args):
-            return lambda: call(*args)
+        def gate_silu():
+            nc.scalar.activation(out=sz[:], in_=z[:], func=ACT.Silu, bias=-1.0)
+            nc.scalar.activation(out=rest[:], in_=z[:], func=ACT.Silu, scale=-1.0, bias=1.0)
 
-        order = opening + [(e, g, t) for e, g in ((2, 0), (0, 1), (1, 1), (3, 0), (2, 1), (3, 1)) for t in range(PACK)]
-        sq = [job(square_tile, *tile) for tile in order]
-        silus = [job(silu_tile, *unit) for unit in units[:SILU_LEAD]]
-        turn_x = [job(x_turn, *part) for part in x_parts[2:]]
-        HALF = RUNS // 2
-        rests = [job(lay, shared[w], SHARES[w - 1], RUNS) for w, lay in ((1, lay_scalar), (2, lay_tensor), (3, lay_tensor))]
-        jobs = (turn_x[:1] + sq[0:7] + turn_x[1:] + sq[7:8] + rests[0:1] + [None]
-                + sq[8:16] + rests[1:2] + sq[16:18] + [None] + sq[18:26] + [job(lay_tensor, alone, 0, HALF)] + sq[26:28] + [None]
-                + sq[28:32] + [gate_root, silus[0], None, None, rests[2], job(lay_tensor, alone, HALF, RUNS)] + silus[1:])
+        def gate_top():
+            nc.vector.tensor_reduce(out=top[:, :, 0], in_=score[:], axis=AX.X, op=ALU.max)
+            nc.gpsimd.tensor_tensor(out=z[:], in0=score[:], in1=over_experts(top), op=ALU.subtract)
 
-        def beside(count=1):
-            for i in range(min(count, len(jobs))):
-                call = jobs.pop(0)
-                if call:
-                    call()
+        queue["s"] = (sq[0:1] + [x_turn(*x_parts[2])] + sq[1:8] + [x_turn(*part) for part in x_parts[3:]] + [plain(lay, scopy, shared[1], SHARES[0], RUNS), nothing]
+                      + sq[8:16] + [lay_tensor(scopy, shared[2], SHARES[1], RUNS)] + sq[16:18] + [nothing] + sq[18:26] + [lay_tensor(scopy, alone, 0, HALF)] + sq[26:28] + [nothing]
+                      + sq[28:32] + [plain(gate_root), silus[0], nothing, nothing, plain(gate_silu), lay_tensor(scopy, shared[3], SHARES[2], RUNS), lay_tensor(scopy, alone, HALF, RUNS)]
+                      + silus[1:])
 
-        for w in range(E):
-            for i in range(2 * PACK):
-                s, t = (opening[i][0], opening[i][2]) if w == 0 else divmod(i, PACK)
-                if i == 0 and w > 0:
-                    lay_gpsimd(own[w], 0, RUNS)
-                    lay_gpsimd(shared[w], 0, SHARES[w - 1])
-                b_tile(*steps[2 * w + s], t, b_stage[w % 2][s])
-                beside({(0, 1): 2}.get((w, i), 1))
-                if (w, i) == (0, 0):
-                    quant(("wd", 1))
-                if (w, i) == (0, 1):
-                    quant(("x", 0), 2 * P, 4 * P)
-                    lay_gpsimd(own[0], 0, RUNS)
-                if (w, i) == (E - 1, 5):
-                    nc.vector.tensor_reduce(out=top[:, :, 0], in_=score[:], axis=AX.X, op=ALU.max)
-                    nc.gpsimd.tensor_tensor(out=z[:], in0=score[:], in1=over_experts(top), op=ALU.subtract)
-                if (w, i) == (E - 1, 7):
-                    nc.scalar.activation(out=sz[:], in_=z[:], func=ACT.Silu, bias=-1.0)
-                    nc.scalar.activation(out=rest[:], in_=z[:], func=ACT.Silu, scale=-1.0, bias=1.0)
-            if w == 0:
-                quant(own[w])
-                beside()
-                quant_b(w)
-                beside(2)
-                quant(shared[w])
-                beside()
-            elif w < E - 1:
-                quant(own[w])
-                beside()
-                quant(shared[w])
-                beside()
-                quant_b(w)
-                beside(2)
+        def window(w):
+            return [b_tile(*steps[2 * w + s], t) for s in range(2) for t in range(PACK)]
 
-        fill = [(own[-1],), (("b2", 1),), (shared[-1], 0, 2 * P), (shared[-1], 2 * P, 4 * P), (("b3", 1), 0, 2 * P), (alone, 0, 2 * P), (alone, 2 * P, 4 * P), (("b3", 1), 2 * P, 4 * P)]
+        first = [b_tile(*tile) for tile in opening]
         chain = [
             lambda: nc.vector.reciprocal(out=quot[:], in_=rest[:]),
             lambda: nc.vector.tensor_tensor(out=ex[:], in0=sz[:], in1=quot[:], op=ALU.mult),
@@ -370,69 +388,86 @@ def tile_autonomyofexpertsnormgate_x1_kernel(tc, x, wdown, rgain, wup, wp, out_0
             lambda: nc.vector.reciprocal(out=inv[:], in_=total[:]),
             lambda: nc.vector.tensor_tensor(out=gate[:], in0=ex[:], in1=over_experts(inv), op=ALU.mult),
         ]
-        for i in range(2):
-            quant(*fill.pop(0))
-            beside()
-        for link, call in zip(chain, fill):
-            link()
-            quant(*call)
-            beside()
-        quant(*fill[-1])
-        lay_gpsimd(late[0], 0, RUNS)
-        lay_gpsimd(late[1], 0, LATE_GPSIMD)
-        while jobs:
-            beside()
+        fill = [quant(shared[-1], 0, 2 * P), quant(shared[-1], 2 * P, 4 * P), quant(("b3", 1), 0, 2 * P), quant(alone, 0, 2 * P), quant(alone, 2 * P, 4 * P)]
+        products = [product(*unit) for unit in units]
+        running = stage_at[3]
+        program = [(first[0], 2), (quant(("wd", 1)), 0), (first[1], 1), (quant(("x", 0), 2 * P, 4 * P), 0, lambda: lay_gpsimd(own[0], 0, RUNS))]
+        program += [(step, 1) for step in first[2:]] + [(quant(own[0]), 1), (quant_b(0), 2), (quant(shared[0]), 1, lambda: shares(1))]
+        for w in (1, 2):
+            program += [(step, 1) for step in window(w)] + [(quant(own[w]), 1), (quant(shared[w]), 1), (quant_b(w), 2, lambda w=w: shares(w + 1))]
 
-        ahead = units[SILU_LEAD:]
-        turns = {9: (0, 1), 23: (2, 3)}
-        skips = (1,)
-        for i, unit in enumerate(units):
-            linear_pass(*unit, "v" if i < len(units) - len(banks["s"]) else "s")
-            product(*unit)
+        def shares(w):
+            lay_gpsimd(own[w], 0, RUNS)
+            lay_gpsimd(shared[w], 0, SHARES[w - 1])
+
+        last = window(3)
+        program += [(step, 1) for step in last[:6]] + [(plain(gate_top), 0)] + [(step, 1) for step in last[6:]]
+        program += [(quant(own[-1]), 2), (quant(("b2", 1)), 1)]
+        for link, call in zip(chain, fill):
+            program += [(plain(link), 0), (call, 1)]
+
+        def lay_late():
+            lay_gpsimd(late[0], 0, RUNS)
+            lay_gpsimd(late[1], 0, LATE_GPSIMD)
+
+        program += [(quant(("b3", 1), 2 * P, 4 * P), 0, lay_late)]
+        queue["v"] = [entry[0] for entry in program] + products
+        for entry in program:
+            turn(entry[1])
+            if len(entry) > 2:
+                entry[2]()
+        while len(queue["s"]) > len(units) - LEAD:
+            run("s")
+        for i in range(len(units)):
+            run("v")
             if i == 1:
-                lay_scalar(late[1], LATE_GPSIMD, RUNS)
-            for e in turns.get(i, ()):
-                sum_turn(e)
+                lay(scopy, late[1], LATE_GPSIMD, RUNS)
+            if i == 9:
+                sum_turn(0, (0, 1))
+            if i == 23:
+                sum_turn(0, (2, 3))
+                sum_out(0)
+                sum_out(1)
             if i == 27:
                 sum_back()
-            if ahead and i not in skips:
-                silu_tile(*ahead.pop(0))
+                sum_home(0, 0)
+                sum_home(0, 1)
+            if queue["s"] and i != 1:
+                run("s")
             if i == 29:
-                dst, rows = o_views(0, 0, F)
-                nc.scalar.copy(out=dst, in_=rows)
+                rounding(scopy, 0, 0, F)
             if i == 7:
-                quant(late[0])
-                quant(late[1])
-                running = slots.tile([P, 2, F], F32, name="running", offset=stage_at[3])
-                nc.gpsimd.tensor_tensor(out=running[:], in0=pair_res(1), in1=terms[1, 1][:], op=ALU.add)
+                for n in late:
+                    quantise(n, 0, 512)
+                    made.extend(made_by(n, 0, 512))
+                sofar = slots.tile([P, 2, F], F32, name="running", offset=running)
+                add(nc.gpsimd, sofar[:], pair_res(1), term_of(1, 1))
             if i == 11:
-                add_term(nc.gpsimd, 1, 2)
+                add(nc.gpsimd, pair_res(2), pair_res(2), term_of(1, 2))
             if i == 15:
-                nc.gpsimd.tensor_tensor(out=running[:], in0=running[:], in1=terms[2, 1][:], op=ALU.add)
+                add(nc.gpsimd, sofar[:], sofar[:], term_of(2, 1))
             if i == 19:
-                nc.gpsimd.tensor_tensor(out=flat(pair_res(1))[:, CUT_A:], in0=flat(running[:])[:, CUT_A:], in1=flat(terms[3, 1][:])[:, CUT_A:], op=ALU.add)
+                add(nc.gpsimd, pair_res(1), sofar[:], term_of(3, 1), slice(CUT_A, 2 * F))
             if i == 23:
-                nc.vector.tensor_tensor(out=flat(pair_res(1))[:, :CUT_A], in0=flat(running[:])[:, :CUT_A], in1=flat(terms[3, 1][:])[:, :CUT_A], op=ALU.add)
+                add(nc.vector, pair_res(1), sofar[:], term_of(3, 1), slice(0, CUT_A))
                 store_pair(1)
-                add_term(nc.vector, 2, 2)
-                add_term(nc.gpsimd, 3, 2, slice(0, CUT_B))
+                add(nc.vector, pair_res(2), pair_res(2), term_of(2, 2))
+                add(nc.gpsimd, pair_res(2), pair_res(2), term_of(3, 2), slice(0, CUT_B))
             if i == 27:
-                add_term(nc.vector, 3, 2, slice(CUT_B, 2 * F))
+                add(nc.vector, pair_res(2), pair_res(2), term_of(3, 2), slice(CUT_B, 2 * F))
                 store_pair(2)
-                add_term(nc.gpsimd, 1, 3)
+                add(nc.gpsimd, pair_res(3), pair_res(3), term_of(1, 3))
         nc.vector.tensor_tensor(out=terms[3, 3][:, 0, :], in0=terms[3, 3][:, 0, :], in1=terms[2, 3][:, 0, :], op=ALU.add)
-        add_term(nc.vector, 2, 3, slice(F + F // 2, 2 * F))
-        add_term(nc.vector, 2, 3, slice(F, F + F // 2))
+        add(nc.vector, pair_res(3), pair_res(3), term_of(2, 3), slice(F + F // 2, 2 * F))
+        add(nc.vector, pair_res(3), pair_res(3), term_of(2, 3), slice(F, F + F // 2))
         halves = (slice(F // 2, F), slice(0, F // 2))
         for cs in halves:
             nc.vector.tensor_tensor(out=pair_res(3)[:, :, cs], in0=pair_res(3)[:, :, cs], in1=terms[3, 3][:, :, cs], op=ALU.add)
             store_pair(3, cs)
             if cs == halves[0]:
-                dst, rows = o_views(1, cs.start, cs.stop)
-                nc.scalar.copy(out=dst, in_=rows)
+                rounding(scopy, 1, cs.start, cs.stop)
         o_quant(0, 0, F)
-        dst, rows = o_views(1, halves[1].start, halves[1].stop)
-        nc.vector.tensor_copy(out=dst, in_=rows)
+        rounding(vcopy, 1, halves[1].start, halves[1].stop)
         for cs in halves:
             o_quant(1, cs.start, cs.stop)
         o_scales()

@@ -27,13 +27,16 @@ WALK = 4
 GAIN_PITCH = 16
 FIRST_SCALAR = 40
 SECOND_SCALAR = 48
-SHARES = (64, 72, 64)
+SHARES = (72, 88, 72)
 LATE_GPSIMD = 96
-CUT_A = 288
-CUT_B = 864
+CUT_A = 384
+CUT_B = 800
 STAGES = 4
 BBUF = 2
 LEAD = 6
+BACK = 28
+SKIPS = (1, 14)
+CUT_D = 896
 
 
 def tile_autonomyofexpertsnormgate_x1_kernel(tc, x, wdown, rgain, wup, wp, out_0, out_1, out_2):
@@ -215,7 +218,6 @@ def tile_autonomyofexpertsnormgate_x1_kernel(tc, x, wdown, rgain, wup, wp, out_0
             return tile[:].to_broadcast([P, G * PACK, E])
 
         terms = {}
-        spare = [SLOT * i for i in range(len(weights))]
 
         def place(pair, s):
             return pair // 2, 2 * (pair % 2) + s
@@ -227,7 +229,7 @@ def tile_autonomyofexpertsnormgate_x1_kernel(tc, x, wdown, rgain, wup, wp, out_0
             if e == 0:
                 return pair_res(pair)
             if (e, pair) not in terms:
-                terms[e, pair] = slots.tile([P, 2, F], F32, name="term%d%d" % (e, pair), offset=spare.pop(0))
+                terms[e, pair] = keep.tile([P, 2, F], F32, name="term%d%d" % (e, pair))
             return terms[e, pair][:]
 
         def silu_tile(e, pair, s):
@@ -315,6 +317,8 @@ def tile_autonomyofexpertsnormgate_x1_kernel(tc, x, wdown, rgain, wup, wp, out_0
                     return
 
         def run(side):
+            if side == "v" and len(queue["v"]) <= len(free["s"]) and not queue["s"] and free["s"]:
+                free["v"].insert(0, free["s"].pop(0))
             fronts(side)
             work, front, needs, gives = queue[side].pop(0)
             bank = fronted[side].pop(0)
@@ -428,11 +432,12 @@ def tile_autonomyofexpertsnormgate_x1_kernel(tc, x, wdown, rgain, wup, wp, out_0
                 sum_turn(0, (2, 3))
                 sum_out(0)
                 sum_out(1)
-            if i == 27:
+            if i == BACK:
+                fronts("v")
                 sum_back()
                 sum_home(0, 0)
                 sum_home(0, 1)
-            if queue["s"] and i != 1:
+            if queue["s"] and i not in SKIPS:
                 run("s")
             if i == 29:
                 rounding(scopy, 0, 0, F)
@@ -456,11 +461,12 @@ def tile_autonomyofexpertsnormgate_x1_kernel(tc, x, wdown, rgain, wup, wp, out_0
             if i == 27:
                 add(nc.vector, pair_res(2), pair_res(2), term_of(3, 2), slice(CUT_B, 2 * F))
                 store_pair(2)
-                add(nc.gpsimd, pair_res(3), pair_res(3), term_of(1, 3))
+                add(nc.gpsimd, pair_res(3), pair_res(3), term_of(1, 3), slice(0, CUT_D))
         nc.vector.tensor_tensor(out=terms[3, 3][:, 0, :], in0=terms[3, 3][:, 0, :], in1=terms[2, 3][:, 0, :], op=ALU.add)
-        add(nc.vector, pair_res(3), pair_res(3), term_of(2, 3), slice(F + F // 2, 2 * F))
+        add(nc.vector, term_of(2, 3), term_of(2, 3), term_of(1, 3), slice(CUT_D, 2 * F))
         add(nc.vector, pair_res(3), pair_res(3), term_of(2, 3), slice(F, F + F // 2))
-        halves = (slice(F // 2, F), slice(0, F // 2))
+        add(nc.vector, pair_res(3), pair_res(3), term_of(2, 3), slice(F + F // 2, 2 * F))
+        halves = (slice(0, F // 2), slice(F // 2, F))
         for cs in halves:
             nc.vector.tensor_tensor(out=pair_res(3)[:, :, cs], in0=pair_res(3)[:, :, cs], in1=terms[3, 3][:, :, cs], op=ALU.add)
             store_pair(3, cs)

@@ -193,8 +193,9 @@ def tile_autonomyofexpertsnormgate_x1_kernel(tc, x, wdown, rgain, wup, wp, out_0
                 return ranks
 
             def work(ranks):
-                nc.vector.tensor_tensor(out=staged["b%d" % e, g][:, cols(t), :], in0=ranks[:].rearrange("p (k n) -> p n k", k=PACK),
-                                        in1=gain[:, e, 0:PACK].unsqueeze(1).to_broadcast([P, P, PACK]), op=ALU.mult)
+                nc.vector.tensor_tensor(out=staged["b%d" % e, g][:, cols(t), :].rearrange("p (m i) k -> p m k i", i=2),
+                                        in0=ranks[:].rearrange("p (k m i) -> p m k i", k=PACK, i=2),
+                                        in1=gain[:, e, 0:PACK].unsqueeze(1).unsqueeze(3).to_broadcast([P, P // 2, PACK, 2]), op=ALU.mult)
             return (work, front, made_by(("wd", e), 0, 512) + [(("x", g), t)], ())
 
         def one_pass(left, t, right):

from contextlib import ExitStack

import concourse.mybir as mybir
from concourse.masks import make_identity

T, D, E, R, F = 1024, 512, 4, 512, 512
FLOPS = 2 * T * E * (D * R + R * F + D * F)

F32 = mybir.dt.float32
BF16 = mybir.dt.bfloat16
U32 = mybir.dt.uint32
I32 = mybir.dt.int32
U8 = mybir.dt.uint8
FP8X4 = mybir.dt.float8_e4m3fn_x4
ALU = mybir.AluOpType
ACT = mybir.ActivationFunctionType
AX = mybir.AxisListType

P = 128
PACK = 4
GROUP = 512
G = T // GROUP
BANK = 2048
SLOT = PACK * 512 * 2
RUNS = 128
WALK = 4
GAIN_PITCH = 16
FIRST_SCALAR = 40
SECOND_SCALAR = 48
SHARES = (72, 88, 72)
LATE_GPSIMD = 96
CUT_A = 384
CUT_B = 800
STAGES = 4
BBUF = 2
LEAD = 6
BACK = 28
SKIPS = (1, 14)
CUT_D = 896


def tile_autonomyofexpertsnormgate_x1_kernel(tc, x, wdown, rgain, wup, wp, out_0, out_1, out_2):
    nc = tc.nc

    with ExitStack() as ctx:
        keep = ctx.enter_context(tc.tile_pool(name="keep", bufs=1))
        slots = ctx.enter_context(tc.tile_pool(name="slots", bufs=1))
        psum = ctx.enter_context(tc.psum_pool(name="psum", bufs=1))
        ctx.enter_context(tc.manual_schedule())
        gain = keep.tile([P, E, GAIN_PITCH], BF16, name="gain")
        ident = keep.tile([P, P], F32, name="ident")
        ident_b = keep.tile([P, P], BF16, name="ident_b")
        warm = keep.tile([P, 1], F32, name="warm")
        ones = keep.tile([P, 512], BF16, name="ones")
        x_parts = [(0, 0, 1), (0, 1, 2), (0, 2, 4), (1, 0, 2), (1, 2, 4)]
        x_raw = {part: keep.tile([P, (part[2] - part[1]) * D], BF16, name="x_raw%d%d%d" % part, align_bytes=64) for part in x_parts}
        weights = [("wd", 0), ("wd", 1), ("wd", 2), ("wu", 0), ("wd", 3), ("wu", 3), ("wp", 0), ("wu", 1), ("wp", 1), ("wu", 2), ("wp", 2), ("wp", 3)]
        src = {}
        for e in range(E):
            src["wd", e], src["wp", e], src["wu", e] = wdown[e], wp[e], wup[e]
        raw = {n: slots.tile([P, PACK, 512], BF16, name="raw_%s%d" % n, offset=SLOT * i) for i, n in enumerate(weights)}
        stage_at = [SLOT * (len(weights) + i) for i in range(STAGES)]
        stage = [slots.tile([P, 512, PACK], BF16, name="stage%d" % i, align_bytes=64, offset=at) for i, at in enumerate(stage_at)]
        b_both = [keep.tile([P, 2 * 512, PACK], BF16, name="b_both%d" % i, align_bytes=64) for i in range(BBUF)]
        b_stage = [[both[:, 512 * s:512 * (s + 1), :] for s in range(2)] for both in b_both]
        staged = {}
        codes, scales = {}, {}
        for n in weights + [("x", g) for g in range(G)]:
            codes[n] = keep.tile([P, 512], U32, name="codes_%s%d" % n, align_bytes=64)
            scales[n] = keep.tile([P, 512], U8, name="scales_%s%d" % n, align_bytes=64)
        steps = [(0, 0), (1, 0), (2, 0), (0, 1), (3, 0), (1, 1), (2, 1), (3, 1)]
        b_codes = [keep.tile([P, 2 * 512], U32, name="codes_b%d" % w, align_bytes=64) for w in range(E)]
        b_scales = [keep.tile([P, 2 * 512], U8, name="scales_b%d" % w, align_bytes=64) for w in range(E)]
        for i, (e, g) in enumerate(steps):
            half = slice(512 * (i % 2), 512 * (i % 2 + 1))
            codes["b%d" % e, g], scales["b%d" % e, g] = b_codes[i // 2][:, half], b_scales[i // 2][:, half]
            staged["b%d" % e, g] = b_stage[i // 2 % BBUF][i % 2]
        squared = keep.tile([P, 2 * PACK, R], BF16, name="squared")
        sumsq = keep.tile([P, G * PACK, E], F32, name="sumsq")
        gate = keep.tile([P, G * PACK, E], F32, name="gate")
        res = [keep.tile([P, PACK, F], F32, name="res%d" % g) for g in range(G)]

        def tokens(ap, g):
            return ap[g * GROUP:(g + 1) * GROUP, :].rearrange("(p t) d -> p t d", t=PACK)

        def load_x(g, lo, hi):
            nc.sync.dma_start(out=x_raw[g, lo, hi][:].rearrange("p (s d) -> p s d", d=D), in_=tokens(x, g)[:, lo:hi, :])

        def load_w(n):
            nc.sync.dma_start(out=raw[n][:], in_=src[n].rearrange("(p j) c -> p j c", j=PACK))

        load_w(weights[0])
        load_x(*x_parts[0])
        load_x(*x_parts[1])
        load_w(weights[1])
        nc.sync.dma_start(out=gain[:, :, 0:PACK], in_=rgain.rearrange("e (p j) -> p e j", j=PACK))
        load_x(*x_parts[2])
        load_w(weights[2])
        load_x(*x_parts[3])
        load_x(*x_parts[4])
        for n in weights[3:]:
            load_w(n)

        nc.vector.memset(ones[:], 1.0)
        nc.scalar.activation(out=warm[:], in_=ones[:, 0:1], func=ACT.Sqrt)
        make_identity(nc, ident[:])
        nc.scalar.copy(out=ident_b[:], in_=ident[:])
        idle = psum.tile([P, 512], F32, name="idle", tag="bank3", offset=3 * BANK)

        def warm_up(moving, count):
            for i in range(count):
                nc.tensor.matmul(out=idle[:], lhsT=ones[:, 0:P], rhs=moving, start=True, stop=True)

        warm_up(ones[:], 3)
        warm_up(raw["wd", 0][:, 0, :], 1)

        free = {"v": [0, 1, 2, 3], "s": [4, 5, 6, 7]}

        def bank_tile(b, shape, dtype):
            return psum.tile(shape, dtype, name="bank%d" % b, tag="bank%d" % b, offset=BANK * b)

        def cols(t):
            return slice(P * t, P * (t + 1))

        def mx(out, left, left_cols, right, right_cols):
            nc.tensor.matmul_mx(out=out, lhsT=codes[left][:, left_cols].bitcast(FP8X4), lhsT_scale=scales[left][:, left_cols],
                                rhs=codes[right][:, right_cols].bitcast(FP8X4), rhs_scale=scales[right][:, right_cols],
                                start=True, stop=True)

        whole = slice(0, 512)

        def run_views(n, lo, hi):
            if n[0] == "wd":
                return (staged[n][:].rearrange("p (q m) j -> p m j q", q=4)[:, lo:hi],
                        raw[n][:].rearrange("p j (m q) -> p m j q", q=4)[:, lo:hi])
            return (staged[n][:, 4 * lo:4 * hi, :].rearrange("p (m q) j -> p m j q", q=WALK),
                    raw[n][:, :, 4 * lo:4 * hi].rearrange("p j (m q) -> p m j q", q=WALK))

        def lay_gpsimd(n, lo, hi):
            dst, rows = run_views(n, lo, hi)
            nc.gpsimd.tensor_scalar(out=dst, in0=rows, scalar1=1.0, scalar2=0.0, op0=ALU.mult, op1=ALU.add)

        def lay(copy, n, lo, hi):
            dst, rows = run_views(n, lo, hi)
            copy(out=dst, in_=rows)

        def plain(call, *args):
            return (lambda bank: call(*args), None, (), ())

        def made_by(n, lo, hi):
            return [(n, t) for t in range(lo // P, hi // P)]

        def quantise(n, lo, hi):
            nc.vector.quantize_mx(out=codes[n][:, lo:hi].bitcast(FP8X4), scales=scales[n][:, lo:hi],
                                  in_=staged[n][:, lo:hi, :].rearrange("p c j -> p (c j)"))

        def quant(n, lo=0, hi=512):
            return (lambda bank: quantise(n, lo, hi), None, (), made_by(n, lo, hi))

        def quant_b(w):
            def work(bank):
                nc.vector.quantize_mx(out=b_codes[w][:].bitcast(FP8X4), scales=b_scales[w][:], in_=b_both[w % BBUF][:].rearrange("p c j -> p (c j)"))
            return (work, None, (), [tile for e, g in steps[2 * w:2 * w + 2] for tile in made_by(("b%d" % e, g), 0, 512)])

        def lay_tensor(copy, n, lo, hi):
            def front(b):
                bank = bank_tile(b, [P, 4 * (hi - lo), PACK], BF16)
                for u in range(2):
                    nc.tensor.matmul(out=bank[:, :, 2 * u:2 * u + 2].rearrange("p c j -> p j c"), lhsT=ident_b[:],
                                     rhs=raw[n][:, 2 * u:2 * u + 2, 4 * lo:4 * hi], start=True, stop=True)
                return bank
            return (lambda bank: copy(out=staged[n][:, 4 * lo:4 * hi, :], in_=bank[:]), front, (), ())

        def x_turn(g, lo, hi):
            def front(b):
                words = x_raw[g, lo, hi][:].bitcast(F32)
                view = bank_tile(b, [P, (hi - lo) * 256], F32)[:].rearrange("p (s u r) -> p s u r", r=P, u=2)
                for s in range(hi - lo):
                    for u in range(2):
                        nc.tensor.transpose(view[:, s, u, :], words[:, 256 * s + u:256 * (s + 1):2], ident[:])
                return view

            def work(view):
                dst = staged["x", g][:].rearrange("p c j -> p (c j)").bitcast(F32).rearrange("p (s r u) -> p s r u", r=P, u=2)
                nc.scalar.copy(out=dst[:, lo:hi], in_=view.rearrange("p s u r -> p s r u"))
            return (work, front, (), ())

        def b_tile(e, g, t):
            def front(b):
                ranks = bank_tile(b, [P, 512], F32)
                for k in range(PACK):
                    mx(ranks[:, cols(k)], ("wd", e), cols(k), ("x", g), cols(t))
                return ranks

            def work(ranks):
                nc.vector.tensor_tensor(out=staged["b%d" % e, g][:, cols(t), :].rearrange("p (m i) k -> p m k i", i=2),
                                        in0=ranks[:].rearrange("p (k m i) -> p m k i", k=PACK, i=2),
                                        in1=gain[:, e, 0:PACK].unsqueeze(1).unsqueeze(3).to_broadcast([P, P // 2, PACK, 2]), op=ALU.mult)
            return (work, front, made_by(("wd", e), 0, 512) + [(("x", g), t)], ())

        def one_pass(left, t, right):
            def front(b):
                bank = bank_tile(b, [P, 512], F32)
                mx(bank[:], left, cols(t), right, whole)
                return bank
            return front, made_by(right, 0, 512) + [(left, t)]

        def square_tile(e, g, t):
            def work(toks):
                nc.scalar.activation(out=squared[:, PACK * (e % 2) + t, :], in_=toks[:], func=ACT.Square,
                                     accum_out=sumsq[:, PACK * g + t, e:e + 1])
            return (work,) + one_pass(("x", g), t, ("wd", e)) + ((),)

        score, z, sz, rest, quot, ex = (keep.tile([P, G * PACK, E], F32, name=name)
                                        for name in ("score", "z", "sz", "rest", "quot", "ex"))
        top, total, inv = (keep.tile([P, G * PACK, 1], F32, name=name) for name in ("top", "total", "inv"))

        def over_experts(tile):
            return tile[:].to_broadcast([P, G * PACK, E])

        terms = {}

        def place(pair, s):
            return pair // 2, 2 * (pair % 2) + s

        def pair_res(pair):
            return res[pair // 2][:, 2 * (pair % 2):2 * (pair % 2) + 2, :]

        def term_of(e, pair):
            if e == 0:
                return pair_res(pair)
            if (e, pair) not in terms:
                terms[e, pair] = keep.tile([P, 2, F], F32, name="term%d%d" % (e, pair))
            return terms[e, pair][:]

        def silu_tile(e, pair, s):
            g, t = place(pair, s)

            def work(up):
                nc.scalar.activation(out=term_of(e, pair)[:, s, :], in_=up[:], func=ACT.Silu)
            return (work,) + one_pass(("b%d" % e, g), t, ("wu", e)) + ((),)

        def product(e, pair, s):
            g, t = place(pair, s)

            def work(lin):
                tile = term_of(e, pair)[:, s, :]
                nc.vector.scalar_tensor_tensor(out=tile, in0=lin[:], scalar=gate[:, PACK * g + t, e:e + 1], in1=tile,
                                               op0=ALU.mult, op1=ALU.mult)
            return (work,) + one_pass(("x", g), t, ("wp", e)) + ((),)

        def flat(ap):
            return ap.rearrange("p t f -> p (t f)")

        def add(engine, out, in0, in1, span=slice(0, 2 * F)):
            engine.tensor_tensor(out=flat(out)[:, span], in0=flat(in0)[:, span], in1=flat(in1)[:, span], op=ALU.add)

        def store_pair(pair, cs=slice(0, F)):
            h = pair % 2
            nc.sync.dma_start(out=tokens(out_0, pair // 2)[:, 2 * h:2 * h + 2, cs], in_=pair_res(pair)[:, :, cs])

        turned = keep.tile([P, 2, F], F32, name="turned")
        sums, held = {}, {}

        def sum_turn(pair, experts):
            for e in experts:
                for s in range(2):
                    if e == 0:
                        held["vs"[s]] = free["vs"[s]].pop(0)
                        sums[s] = bank_tile(held["vs"[s]], [P, F], F32)
                    for c in range(4):
                        nc.tensor.matmul(out=sums[s][:, cols(c)], lhsT=term_of(e, pair)[:, s, cols(c)], rhs=ident[:], is_transpose=True,
                                         start=(e, c) == (0, 0), stop=(e, c) == (E - 1, 3))

        def sum_out(s):
            nc.scalar.copy(out=turned[:, s, :], in_=sums[s][:])

        def sum_back():
            for s in range(2):
                sums[s] = bank_tile(held["vs"[s]], [P, F], F32)
                for c in range(4):
                    nc.tensor.transpose(sums[s][:, cols(c)], turned[:, s, cols(c)], ident[:])

        def sum_home(pair, s):
            nc.scalar.copy(out=pair_res(pair)[:, s, :], in_=sums[s][:])
            if s == 1:
                store_pair(pair)

        og = b_stage[0]
        oc = [keep.tile([P, F], U32, name="oc%d" % g, align_bytes=64) for g in range(G)]
        osc = keep.tile([P, F], U8, name="osc", align_bytes=64)

        def rounding(copy, g, lo, hi):
            copy(out=og[g][:, lo:hi, :].rearrange("p (m q) t -> p m t q", q=4), in_=res[g][:, :, lo:hi].rearrange("p t (m q) -> p m t q", q=4))

        def o_quant(g, lo, hi):
            nc.vector.quantize_mx(out=oc[g][:, lo:hi].bitcast(FP8X4), scales=osc[4 * g:P, lo:hi],
                                  in_=og[g][:, lo:hi, :].rearrange("p c j -> p (c j)"))
            nc.sync.dma_start(out=out_1[g].rearrange("p m b -> p (m b)").bitcast(I32)[:, lo:hi], in_=oc[g][:, lo:hi].bitcast(I32))

        def o_scales():
            for q in range(4):
                nc.sync.dma_start(out=out_2[:, 4 * q:4 * q + 4, :].bitcast(I32), in_=osc[32 * q:32 * q + 4 * G, :].bitcast(I32))

        made = []
        queue = {"v": [], "s": []}
        fronted = {"v": [], "s": []}

        def fronts(side, look=0):
            while len(fronted[side]) < min(len(queue[side]), look + 1):
                work, front, needs, gives = queue[side][len(fronted[side])]
                if front is None:
                    fronted[side].append(None)
                elif free[side] and all(tile in made for tile in needs):
                    b = free[side].pop(0)
                    fronted[side].append((b, front(b)))
                else:
                    return

        def run(side):
            if side == "v" and len(queue["v"]) <= len(free["s"]) and not queue["s"] and free["s"]:
                free["v"].insert(0, free["s"].pop(0))
            fronts(side)
            work, front, needs, gives = queue[side].pop(0)
            bank = fronted[side].pop(0)
            work(bank[1] if bank else None)
            if bank:
                free[side].append(bank[0])
            return gives

        def turn(beside=1, ahead=None):
            if ahead:
                ahead()
            gives = run("v")
            for i in range(min(beside, len(queue["s"]))):
                run("s")
            made.extend(gives)

        staged["x", 0], staged["x", 1], staged["wd", 0], staged["wd", 1] = stage[3], stage[1], stage[2], stage[0]
        own = [("wd", 2), ("wd", 3), ("wp", 0), ("wp", 1)]
        shared = [("x", 1), ("wu", 0), ("wu", 1), ("wu", 2)]
        for w, (mine, other) in enumerate(((3, 1), (1, 2), (2, 0), (0, 1))):
            staged[own[w]], staged[shared[w]] = stage[mine], stage[other]
        alone, late = ("wu", 3), [("wp", 2), ("wp", 3)]
        staged[alone], staged[late[0]], staged[late[1]] = stage[3], stage[3], stage[2]
        nothing = plain(lambda: None)
        scopy, vcopy = nc.scalar.copy, nc.vector.tensor_copy

        lay(scopy, ("wd", 0), 0, FIRST_SCALAR)
        lay(vcopy, ("wd", 0), FIRST_SCALAR, RUNS)
        queue["s"] = [x_turn(*part) for part in x_parts[:2]]
        run("s")
        run("s")
        warm_up(ones[:], 2)
        for n, lo, hi in ((("wd", 0), 0, 512), (("x", 0), 0, P), (("x", 0), P, 2 * P)):
            quantise(n, lo, hi)
            made.extend(made_by(n, lo, hi))
        lay(scopy, ("wd", 1), 0, SECOND_SCALAR)
        lay(vcopy, ("wd", 1), SECOND_SCALAR, RUNS)

        opening = [(e, 0, 2 * h + s) for h in range(2) for e in range(2) for s in range(2)]
        order = opening + [(e, g, t) for e, g in ((2, 0), (0, 1), (1, 1), (3, 0), (2, 1), (3, 1)) for t in range(PACK)]
        sq = [square_tile(*tile) for tile in order]
        cycles = [[(0, 0), (0, 1)], [(1, 0), (1, 1)], [(0, 2), (1, 2)], [(2, 0), (2, 1)], [(3, 0), (3, 1)], [(2, 2), (3, 2)], [(0, 3), (1, 3)], [(2, 3), (3, 3)]]
        units = [(e, pair, s) for cycle in cycles for e, pair in cycle for s in range(2)]
        silus = [silu_tile(*unit) for unit in units]
        HALF = RUNS // 2

        def gate_root():
            nc.scalar.activation(out=score[:], in_=sumsq[:], func=ACT.Sqrt)

        def gate_silu():
            nc.scalar.activation(out=sz[:], in_=z[:], func=ACT.Silu, bias=-1.0)
            nc.scalar.activation(out=rest[:], in_=z[:], func=ACT.Silu, scale=-1.0, bias=1.0)

        def gate_top():
            nc.vector.tensor_reduce(out=top[:, :, 0], in_=score[:], axis=AX.X, op=ALU.max)
            nc.gpsimd.tensor_tensor(out=z[:], in0=score[:], in1=over_experts(top), op=ALU.subtract)

        queue["s"] = (sq[0:1] + [x_turn(*x_parts[2])] + sq[1:8] + [x_turn(*part) for part in x_parts[3:]] + [plain(lay, scopy, shared[1], SHARES[0], RUNS), nothing]
                      + sq[8:16] + [lay_tensor(scopy, shared[2], SHARES[1], RUNS)] + sq[16:18] + [nothing] + sq[18:26] + [lay_tensor(scopy, alone, 0, HALF)] + sq[26:28] + [nothing]
                      + sq[28:32] + [plain(gate_root), silus[0], nothing, nothing, plain(gate_silu), lay_tensor(scopy, shared[3], SHARES[2], RUNS), lay_tensor(scopy, alone, HALF, RUNS)]
                      + silus[1:])

        def window(w):
            return [b_tile(*steps[2 * w + s], t) for s in range(2) for t in range(PACK)]

        first = [b_tile(*tile) for tile in opening]
        chain = [
            lambda: nc.vector.reciprocal(out=quot[:], in_=rest[:]),
            lambda: nc.vector.tensor_tensor(out=ex[:], in0=sz[:], in1=quot[:], op=ALU.mult),
            lambda: nc.vector.tensor_reduce(out=total[:, :, 0], in_=ex[:], axis=AX.X, op=ALU.add),
            lambda: nc.vector.reciprocal(out=inv[:], in_=total[:]),
            lambda: nc.vector.tensor_tensor(out=gate[:], in0=ex[:], in1=over_experts(inv), op=ALU.mult),
        ]
        fill = [quant(shared[-1], 0, 2 * P), quant(shared[-1], 2 * P, 4 * P), quant(("b3", 1), 0, 2 * P), quant(alone, 0, 2 * P), quant(alone, 2 * P, 4 * P)]
        products = [product(*unit) for unit in units]
        running = stage_at[3]
        program = [(first[0], 2), (quant(("wd", 1)), 0), (first[1], 1), (quant(("x", 0), 2 * P, 4 * P), 0, lambda: lay_gpsimd(own[0], 0, RUNS))]
        program += [(step, 1) for step in first[2:]] + [(quant(own[0]), 1), (quant_b(0), 2), (quant(shared[0]), 1, lambda: shares(1))]
        for w in (1, 2):
            program += [(step, 1) for step in window(w)] + [(quant(own[w]), 1), (quant(shared[w]), 1), (quant_b(w), 2, lambda w=w: shares(w + 1))]

        def shares(w):
            lay_gpsimd(own[w], 0, RUNS)
            lay_gpsimd(shared[w], 0, SHARES[w - 1])

        last = window(3)
        program += [(step, 1) for step in last[:6]] + [(plain(gate_top), 0)] + [(step, 1) for step in last[6:]]
        program += [(quant(own[-1]), 2), (quant(("b2", 1)), 1)]
        for link, call in zip(chain, fill):
            program += [(plain(link), 0), (call, 1)]

        def lay_late():
            lay_gpsimd(late[0], 0, RUNS)
            lay_gpsimd(late[1], 0, LATE_GPSIMD)

        program += [(quant(("b3", 1), 2 * P, 4 * P), 0, lay_late)]
        queue["v"] = [entry[0] for entry in program] + products
        for entry in program:
            turn(entry[1])
            if len(entry) > 2:
                entry[2]()
        while len(queue["s"]) > len(units) - LEAD:
            run("s")
        for i in range(len(units)):
            run("v")
            if i == 1:
                lay(scopy, late[1], LATE_GPSIMD, RUNS)
            if i == 9:
                sum_turn(0, (0, 1))
            if i == 23:
                sum_turn(0, (2, 3))
                sum_out(0)
                sum_out(1)
            if i == BACK:
                fronts("v")
                sum_back()
                sum_home(0, 0)
                sum_home(0, 1)
            if queue["s"] and i not in SKIPS:
                run("s")
            if i == 29:
                rounding(scopy, 0, 0, F)
            if i == 7:
                for n in late:
                    quantise(n, 0, 512)
                    made.extend(made_by(n, 0, 512))
                sofar = slots.tile([P, 2, F], F32, name="running", offset=running)
                add(nc.gpsimd, sofar[:], pair_res(1), term_of(1, 1))
            if i == 11:
                add(nc.gpsimd, pair_res(2), pair_res(2), term_of(1, 2))
            if i == 15:
                add(nc.gpsimd, sofar[:], sofar[:], term_of(2, 1))
            if i == 19:
                add(nc.gpsimd, pair_res(1), sofar[:], term_of(3, 1), slice(CUT_A, 2 * F))
            if i == 23:
                add(nc.vector, pair_res(1), sofar[:], term_of(3, 1), slice(0, CUT_A))
                store_pair(1)
                add(nc.vector, pair_res(2), pair_res(2), term_of(2, 2))
                add(nc.gpsimd, pair_res(2), pair_res(2), term_of(3, 2), slice(0, CUT_B))
            if i == 27:
                add(nc.vector, pair_res(2), pair_res(2), term_of(3, 2), slice(CUT_B, 2 * F))
                store_pair(2)
                add(nc.gpsimd, pair_res(3), pair_res(3), term_of(1, 3), slice(0, CUT_D))
        nc.vector.tensor_tensor(out=terms[3, 3][:, 0, :], in0=terms[3, 3][:, 0, :], in1=terms[2, 3][:, 0, :], op=ALU.add)
        add(nc.vector, term_of(2, 3), term_of(2, 3), term_of(1, 3), slice(CUT_D, 2 * F))
        add(nc.vector, pair_res(3), pair_res(3), term_of(2, 3), slice(F, F + F // 2))
        add(nc.vector, pair_res(3), pair_res(3), term_of(2, 3), slice(F + F // 2, 2 * F))
        halves = (slice(0, F // 2), slice(F // 2, F))
        for cs in halves:
            nc.vector.tensor_tensor(out=pair_res(3)[:, :, cs], in0=pair_res(3)[:, :, cs], in1=terms[3, 3][:, :, cs], op=ALU.add)
            store_pair(3, cs)
            if cs == halves[0]:
                rounding(scopy, 1, cs.start, cs.stop)
        o_quant(0, 0, F)
        rounding(vcopy, 1, halves[1].start, halves[1].stop)
        for cs in halves:
            o_quant(1, cs.start, cs.stop)
        o_scales()
